import numpy as np, ml_dtypes
CORES = [2,3,42,43,82,83,122,123]
N = 8
BF = ml_dtypes.bfloat16
V, P, B, C, RO, LG = 2048, 224, 4, 96, 3, 3
PAR = np.array([bin(i).count("1") % 2 for i in range(N)]).reshape(N, 1)
GRP = np.arange(8).reshape(1, 8)
def base(rng):
    nbr = rng.integers(0, V, (8, 16, V)); w = rng.integers(100, 256, (8, 16, V)); b = rng.integers(2 ** 12, 2 ** 19, (8, 16, 1))
    return nbr, w, b, b + rng.integers(0, 100, (N, 8, 16, V))
def stir(rng, x, up, down):
    hi = rng.random((N, 8, V)) < up; lo = (rng.random((N, 8, V)) < down) & ~hi
    m = rng.random(x.shape) < rng.random((N, 8, 1, V))
    a = np.exp2(6 + 13 * rng.random(x.shape)).astype(np.int64); d = np.exp2(12 * rng.random(x.shape)).astype(np.int64)
    x = np.where(hi[:, :, None, :] & m, np.minimum(x + a, 2 ** 20 - 1), x)
    return np.where(lo[:, :, None, :] & m, np.maximum(x - d, 0), x), hi
def names(rng, hi):
    o = np.argsort(rng.random((N, 8, V)) - hi, axis=-1); h = np.add.reduce(hi.astype(np.int64), axis=-1)[:, :, None]
    a = np.take_along_axis(o, (rng.random((N, 8, 16 * P)) * h).astype(np.int64), -1)
    return np.where(rng.random(a.shape) < 0.5, a, rng.integers(0, V, a.shape)).reshape(N, 8, 16, P)
def heights(rng):
    e = rng.choice(np.array([0.1, 0.25, 0.4, 0.6]), (N, 8, 1))
    return np.where(rng.random((N, 8, P)) < e, 0, rng.integers(1, 17, (N, 8, P)))
def pack(nbr, w, x, st, n):
    st = np.where(np.arange(16)[:, None] < n[:, :, None, :], st, 0)
    return {"nb": np.tile(nbr.reshape(1, 128, V), (N, 1, 1)).astype(np.int32), "ln": np.tile(w.reshape(1, 128, V), (N, 1, 1)).astype(np.float32).astype(BF),
            "lab": np.ascontiguousarray(x.reshape(N, 128, V)).astype(np.int32), "stk": np.ascontiguousarray(st.reshape(N, 128, P)).astype(np.int32), "cnt": n.astype(np.int32)}
def setup_inputs(rng):
    nbr, w, b, x = base(rng)
    x, hi = stir(rng, x, rng.choice(np.array([0.02, 0.04, 0.08, 0.16]), (N, 8, 1)), rng.choice(np.array([0.0, 0.001, 0.004]), (N, 8, 1)))
    return pack(nbr, w, x, names(rng, hi), heights(rng))
def setup_inputs_spread(rng):
    nbr, w, b, x = base(rng)
    nbr[1::2] = (V * rng.random((4, 16, V)) ** 3).astype(np.int64); w[1::2] = np.exp2(8 * rng.random((4, 16, V))).astype(np.int64)
    b = np.minimum(np.exp2(20 * rng.random((8, 16, 1))).astype(np.int64), 2 ** 20 - 5000)
    x, hi = stir(rng, b + rng.integers(0, 100, x.shape), 0.06, 0.002)
    x[:, 1::2] = np.minimum((np.exp2(20 * rng.random((N, 4, 1, V))) * rng.random((N, 4, 16, V))).astype(np.int64), 2 ** 20 - 1)
    return pack(nbr, w, x, names(rng, hi), heights(rng))
def setup_inputs_ends(rng):
    e = np.array([0, V - 1])
    nbr = np.where(rng.random((8, 16, V)) < 0.75, rng.choice(e, (8, 16, V)), rng.integers(0, V, (8, 16, V)))
    w = rng.choice(np.array([1, 255]), (8, 16, V))
    k = rng.random((N, 8, 1, V)); x = (2 ** 20 - 1) * np.where(k < 0.7, 1, np.where(k < 0.8, 0, rng.integers(0, 2, (N, 8, 16, V))))
    x[..., e] = (2 ** 20 - 1) * rng.integers(0, 2, (N, 8, 16, 2))
    full = rng.random((N, 8, P)) < rng.choice(np.array([0.3, 0.5, 0.7]), (N, 8, 1))
    n = np.where(rng.random((N, 8, P)) < 0.8, 16 * full, rng.choice(np.array([1, 2, B + 1, B + 2, 15]), (N, 8, P)))
    st = np.where(rng.random((N, 8, 16, P)) < 0.75, rng.choice(e, (N, 8, 16, P)), rng.integers(0, V, (N, 8, 16, P)))
    n[N - 1, 7, P - 1] = 16; st[N - 1, 7, 15, P - 1] = V - 1; n[0, 7, P - 1] = 0; n[0, 0, 0] = 16; st[0, 0, 15, 0] = 0
    return pack(nbr, w, x, st, n)
def setup_inputs_corners(rng):
    nbr, w, b, x = base(rng); v = np.arange(V)
    nbr[1] = v; nbr[2] = rng.choice(np.array([0, V - 1]), (16, V)); nbr[3] = (v + 1) % V; nbr[4] = np.where(rng.random((16, V)) < 0.5, v, V - 1 - v)
    y, hi = stir(rng, x, 0.05, 0.002); x[:, 6:] = y[:, 6:]
    w[0] = rng.choice(np.array([1, 255]), (16, V)); x[:, 0] = b[0] + rng.integers(0, 2, (N, 16, V))
    w[5] = 255; x[:, 5] = 255 * rng.integers(0, 2, (N, 16, V))
    sn = rng.choice(np.array([0, 1, C - 1, C, C + 1, P - C - 1]), (N, 8)); em = rng.choice(np.array([0, 1, C - 1, C, C + 1]), (N, 8))
    sn[0] = (C, C + 1, C, C - 1, 0, C + 1, 1, C); em[1] = (C, C, C + 1, C + 1, C + 1, 0, C, 1)
    sn[N - 1] = (1, P - C - 1, 0, C, C + 1, C - 1, C, C); em[N - 2] = (C, C, C, C - 1, C, C, C, C + 1)
    pos = np.argsort(rng.random((N, 8, P)), axis=-1); sn = sn[:, :, None]; em = em[:, :, None]
    n = np.where(pos < sn, rng.choice(np.array([B + 2, 15, 16]), pos.shape), np.where(pos < sn + em, rng.integers(0, 2, pos.shape), rng.choice(np.array([2, B, B + 1]), pos.shape)))
    return pack(nbr, w, x, names(rng, hi), n)
def setup_inputs_crowd(rng):
    nbr, w, b, x = base(rng); c = rng.integers(1, V - 1, 8); c[0] = 0; c[7] = V - 1
    full = (PAR + GRP) % 2 == 0
    nbr[0:2, :8] = rng.choice(np.array([5, 6, V - 2]), (2, 8, V)); nbr[:, 15] = c[:, None]
    n = np.where(full, 16, 0)[:, :, None] * np.ones((1, 1, P), np.int64)
    st = np.tile(c.reshape(1, 8, 1, 1), (N, 1, 16, P))
    st[:, 3::4] = rng.integers(0, V, (N, 2, 16, 1))
    for q in range(8):
        u = int(c[q]); a = nbr[q, :, u].copy(); a = np.where(a == u, (u + 1) % V, a)
        if q % 2 == 1: a[15] = u
        nbr[q, :, u] = a
        if q % 4 == 2: st[:, q] = rng.choice(np.array([u, 0, V - 1]), (N, 16, P))
        for r in range(N):
            if q % 4 == 1: st[r, q, :, int(rng.integers(0, P))] = rng.integers(0, V, 16)
            if full[r, q] or q >= 4: x[r, q, :, u] = 0
            if q >= 4: n[r, q, int(rng.integers(0, P))] = 0 if full[r, q] else 1
    return pack(nbr, w, x, st, n)
def setup_inputs_calm(rng):
    nbr, w, b, x = base(rng); w = rng.choice(np.array([1, 255]), w.shape)
    b = rng.integers(2 ** 19, 2 ** 20 - 3, b.shape); b[2:4] = 2 ** 20 - 2; b[6:8] = 2 ** 20 - 3; x = b + rng.integers(0, 2, x.shape)
    x[:, 4:] = np.where(rng.random((N, 4, 16, V)) < 0.0005, b[4:] + 2, x[:, 4:])
    r = np.arange(N).reshape(N, 1)
    big = (np.where(GRP % 4 == 2, 0, np.where(GRP % 4 == 3, 1, (PAR + GRP) % 2)) == 1)[:, :, None]
    h = ((r + GRP + rng.integers(0, 4)) % 4)[:, :, None]; few = ((3 * r + GRP + rng.integers(0, 4)) % 4)[:, :, None]
    pos = np.argsort(rng.random((N, 8, P)), axis=-1)
    n = np.where(pos < few, np.where(big, RO, B + 1 + RO), np.where(big, B + RO + rng.integers(0, 2, pos.shape), h + RO - 1))
    return pack(nbr, w, x, rng.integers(0, V, (N, 8, 16, P)), n)
def check_inputs(d):
    bad = []
    for k, lo, hi in (("nb", 0, V - 1), ("ln", 1, 255), ("lab", 0, 2 ** 20 - 1), ("stk", 0, V - 1), ("cnt", 0, 16)):
        a = np.asarray(d[k]).astype(np.float64)
        if not (np.min(a) >= lo and np.max(a) <= hi): bad.append("range of " + k)
        if k == "ln" and not np.all(a == np.floor(a)): bad.append("whole numbers in ln")
        if k in ("nb", "ln") and not np.all(a == a[:1]): bad.append(k + " alike on all ranks")
    s = np.asarray(d["stk"]).reshape(N, 8, 16, P); n = np.asarray(d["cnt"]).reshape(N, 8, 1, P)
    if np.any((np.arange(16)[:, None] >= n) & (s != 0)): bad.append("zeros in the empty slots of stk")
    return bad
def reference(nb, ln, lab, stk, cnt):
    nbr = nb.astype(np.int64).reshape(N, 8, 16, V); w = ln.astype(np.float32).astype(np.int64).reshape(N, 8, 16, V)
    x = lab.astype(np.int64).reshape(N, 8, 16, V); st = stk.astype(np.int64).reshape(N, 8, 16, P); n = cnt.astype(np.int64).reshape(N, 8, P)
    for t in range(RO):
        live = n > 0
        v = np.take_along_axis(st, np.maximum(n - 1, 0)[:, :, None, :], 2)
        k = np.take_along_axis(nbr, v, 3)
        kk = np.ascontiguousarray(k.transpose(0, 1, 3, 2)).reshape(N, 8, 1, 16 * P)
        xk = np.take_along_axis(x, kk, 3).reshape(N, 8, 16, P, 16); wk = np.take_along_axis(w, kk, 3).reshape(N, 8, 16, P, 16)
        y = np.minimum(np.take_along_axis(x, v, 3), np.min(xk, axis=4) + np.take_along_axis(w, v, 3))
        hit = np.any(xk > y[..., None] + wk, axis=2) & live[..., None]
        a, g, l = np.nonzero(live); x[a, g, :, v[a, g, 0, l]] = y[a, g, :, l]
        n = n - live.astype(np.int64); st = np.where(np.arange(16)[:, None] < n[:, :, None, :], st, 0)
        rank = np.add.accumulate(hit.astype(np.int64), axis=3); slot = n[..., None] + rank - 1
        a, g, l, i = np.nonzero(hit & (slot < 16)); st[a, g, slot[a, g, l, i], l] = k[a, g, i, l]
        n = np.minimum(n + rank[..., 15], 16)
        x2, st2, n2 = x.copy(), st.copy(), n.copy()
        for r in range(N):
            q = r ^ (1 << (t % LG))
            for g in range(8):
                give = np.nonzero(n[r, g] > B)[0]; get = np.nonzero(n[q, g] == 0)[0]
                m = min(len(give), len(get), C); give, get = give[:m], get[:m]
                s = st[r, g]; e = s[:B][:, give]
                st2[r, g][:, give] = np.concatenate([s[B:][:, give], np.zeros((B, m), np.int64)]); n2[r, g][give] = n[r, g][give] - B
                st2[q, g][:B, get] = e; n2[q, g][get] = B
                u = e.reshape(-1); x2[q, g][:, u] = np.minimum(x[q, g][:, u], x[r, g][:, u])
        x, st, n = x2, st2, n2
    return {"ylab": x.reshape(N, 128, V).astype(np.float32), "ystk": st.reshape(N, 128, P).astype(np.float32), "ycnt": n.astype(np.float32)}

@@ -1,0 +1,497 @@
+from concourse.mybir import AluOpType as A, ActivationFunctionType as F
+
+V, P, STEPS = 2048, 224, 3
+CH = [(0, 64), (64, 128), (128, 192), (192, 224)]
+DPE = 1
+GORDER = [("x", 1), ("d", 0), ("x", 2), ("d", 1), ("x", 3), ("d", 2), ("d", 3)]
+BIG = 2097152.0
+f32, b16, h16, i32, u16 = "float32", "bfloat16", "float16", "int32", "uint16"
+_B = {
+    "nbs": (V, i32), "labs": (V, i32), "W": (V, b16), "X": (V + 32, f32), "D": (V, f32),
+    "stks": (P, i32), "cnts": (P, i32), "cntb": (P, b16),
+    "G": (P * 16, f32), "A0": (1024, b16), "SO": (P * 16, f32), "Dg": (P * 16, f32), "Ind": (P * 16, b16),
+    "Zt": (P, f32), "Z": (P, f32),
+    "XM": (256, f32), "GM": (128, f32), "PI": (4, i32), "CC": (16, f32), "NB": (16, f32), "QS": (4, f32),
+    "TJ": (576, f32), "TZ": (336, f32), "ZO": (64, u16), "C1": (16, f32), "JC": (24, f32), "ONE": (P, b16),
+    "M1": (144, b16), "M16": (144, b16), "MK4": (144, b16), "Mh": (144, h16), "M3h": (144, h16),
+    "PQ": (144, f32), "Q15": (144, f32), "IW": (144, f32),
+    "I1": (128, b16), "In1": (128, b16), "I2k": (128, b16), "In2k": (128, b16), "I4": (128, b16), "In4": (128, b16),
+    "Ih": (128, h16), "SHI": (128, h16), "ONES": (128, b16), "REP": (128, b16), "TR1": (128, b16), "TR2": (128, b16),
+    "IW4": (144, f32), "NS": (V, h16), "INV": (512, h16),
+    "v16": (16, u16), "Vh": (28, h16), "V0": (16, h16), "K": (P, u16), "Kf": (P, h16),
+    "n1": (P, b16), "dead": (P, b16), "r1": (P, b16), "r2": (P, b16), "pm": (P, b16), "Sold": (P, h16),
+    "eqz": (336, b16), "zoff": (14, u16), "hit": (P, b16), "RG": (4 * P, b16), "nnm": (P, b16),
+    "q": (16 * P, f32), "B4": (P, f32), "Bc": (P, f32), "tw": (32, f32), "pos": (16, u16), "epos": (16, u16),
+    "U16": (24, u16), "mt": (P, b16), "m2": (P, b16), "ab1": (P, b16), "T1": (P, h16), "T2": (P, h16),
+    "Uh": (48, h16), "Uq": (24, u16), "cio": (2, f32), "MK": (112, b16), "inval": (24, f32), "RB": (104, f32),
+    "Rg": (P, h16), "eqj": (576, b16), "GW": (P, b16), "recv": (P, b16), "giv": (P, b16),
+    "jm": (384, f32), "Bg": (P, h16), "ostk": (P, f32), "ocnt": (P, f32), "Uf": (24, h16),
+    "LE": (16, f32), "SG": (64, f32),
+}
+for _t in range(STEPS):
+    _B.update({"ms%d" % _t: (24, f32), "mr%d" % _t: (24, f32), "ls%d" % _t: (384, f32), "lr%d" % _t: (384, f32),
+               "cs%d" % _t: (2, f32), "cr%d" % _t: (2, f32), "js%d" % _t: (24, u16), "jr%d" % _t: (24, u16)})
+SCRATCH = {k: ("sbuf", [128, n], d) for k, (n, d) in _B.items()}
+for _k in range(8):
+    SCRATCH["pb%d" % _k] = ("psum", [128, 512], f32)
+
+LOADS = ["stk", "cnt", "lab0", "lab1", "nb", "ln", "ylab", "ystk", "ycnt"]
+SEMAPHORES = (["ve", "ac", "pe", "po", "sent"] + ["d_" + s for s in LOADS]
+              + ["r%d%s" % (t, s) for t in range(STEPS) for s in "cnabj"])
+
+CYC, FIX, GATHER, SCATTER, PECYC, WAKE = 1.04e-3, 0.06, 1.56, 3.8, 0.52e-3, 0.1
+HBM, LINK, ISSUE, FLY, SLACK = 200e3, 60e3, 1.0, 2.0, 0.1
+ROUNDS, MIX, EARLY, LATE, SHAKE = 40, 0.5, 4, 8, 1.5
+PARTS = [(0, 128), (128, P)]
+_PLAN = {}
+
+
+def order_calls(ops):
+    n = len(ops)
+    pred = [[(d, ops[d]["lat"] + WAKE if d in o["wait"] else 0.0) for d in sorted(o["after"])] for o in ops]
+    succ = [[] for _ in range(n)]
+    for k in range(n):
+        for d, lag in pred[k]:
+            succ[d].append((k, lag))
+
+    def plan(before, behind, rank):
+        end, free, bank, due = [0.0] * n, {}, {}, [0.0] * n
+        left = [len(x) for x in before]
+        pool = [k for k in range(n) if left[k] == 0]
+        order, extra = [], [set() for _ in range(n)]
+        while pool:
+            at = {k: max([due[k], free.get(ops[k]["q"], 0.0)]
+                         + [end[d] + WAKE for b in ops[k]["banks"] for q, d in bank.get(b, {}).items()
+                            if q != ops[k]["q"]]) for k in pool}
+            pick = first = min(pool, key=lambda j: (at[j], -rank[j], j))
+            for k in sorted((j for j in pool if ops[j]["q"] == ops[first]["q"]), key=lambda j: (at[j], j)):
+                if rank[k] > rank[pick] and at[pick] + ops[pick]["cost"] > at[k] + SLACK:
+                    pick = k
+            o = ops[pick]
+            end[pick] = free[o["q"]] = at[pick] + o["cost"]
+            for b in o["banks"]:
+                extra[pick] |= {d for q, d in bank.get(b, {}).items() if q != o["q"]}
+                bank.setdefault(b, {})[o["q"]] = pick
+            order.append(pick)
+            pool.remove(pick)
+            for s, lag in behind[pick]:
+                due[s] = max(due[s], end[pick] + lag)
+                left[s] -= 1
+                if left[s] == 0:
+                    pool.append(s)
+        return max(end[k] + ops[k]["lat"] for k in range(n)), end, order, extra
+
+    rank = [0.0] * n
+    for k in range(n - 1, -1, -1):
+        rank[k] = ops[k]["cost"] + max([lag + rank[s] for s, lag in succ[k]], default=ops[k]["lat"])
+    best, seed = None, 1
+    for r in range(ROUNDS):
+        made = plan(pred, succ, rank)
+        if best is None or made[0] < best[0]:
+            best, kept = made, rank
+        if r % 4 == 3:
+            rank = []
+            for x in kept:
+                seed = (seed * 1103515245 + 12345) % 2147483648
+                rank.append(x + SHAKE * seed / 2147483648)
+        else:
+            back = plan(succ, pred, made[1])[1]
+            rank = [MIX * x + (1 - MIX) * y for x, y in zip(back, rank)]
+    _PLAN["time"] = best[0]
+    return best[2], best[3]
+
+
+def rank_program(g, core, T, topo):
+    rank = T.rank_of(core)
+    if rank is None:
+        return
+    Q = {"ve": g.vector, "ac": g.scalar, "pe": g.tensor, "po": g, "sy": g.sync}
+    ops, hist = [], {}
+
+    def c(name, a=0, b=None, st=1, p=None):
+        b = SCRATCH[name][1][1] if b is None else b
+        ps = slice(None) if p is None else slice(p[0], p[1])
+        ap = T[name][ps, a:b] if st == 1 else T[name][ps, a:b:st]
+        return (ap, [(name, a, b, st)], [], len(range(a, b, st)), name, False)
+
+    def ind(win, off):
+        return (win[0].indirect(off[0]), win[1], off[1], 16 * off[3], win[4], True)
+
+    def rec(q, call, outs, ins, cost, sem=None, inc=1, lat=0.0, after=(), opened=False):
+        k = len(ops)
+        wait, order, acc = set(), set(after), []
+        for o in outs:
+            acc += [(r, True) for r in o[1]] + [(r, False) for r in o[2]]
+        for o in ins:
+            if isinstance(o, tuple):
+                acc += [(r, False) for r in o[1] + o[2]]
+        for (name, lo, hi, st), w in acc:
+            for l2, h2, s2, k2, w2 in hist.get(name, []):
+                same = ops[k2]["q"] == q and ops[k2]["sem"] is None and sem is None
+                if l2 < hi and lo < h2 and (w or w2) and not (st == s2 > 1 and (lo - l2) % st):
+                    (order if same and ops[k2]["open"] else wait).add(k2)
+                elif q == "pe" and same and name.startswith("pb"):
+                    order.add(k2)
+        for (name, lo, hi, st), w in acc:
+            hist.setdefault(name, []).append((lo, hi, st, k, w))
+        ops.append(dict(q=q, call=call, sem=sem, inc=inc, wait=wait, after=wait | order, cost=cost, lat=lat,
+                        open=opened, banks={r[0] for r, w in acc if r[0].startswith("pb")}))
+        return k
+
+    def a(x):
+        return x[0] if isinstance(x, tuple) else x
+
+    def price(o, x, per):
+        return FIX + CYC * (SCATTER * o[3] if o[5] else GATHER * o[3] if x[5] else max(64, per * o[3]))
+
+    def narrow(*xs):
+        return 0.5 if all(SCRATCH[x[4]][2] in (b16, h16, u16) for x in xs) else 1
+
+    def tt(o, x, y, op):
+        per = 1 if x[4].startswith("pb") or y[4].startswith("pb") else 2
+        return rec("ve", lambda e: e.tensor_tensor(o[0], x[0], y[0], op), [o], [x, y], price(o, x, per))
+
+    def ts(o, x, s1, op0, s2=None, op1=None):
+        if op1 is None:
+            call = lambda e: e.tensor_scalar(o[0], x[0], a(s1), None, op0)
+        else:
+            call = lambda e: e.tensor_scalar(o[0], x[0], a(s1), a(s2), op0, op1)
+        return rec("ve", call, [o], [x, s1, s2], price(o, x, narrow(o, x)))
+
+    def cp(o, x):
+        return rec("ve", lambda e: e.tensor_copy(o[0], x[0]), [o], [x], price(o, x, narrow(o, x)))
+
+    def fill(o, v):
+        rec("ve", lambda e: e.memset(o[0], v), [o], [], price(o, o, narrow(o)))
+
+    def scan(o, x, y, init, op0, op1):
+        rec("ve", lambda e: e.tensor_tensor_scan(o[0], x[0], y[0], init, op0, op1), [o], [x, y],
+            price(o, x, narrow(o, x, y)))
+
+    def act(o, x, f=F.Identity, bias=0.0, scale=1.0, after=()):
+        return rec("ac", lambda e: e.activation(o[0], x[0], f, bias=a(bias), scale=a(scale)), [o], [x, bias, scale],
+                   price(o, x, 1), after=after)
+
+    def group(o, terms, start=True, stop=True, after=()):
+        parts = o if isinstance(o, list) else [(o, terms)]
+
+        def call(e):
+            for out, tm in parts:
+                for j, (l, r) in enumerate(tm):
+                    ins = e.matmul(out[0], l[0], r[0], start and j == 0, stop and j == len(tm) - 1)
+            return ins
+        cost = sum(PECYC * max(64, r[3]) * (4 if SCRATCH[r[4]][2] == f32 else 1) for out, tm in parts for l, r in tm)
+        outs = [out if start and stop else c(out[4]) for out, tm in parts]
+        return rec("pe", call, outs, [x for out, tm in parts for lr in tm for x in lr], cost,
+                   opened=not stop, after=after)
+
+    def wrap(m, name, a0, b0):
+        return [(c(m, 15 - p, 143 - p), c(name, a0 + p, b0, 16)) for p in range(16)]
+
+    def iota(o, pat, base, cm):
+        kw = {} if SCRATCH[o[4]][2] == i32 else {"allow_small_or_imprecise_dtypes": True}
+        rec("po", lambda e: e.iota(o[0], pat, base, cm, **kw), [o], [], 0.13 + 2 * CYC * o[3])
+
+    landed = [2.0]
+
+    def load(q, o, src, s, nbytes):
+        landed[0] += nbytes / HBM
+        prev = [k for k, x in enumerate(ops) if x["q"] == q]
+        rec(q, lambda e: e.dma_start(o[0], src), [o], [], 0.05, "d_" + s, 16, landed[0], prev[-1:])
+
+    def store(q, dst, x, s, nbytes):
+        rec(q, lambda e: e.dma_start(dst, x[0]), [], [x], 0.05, "d_" + s, 16, 2.0 + nbytes / HBM)
+
+    def common(x):
+        near = [T.cores[T.rank_of(x) ^ (1 << s)] for s in range(STEPS)]
+        return [e for e in topo.engines(x, near[0]) if all(e in topo.engines(x, y) for y in near)]
+
+    peers = [T.cores[rank ^ (1 << t)] for t in range(STEPS)]
+    emask = sum(1 << e for e in common(core))
+    sends = []
+
+    def exchange(t, dst, src, s):
+        rid, pid = topo.addr(peers[t])[:2]
+        k = rec("po", lambda e: e.remote_dma(dst[0], src[0], T.sem[s], T.sem["sent"], pid, rid, emask),
+                [], [src], ISSUE, "sent", len(common(core)), 0.0, sends[-1:])
+        sends.append(k)
+        prev = [j for j, x in enumerate(ops) if x["q"] == "rx"]
+        rec("rx", None, [dst], [], 512 * src[3] / LINK, s, len(common(peers[t])), FLY, [k] + prev[-1:])
+
+    col = lambda j: c("CC", j, j + 1)
+    PCOL, ACOL, QCOL, GCOL, DUM, LT4, GE4, EQ3, S1, SM31, Q24, G16, DUM2 = range(13)
+    I1, I2k, In2k, Ih = c("I1"), c("I2k"), c("In2k"), c("Ih")
+    xm = lambda o, n: c("XM", 16 + o, 16 + o + n)
+    m143 = lambda s: c(s, 0, 143)
+
+    load("ac", c("cnts", p=(0, 8)), T.cnt[:], "cnt", 0)
+    load("ac", c("stks"), T.stk[:], "stk", 1e5)
+    load("sy", c("labs", 0, 1024), T.lab[:, 0:1024], "lab0", 5e5)
+    load("sy", c("labs", 1024, V), T.lab[:, 1024:V], "lab1", 5e5)
+    load("sy", c("nbs"), T.nb[:], "nb", 1e6)
+    load("sy", c("W"), T.ln[:], "ln", 5e5)
+    iota(c("PI", 0, 1), [[0, 1]], 0, 1)
+    iota(col(PCOL), [[0, 1]], 0, 1)
+    iota(col(G16), [[0, 1]], 0, 16)
+    iota(c("GM"), [[16, 8], [0, 16]], 0, 0)
+    iota(c("XM"), [[1, 256]], -16, 0)
+    iota(c("C1"), [[-16, 16]], P, 0)
+    fill(c("A0"), 0.0)
+    fill(c("A0", 0, 1024, 16), BIG)
+    ts(c("PI", 1, 2), c("PI", 0, 1), 15, A.bitwise_and)
+    ts(c("PI", 2, 3), c("PI", 0, 1), 2, A.arith_shift_right, 3, A.bitwise_and)
+    cp(c("CC", ACOL, ACOL + 2), c("PI", 1, 3))
+    tt(col(GCOL), col(PCOL), col(ACOL), A.subtract)
+    for j, s in ((SM31, -31.0), (S1, 1.0), (DUM, float(V)), (DUM2, V + 16.0)):
+        act(col(j), col(ACOL), bias=s)
+    act(col(Q24), col(QCOL), scale=24.0)
+    ts(col(LT4), col(ACOL), 4.0, A.is_lt)
+    ts(col(GE4), col(ACOL), 4.0, A.is_ge)
+    ts(col(EQ3), col(ACOL), 3.0, A.is_equal)
+    ts(c("REP", p=(0, 8)), c("GM", p=(0, 8)), c("CC", G16, G16 + 1, p=(0, 8)), A.is_equal)
+    ts(m143("Mh"), xm(-15, 143), col(GCOL), A.is_equal)
+    ts(m143("M3h"), m143("Mh"), col(EQ3), A.mult)
+    cp(m143("M1"), m143("Mh"))
+    act(m143("M16"), m143("M1"), scale=0.0625)
+    act(m143("MK4"), m143("M1"), scale=4096.0)
+    act(m143("Q15"), m143("M1"), scale=-1.0)
+    ts(c("IW", 0, 140), xm(-12, 140), col(PCOL), A.is_equal)
+    I32 = c("IW", 12, 140)
+    cp(Ih, I32)
+    act(c("IW4", 0, 140), c("IW", 0, 140), scale=col(LT4))
+    for nm, s in (("I1", 1.0), ("In1", -1.0), ("I2k", 2048.0), ("In2k", -2048.0), ("I4", 4.0), ("In4", -4.0)):
+        act(c(nm), I32, scale=s)
+    act(c("B4", 0, 128), I32, scale=-32.0)
+    cp(c("ZO"), xm(0, 64))
+    ts(c("ONES"), c("GM"), col(GCOL), A.is_equal)
+    ts(c("NB"), xm(0, 16), col(ACOL), A.is_equal, -1.0, A.mult)
+    for b in range(16):
+        ts(c("NS", 128 * b, 128 * b + 128), c("ONES"), c("NB", b, b + 1), A.mult)
+    ts(c("LE"), xm(0, 16), col(ACOL), A.is_le)
+    for nm, n, o in (("TZ", 7, 0), ("TJ", 12, 24)):
+        iota(c("SG", o, o + 3 * n), [[1, 3], [0, n]], -1, 0)
+        act(c("SG", o, o + 3 * n), c("SG", o, o + 3 * n), F.Abs, scale=0.5)
+        for b in range(16):
+            act(c(nm, 3 * n * b, 3 * n * b + 3 * n), c("SG", o, o + 3 * n), scale=c("LE", b, b + 1))
+    ts(c("Zt", 0, 128), xm(0, 128), col(PCOL), A.is_ge)
+    tt(c("Zt", 0, 128), c("Zt", 0, 128), c("ONES"), A.mult)
+    tt(c("TR1"), c("Zt", 0, 128), c("B4", 0, 128), A.add)
+    act(c("TR2"), c("TR1"), scale=2048.0)
+    ts(m143("PQ"), xm(-16, 143), col(GCOL), A.is_equal)
+    tt(m143("PQ"), m143("PQ"), m143("Q15"), A.add)
+    fill(c("ONE"), 1.0)
+    ts(c("C1"), c("C1"), col(ACOL), A.subtract)
+    ts(c("QS"), xm(0, 4), col(QCOL), A.is_equal)
+    ts(c("Bc", 0, 128), xm(4, 128), col(PCOL), A.is_equal, col(GE4), A.mult)
+    tt(c("SHI"), c("Bc", 0, 128), I32, A.subtract)
+    act(c("JC"), xm(0, 24), bias=col(Q24))
+    for qq in range(4):
+        ts(c("INV", 128 * qq, 128 * qq + 128), xm(4 * qq, 128), col(PCOL), A.is_equal, c("QS", qq, qq + 1), A.mult)
+    fill(c("RB", 96, 104), 0.0)
+    fill(c("X", V, V + 32), 0.0)
+
+    XW, v14 = c("X"), c("v16", 0, 14)
+    PA, PB, PC = c("pb0", 0, P), c("pb1", 0, P), c("pb2", 0, P)
+    PV, PS, PN = c("pb5", 0, 14), c("pb6", 0, P), c("pb7", 0, P)
+
+    def distinct(src, n, banks, tri, eq, y, off):
+        per, w = 16 // len(banks), 3 * n
+        for j, bk in enumerate(banks):
+            group([(c(bk, w * b, w * b + w), [(Ih, c(src, 0, w)),
+                                              (c("NS", 128 * (per * j + b), 128 * (per * j + b) + 128), c(src, n, 4 * n))])
+                   for b in range(per)], None)
+            piece = (w * per * j, w * per * (j + 1))
+            tt(c(eq, *piece), c(bk, 0, w * per), c(tri, *piece), A.is_equal)
+        mk = lambda b: c("MK4", 15 - b, 143 - b)
+        group(c(y[0], y[1], y[1] + 2 * n),
+              [(Ih, c(src, n, 3 * n))] + [(mk(b), c(eq, w * b, w * b + 2 * n)) for b in range(16)], True, False)
+        k = group(c(y[0], y[1] + n, y[1] + 2 * n), [(mk(b), c(eq, w * b + 2 * n, w * b + w)) for b in range(16)],
+                  False, True)
+        ts(c(off, 0, 2 * n, 2), c(y[0], y[1], y[1] + n), col(DUM), A.min)
+        ts(c(off, 1, 2 * n, 2), c(y[0], y[1] + n, y[1] + 2 * n), col(DUM2), A.min)
+        return k
+
+    def push(s, stop=False, after=(), pt=(0, P), late=()):
+        qs = c("q", P * s + pt[0], P * s + pt[1])
+        act(qs, c("pb1", *pt), F.Relu, 2048.0 * (s + 1) - 63488.0, -1.0, late)
+        group(c("pb6", *pt), [(c("Q15" if s == 15 else "PQ", 15 - s, 143 - s), qs)], False, stop, after)
+
+    def popped():
+        cp(v14, PV)
+        cp(c("V0", 0, 14), PV)
+        cp(c("K"), ind(c("nbs"), v14))
+        cp(c("Kf"), c("K"))
+        act(c("n1"), PN, F.Relu, 31.0)
+        act(c("dead"), PN, F.Relu, -256.0 * 31, -256.0)
+        act(c("r1"), c("n1"), F.Relu, col(S1), -1.0)
+        act(c("pm"), c("r1"), F.Relu, 1.0, -1.0)
+        k = group(c("pb7", 256, 270), wrap("M1", "dead", 0, P))
+        for j in range(4):
+            tt(c("Vh", 7 * j, 7 * j + 7), c("pb7", 256 + j // 2, 270, 2), c("V0", j // 2, 14, 2), A.add)
+        distinct("Vh", 7, ["pb5"], "TZ", "eqz", ("pb5", 352), "zoff")
+        return [k]
+
+    def lengths():
+        for k in range(4):
+            group(c("pb%d" % k), [(c("In1"), c("W", 512 * k, 512 * k + 512))], True, k >= DPE)
+
+    ts(c("cntb", p=(0, 8)), c("cnts", p=(0, 8)), 32.0, A.subtract)
+    group(PN, [(c("REP", p=(0, 8)), c("cntb", p=(0, 8)))])
+    ts(c("m2"), PN, col(SM31), A.is_equal)
+    tt(c("T2"), c("m2"), c("stks"), A.mult)
+    group(PV, wrap("Mh", "T2", 0, P))
+    cp(c("X", 0, 1024), c("labs", 0, 1024))
+    cp(c("X", 1024, V), c("labs", 1024, V))
+    popped()
+    lengths()
+    tt(c("Sold"), c("pm"), c("stks"), A.mult)
+
+    for t in range(STEPS):
+        last = t == STEPS - 1
+        ms, mr, ls, lr, cs, cr, js, jr = (x + str(t) for x in ("ms", "mr", "ls", "lr", "cs", "cr", "js", "jr"))
+        wide = [(16 * l0, 16 * l1) for l0, l1 in CH]
+        gather = {"x": lambda k, af: act(c("G", *wide[k]), ind(XW, c("K", *CH[k])), after=af),
+                  "d": lambda k, af: act(c("Dg", *wide[k]), ind(c("D"), c("K", *CH[k])), after=af)}
+        prev = [gather["x"](0, [])]
+        for k in range(4):
+            piece = (512 * k, 512 * k + 512)
+            if k < DPE:
+                group(c("pb%d" % k), [(I32, c("X", *piece))], False, True)
+                prev = [act(c("D", *piece), c("pb%d" % k), after=prev)]
+            else:
+                tt(c("D", *piece), c("X", *piece), c("pb%d" % k), A.add)
+        for kind, k in GORDER:
+            prev = [gather[kind](k, prev)]
+        for k, (l0, l1) in enumerate(CH):
+            vk = c("v16", l0 // 16, l1 // 16)
+            scan(c("SO", *wide[k]), c("A0", 0, 16 * (l1 - l0)), c("G", *wide[k]), 0.0, A.add, A.min)
+            tt(c("Zt", l0, l1), ind(c("W"), vk), c("SO", 16 * l0 + 15, 16 * l1, 16), A.add)
+            tt(c("Z", l0, l1), ind(XW, vk), c("Zt", l0, l1), A.min)
+            tt(c("Ind", *wide[k]), ind(c("Z", l0, l1), c("ZO", 0, l1 - l0)), c("Dg", *wide[k]), A.is_lt)
+            hb = c("pb4" if k % 2 == 0 else "pb3", l0, l1)
+            group(hb, [(c("M1", 15 - i, 143 - i), c("Ind", 16 * l0 + i, 16 * l1, 16)) for i in range(16)])
+            tt(c("hit", l0, l1), hb, c("dead", l0, l1), A.is_gt)
+        for j in range(7):
+            cp(ind(XW, c("zoff", 2 * j, 2 * j + 2)), c("Z", 32 * j, 32 * j + 32))
+        for pt in PARTS:
+            group(c("pb0", *pt), [(I1, c("n1", *pt))], True, False)
+            group(c("pb0", *pt), [(c("ONES"), c("hit", *pt))], False, True)
+            group(c("pb1", *pt), [(I2k, c("n1", *pt)), (Ih, c("Kf", *pt))], True, False)
+            group(c("pb1", *pt), [(c("TR2"), c("hit", *pt))], False, True)
+            group(c("pb6", *pt), [(Ih, c("Sold", *pt)), (I2k, c("r1", *pt))], True, False)
+            for s in range(4):
+                push(s, pt=pt)
+            act(c("r2", *pt), c("pb0", *pt), F.Relu, col(S1), -1.0)
+            group(c("pb6", *pt), [(In2k, c("r2", *pt))], False, True)
+            act(c("B4", *pt), c("pb6", *pt))
+        ts(c("RG", P, 2 * P), PA, 5.0, A.is_lt)
+        ts(c("nnm"), PA, 16.0, A.min, 32.0, A.subtract)
+        scan(c("RG", 0, P), c("ONE"), c("RG", P, 2 * P), -1.0, A.add, A.subtract)
+        ts(c("RG", 3 * P, 4 * P), c("nnm"), -32.0, A.is_gt)
+        scan(c("RG", 2 * P, 3 * P), c("ONE"), c("RG", 3 * P, 4 * P), -1.0, A.add, A.subtract)
+        group(c("pb5", 0, 28), wrap("M16", "RG", 0, 2 * P))
+        tt(c("tw", 0, 14), c("pb5", 14, 28), c("C1", 0, 14), A.mult)
+        tt(c("tw", 16, 30), c("pb5", 0, 14), c("tw", 0, 14), A.add)
+        cp(c("pos", 0, 14), c("tw", 16, 30))
+        act(c(cs, 0, 2), c("RG", P - 1, 3 * P, 2 * P), bias=0.5)
+        exchange(t, c(cr), c(cs), "r%dc" % t)
+        ts(c("cio", 0, 1), c(cr, 0, 1), c(cs, 1, 2), A.min, 95.5, A.min)
+        ts(c("cio", 1, 2), c(cr, 1, 2), c(cs, 0, 1), A.min, 95.5, A.min)
+        ts(c("inval"), c("JC"), c("cio", 1, 2), A.is_gt, 4096.0, A.mult)
+        cp(ind(c("Bc"), c("pos", 0, 14)), c("B4"))
+        PU = c("pb4", 256, 280)
+        pu = [group(PU, [(c("IW4", 12 - 4 * qq, 140 - 4 * qq), c("Bc", 24 * qq, 24 * qq + 24)) for qq in range(4)])]
+        cp(c(ms, 0, 24), PU)
+        cp(c("U16"), PU)
+        exchange(t, c(mr), c(ms), "r%dn" % t)
+        for hh in range(2):
+            half = (192 * hh, 192 * hh + 192)
+            act(c(ls, *half), ind(XW, c("U16", 12 * hh, 12 * hh + 12)))
+            exchange(t, c(lr, *half), c(ls, *half), "r%d%s" % (t, "ab"[hh]))
+        for j in range(4):
+            tt(c("Uh", 12 * j, 12 * j + 12), c("pb4", 256 + j // 2, 280, 2), c("inval", j // 2, 24, 2), A.max)
+        pu.append(distinct("Uh", 12, ["pb7", "pb3"], "TJ", "eqj", ("pb4", 128), js))
+        exchange(t, c(jr), c(js), "r%dj" % t)
+        PE_ = c("pb0", 288, 302)
+        group(PE_, wrap("M16", "RG", 2 * P, 3 * P), True, False)
+        group(PE_, wrap("MK4", "RG", 3 * P, 4 * P), False, True)
+        ts(c("epos", 0, 14), PE_, 96.0, A.min)
+        if not last:
+            group(PC, [(I1, c("n1")), (c("TR1"), c("hit")), (c("In1"), c("nnm"))])
+            act(c("ab1"), PC, F.Abs)
+            act(c("mt"), c("ab1"), F.Relu, 1.0, -1.0)
+            ts(c("m2"), c("nnm"), col(SM31), A.is_equal)
+            tt(c("T1"), c("mt"), c("Kf"), A.mult)
+            tt(c("T2"), c("m2"), c("Sold"), A.mult)
+            group(PV, wrap("Mh", "T1", 0, P), True, False)
+            group(PV, wrap("Mh", "T2", 0, P), False, False)
+        cp(c("Uf"), c(mr))
+        cp(c("Uq"), c(mr))
+        group([(c("pb4", 24 * qq, 24 * qq + 24), [(c("INV", 128 * qq, 128 * qq + 128), c("Uf"))]) for qq in range(4)],
+              None)
+        act(c("MK"), xm(0, 112), F.Sign, c("cio", 0, 1), -1.0)
+        tt(c("RB", 0, 96), c("pb4", 0, 96), c("MK", 0, 96), A.mult)
+        act(c("GW"), xm(0, P), F.Sign, c("cio", 1, 2), -1.0)
+        ts(c("Rg"), ind(c("RB"), c("epos", 0, 14)), 0.0, A.max)
+        late = [act(c("recv"), ind(c("MK"), c("epos", 0, 14)), F.Relu),
+                act(c("giv"), ind(c("GW"), c("pos", 0, 14)), F.Relu)]
+        pn = group(PN, [(I1, c("nnm")), (c("I4"), c("recv")), (c("In4"), c("giv"))])
+        if not last:
+            pu += [pn, group(PV, wrap("M3h", "Rg", 0, P), False, True)]
+            pu += popped()
+        group(PS, [(I32, c("B4"))], True, False, pu[:1])
+        for s in range(4, 16):
+            push(s, s == 15, pu if s >= EARLY else pu[:1], late=late if s >= LATE else ())
+        tt(c("Bg"), PS, c("giv"), A.mult)
+        act(c("ostk"), PS)
+        group(PS, [(I32, c("ostk")), (c("SHI"), c("Bg")), (Ih, c("Rg"))])
+        for hh in range(2):
+            half = (192 * hh, 192 * hh + 192)
+            tt(c("jm", *half), ind(XW, c("Uq", 12 * hh, 12 * hh + 12)), c(lr, *half), A.min)
+        for j in range(12):
+            cp(ind(XW, c(jr, 2 * j, 2 * j + 2)), c("jm", 32 * j, 32 * j + 32))
+        if not last:
+            lengths()
+            tt(c("Sold"), PS, c("pm"), A.mult)
+        else:
+            act(c("ocnt"), PN, F.Identity, 32.0)
+            store("ac", T.ycnt[:], (T["ocnt"][0:128:16, :],) + c("ocnt")[1:], "ycnt", 0)
+            act(c("ostk"), PS)
+            store("ac", T.ystk[:], c("ostk"), "ystk", 1e5)
+            store("sy", T.ylab[:], c("X", 0, V), "ylab", 1e6)
+
+    if "order" not in _PLAN:
+        _PLAN["order"] = order_calls(ops)
+    order, extra = _PLAN["order"]
+    place = {k: j for j, k in enumerate(order)}
+    keyof = lambda k: ops[k]["sem"] or ops[k]["q"]
+    need, covered, signal = {}, {}, set()
+    for k in order:
+        best = {}
+        if ops[k]["q"] != "rx":
+            for d in ops[k]["wait"] | extra[k]:
+                if place[d] > place.get(best.get(keyof(d)), -1):
+                    best[keyof(d)] = d
+        need[k] = {}
+        for key, d in best.items():
+            if covered.get((ops[k]["q"], key), -1) < place[d]:
+                covered[(ops[k]["q"], key)] = place[d]
+                need[k][key] = d
+                signal.add(d)
+    total, value = {}, {}
+    for k in order:
+        if ops[k]["sem"] or k in signal:
+            total[keyof(k)] = total.get(keyof(k), 0) + ops[k]["inc"]
+            value[k] = total[keyof(k)]
+    for k in order:
+        o = ops[k]
+        if o["q"] == "rx":
+            continue
+        e = Q[o["q"]]
+        for key, d in need[k].items():
+            e.wait_ge(T.sem[key], value[d])
+        ins = o["call"](e)
+        if o["sem"] != "sent" and k in value:
+            ins.then_inc(T.sem[keyof(k)], o["inc"])
+    for key, n in total.items():
+        g.wait_ge(T.sem[key], n)

@@ -1,18 +1,20 @@
+import numpy as np
 from concourse.mybir import AluOpType as A, ActivationFunctionType as F
 
 V, P, STEPS = 2048, 224, 3
 CH = [(0, 64), (64, 128), (128, 192), (192, 224)]
 DPE = 1
-GORDER = [("x", 1), ("d", 0), ("x", 2), ("d", 1), ("x", 3), ("d", 2), ("d", 3)]
+ZPE, GV, HINT = True, [], (1, 2)
+GORDER = ["x1 d0 x2 d1 x3 d2 d3", "x1 d0 x2 d1 x3 d2 d3"]
 BIG = 2097152.0
 f32, b16, h16, i32, u16 = "float32", "bfloat16", "float16", "int32", "uint16"
 _B = {
     "nbs": (V, i32), "labs": (V, i32), "W": (V, b16), "X": (V + 32, f32), "D": (V, f32),
     "stks": (P, i32), "cnts": (P, i32), "cntb": (P, b16),
-    "G": (P * 16, f32), "A0": (1024, b16), "SO": (P * 16, f32), "Dg": (P * 16, f32), "Ind": (P * 16, b16),
+    "G": (P * 16, f32), "A0": (1536, b16), "SO": (P * 16, f32), "Dg": (P * 16, f32), "Ind": (P * 16, b16),
     "Zt": (P, f32), "Z": (P, f32),
     "XM": (256, f32), "GM": (128, f32), "PI": (4, i32), "CC": (16, f32), "NB": (16, f32), "QS": (4, f32),
-    "TJ": (576, f32), "TZ": (336, f32), "ZO": (64, u16), "C1": (16, f32), "JC": (24, f32), "ONE": (P, b16),
+    "TJ": (576, f32), "TZ": (336, f32), "ZO": (96, u16), "C1": (16, f32), "JC": (24, f32), "ONE": (P, b16),
     "M1": (144, b16), "M16": (144, b16), "MK4": (144, b16), "Mh": (144, h16), "M3h": (144, h16),
     "PQ": (144, f32), "Q15": (144, f32), "IW": (144, f32),
     "I1": (128, b16), "In1": (128, b16), "I2k": (128, b16), "In2k": (128, b16), "I4": (128, b16), "In4": (128, b16),
@@ -23,13 +25,12 @@ _B = {
     "eqz": (336, b16), "zoff": (14, u16), "hit": (P, b16), "RG": (4 * P, b16), "nnm": (P, b16),
     "q": (16 * P, f32), "B4": (P, f32), "Bc": (P, f32), "tw": (32, f32), "pos": (16, u16), "epos": (16, u16),
     "U16": (24, u16), "mt": (P, b16), "m2": (P, b16), "ab1": (P, b16), "T1": (P, h16), "T2": (P, h16),
-    "Uh": (48, h16), "Uq": (24, u16), "cio": (2, f32), "MK": (112, b16), "inval": (24, f32), "RB": (104, f32),
+    "Uh": (48, h16), "Uq": (24, u16), "cio": (2, f32), "MK": (112, b16), "inval": (24, b16), "RB": (104, f32),
     "Rg": (P, h16), "eqj": (576, b16), "GW": (P, b16), "recv": (P, b16), "giv": (P, b16),
     "jm": (384, f32), "Bg": (P, h16), "ostk": (P, f32), "ocnt": (P, f32), "Uf": (24, h16),
-    "LE": (16, f32), "SG": (64, f32),
 }
 for _t in range(STEPS):
-    _B.update({"ms%d" % _t: (24, f32), "mr%d" % _t: (24, f32), "ls%d" % _t: (384, f32), "lr%d" % _t: (384, f32),
+    _B.update({"ls%d" % _t: (408, f32), "lr%d" % _t: (408, f32),
                "cs%d" % _t: (2, f32), "cr%d" % _t: (2, f32), "js%d" % _t: (24, u16), "jr%d" % _t: (24, u16)})
 SCRATCH = {k: ("sbuf", [128, n], d) for k, (n, d) in _B.items()}
 for _k in range(8):
@@ -37,11 +38,12 @@ for _k in range(8):
 
 LOADS = ["stk", "cnt", "lab0", "lab1", "nb", "ln", "ylab", "ystk", "ycnt"]
 SEMAPHORES = (["ve", "ac", "pe", "po", "sent"] + ["d_" + s for s in LOADS]
-              + ["r%d%s" % (t, s) for t in range(STEPS) for s in "cnabj"])
+              + ["r%d%s" % (t, s) for t in range(STEPS) for s in "cabj"])
 
-CYC, FIX, GATHER, SCATTER, PECYC, WAKE = 1.04e-3, 0.06, 1.56, 3.8, 0.52e-3, 0.1
-HBM, LINK, ISSUE, FLY, SLACK = 200e3, 60e3, 1.0, 2.0, 0.1
-ROUNDS, MIX, EARLY, LATE, SHAKE = 40, 0.5, 4, 8, 1.5
+CYC, GATHER, SCATTER = np.array([0.85e-3, 1.0e-3]), np.array([1.7, 1.3]), np.array([3.0, 4.2])
+PECYC, HBM, LINK, FLY = np.array([0.42e-3, 0.52e-3]), np.array([400e3, 260e3]), np.array([100e3, 60e3]), np.array([1.4, 2.0])
+FIX, WAKE, ISSUE, SLACK, MOVES, EAGER = 0.06, 0.1, 1.0, 0.1, 5000, 1.0
+ROUNDS, MIX, EARLY, LATE, SHAKE = 16, 0.5, 16, 16, 1.5
 PARTS = [(0, 128), (128, P)]
 _PLAN = {}
 
@@ -97,8 +99,60 @@ def order_calls(ops):
         else:
             back = plan(succ, pred, made[1])[1]
             rank = [MIX * x + (1 - MIX) * y for x, y in zip(back, rank)]
-    _PLAN["time"] = best[0]
-    return best[2], best[3]
+    sets = [([float(o["both"][0][s]) for o in ops],
+             [[(d, float(ops[d]["both"][1][s]) + WAKE if d in o["wait"] else 0.0) for d in o["after"]] for o in ops],
+             [float(o["both"][1][s]) for o in ops]) for s in range(2)]
+    queue, banks = [o["q"] for o in ops], [sorted(o["banks"]) for o in ops]
+
+    def length(order):
+        total = 0.0
+        for cost, before, lat in sets:
+            end, free, bank, worst = [0.0] * n, {}, {}, 0.0
+            for k in order:
+                q = queue[k]
+                t = free.get(q, 0.0)
+                for d, lag in before[k]:
+                    if end[d] + lag > t:
+                        t = end[d] + lag
+                for b in banks[k]:
+                    x = bank.get(b)
+                    if x and x[0] != q and x[1] + WAKE > t:
+                        t = x[1] + WAKE
+                t += cost[k]
+                end[k] = free[q] = t
+                for b in banks[k]:
+                    bank[b] = (q, t)
+                if t + lat[k] > worst:
+                    worst = t + lat[k]
+            total += worst + EAGER * sum(end) / n
+        return total
+
+    order = best[2]
+    now = length(order)
+    ahead, behind = [o["after"] for o in ops], [{s for s, lag in x} for x in succ]
+    for _ in range(MOVES):
+        seed = (seed * 1103515245 + 12345) % 2147483648
+        i = (seed >> 8) % n
+        k, step = order[i], 1 if seed & 64 else -1
+        j, hops, stop = i, 1 + (seed >> 3) % 3, behind[k] if step > 0 else ahead[k]
+        to = i
+        while hops and 0 <= j + step < n and order[j + step] not in stop:
+            j += step
+            if queue[order[j]] == queue[k]:
+                hops, to = hops - 1, j
+        if to != i:
+            new = order[:i] + order[i + 1:]
+            new.insert(to, k)
+            t = length(new)
+            if t <= now:
+                order, now = new, t
+    extra, seen = [set() for _ in range(n)], {}
+    for k in order:
+        for b in banks[k]:
+            extra[k] |= {d for q, d in seen.get(b, {}).items() if q != queue[k]}
+            seen.setdefault(b, {})[queue[k]] = k
+    _PLAN["time"] = now / 2
+    return order, extra
 
 
 def rank_program(g, core, T, topo):
@@ -106,7 +160,7 @@ def rank_program(g, core, T, topo):
     if rank is None:
         return
     Q = {"ve": g.vector, "ac": g.scalar, "pe": g.tensor, "po": g, "sy": g.sync}
-    ops, hist = [], {}
+    ops, hist, soon = [], {}, {}
 
     def c(name, a=0, b=None, st=1, p=None):
         b = SCRATCH[name][1][1] if b is None else b
@@ -134,7 +188,9 @@ def rank_program(g, core, T, topo):
                     order.add(k2)
         for (name, lo, hi, st), w in acc:
             hist.setdefault(name, []).append((lo, hi, st, k, w))
-        ops.append(dict(q=q, call=call, sem=sem, inc=inc, wait=wait, after=wait | order, cost=cost, lat=lat,
+        both = (cost + np.zeros(2), lat + np.zeros(2))
+        ops.append(dict(q=q, call=call, sem=sem, inc=inc, wait=wait, after=wait | order, both=both,
+                        cost=float(both[0].mean()), lat=float(both[1].mean()),
                         open=opened, banks={r[0] for r, w in acc if r[0].startswith("pb")}))
         return k
 
@@ -195,7 +251,7 @@ def rank_program(g, core, T, topo):
     landed = [2.0]
 
     def load(q, o, src, s, nbytes):
-        landed[0] += nbytes / HBM
+        landed[0] = landed[0] + nbytes / HBM
         prev = [k for k, x in enumerate(ops) if x["q"] == q]
         rec(q, lambda e: e.dma_start(o[0], src), [o], [], 0.05, "d_" + s, 16, landed[0], prev[-1:])
 
@@ -219,7 +275,7 @@ def rank_program(g, core, T, topo):
         rec("rx", None, [dst], [], 512 * src[3] / LINK, s, len(common(peers[t])), FLY, [k] + prev[-1:])
 
     col = lambda j: c("CC", j, j + 1)
-    PCOL, ACOL, QCOL, GCOL, DUM, LT4, GE4, EQ3, S1, SM31, Q24, G16, DUM2 = range(13)
+    PCOL, ACOL, QCOL, GCOL, DUM, LT4, GE4, EQ3, S1, SM31, Q24, G16, DUM2, HALF = range(14)
     I1, I2k, In2k, Ih = c("I1"), c("I2k"), c("In2k"), c("Ih")
     xm = lambda o, n: c("XM", 16 + o, 16 + o + n)
     m143 = lambda s: c(s, 0, 143)
@@ -236,15 +292,16 @@ def rank_program(g, core, T, topo):
     iota(c("GM"), [[16, 8], [0, 16]], 0, 0)
     iota(c("XM"), [[1, 256]], -16, 0)
     iota(c("C1"), [[-16, 16]], P, 0)
-    fill(c("A0"), 0.0)
-    fill(c("A0", 0, 1024, 16), BIG)
+    most = max(l1 - l0 for l0, l1 in CH)
+    fill(c("A0", 0, 16 * most), 0.0)
+    fill(c("A0", 0, 16 * most, 16), BIG)
     ts(c("PI", 1, 2), c("PI", 0, 1), 15, A.bitwise_and)
     ts(c("PI", 2, 3), c("PI", 0, 1), 2, A.arith_shift_right, 3, A.bitwise_and)
     cp(c("CC", ACOL, ACOL + 2), c("PI", 1, 3))
     tt(col(GCOL), col(PCOL), col(ACOL), A.subtract)
     for j, s in ((SM31, -31.0), (S1, 1.0), (DUM, float(V)), (DUM2, V + 16.0)):
         act(col(j), col(ACOL), bias=s)
-    act(col(Q24), col(QCOL), scale=24.0)
+    act(col(Q24), col(QCOL), bias=4.0)
     ts(col(LT4), col(ACOL), 4.0, A.is_lt)
     ts(col(GE4), col(ACOL), 4.0, A.is_ge)
     ts(col(EQ3), col(ACOL), 3.0, A.is_equal)
@@ -262,17 +319,18 @@ def rank_program(g, core, T, topo):
     for nm, s in (("I1", 1.0), ("In1", -1.0), ("I2k", 2048.0), ("In2k", -2048.0), ("I4", 4.0), ("In4", -4.0)):
         act(c(nm), I32, scale=s)
     act(c("B4", 0, 128), I32, scale=-32.0)
-    cp(c("ZO"), xm(0, 64))
+    cp(c("ZO"), xm(0, 96))
     ts(c("ONES"), c("GM"), col(GCOL), A.is_equal)
     ts(c("NB"), xm(0, 16), col(ACOL), A.is_equal, -1.0, A.mult)
     for b in range(16):
         ts(c("NS", 128 * b, 128 * b + 128), c("ONES"), c("NB", b, b + 1), A.mult)
-    ts(c("LE"), xm(0, 16), col(ACOL), A.is_le)
-    for nm, n, o in (("TZ", 7, 0), ("TJ", 12, 24)):
-        iota(c("SG", o, o + 3 * n), [[1, 3], [0, n]], -1, 0)
-        act(c("SG", o, o + 3 * n), c("SG", o, o + 3 * n), F.Abs, scale=0.5)
-        for b in range(16):
-            act(c(nm, 3 * n * b, 3 * n * b + 3 * n), c("SG", o, o + 3 * n), scale=c("LE", b, b + 1))
+    act(col(HALF), col(ACOL), bias=0.5)
+    for nm, n in (("TZ", 7), ("TJ", 12)):
+        iota(c(nm), [[1, 16], [0, 3 * n]], 0, 0)
+        rec("po", lambda e, x=c(nm), n=n: e.affine_select(x[0], x[0], [[0, 16], [1, 3], [0, n]], A.not_equal, 100.0, -1, 0),
+            [c(nm)], [c(nm)], 0.17 + 2 * CYC * 48 * n)
+        act(c(nm), c(nm), F.Sign, col(HALF), -1.0)
+        act(c(nm), c(nm), F.Relu, scale=0.5)
     ts(c("Zt", 0, 128), xm(0, 128), col(PCOL), A.is_ge)
     tt(c("Zt", 0, 128), c("Zt", 0, 128), c("ONES"), A.mult)
     tt(c("TR1"), c("Zt", 0, 128), c("B4", 0, 128), A.add)
@@ -284,7 +342,8 @@ def rank_program(g, core, T, topo):
     ts(c("QS"), xm(0, 4), col(QCOL), A.is_equal)
     ts(c("Bc", 0, 128), xm(4, 128), col(PCOL), A.is_equal, col(GE4), A.mult)
     tt(c("SHI"), c("Bc", 0, 128), I32, A.subtract)
-    act(c("JC"), xm(0, 24), bias=col(Q24))
+    act(c("JC", 0, 12), xm(0, 12), bias=col(QCOL), scale=8.0)
+    act(c("JC", 12, 24), xm(0, 12), bias=col(Q24), scale=8.0)
     for qq in range(4):
         ts(c("INV", 128 * qq, 128 * qq + 128), xm(4 * qq, 128), col(PCOL), A.is_equal, c("QS", qq, qq + 1), A.mult)
     fill(c("RB", 96, 104), 0.0)
@@ -294,7 +353,7 @@ def rank_program(g, core, T, topo):
     PA, PB, PC = c("pb0", 0, P), c("pb1", 0, P), c("pb2", 0, P)
     PV, PS, PN = c("pb5", 0, 14), c("pb6", 0, P), c("pb7", 0, P)
 
-    def distinct(src, n, banks, tri, eq, y, off):
+    def distinct(src, n, banks, tri, eq, y, off, more=None):
         per, w = 16 // len(banks), 3 * n
         for j, bk in enumerate(banks):
             group([(c(bk, w * b, w * b + w), [(Ih, c(src, 0, w)),
@@ -303,10 +362,12 @@ def rank_program(g, core, T, topo):
             piece = (w * per * j, w * per * (j + 1))
             tt(c(eq, *piece), c(bk, 0, w * per), c(tri, *piece), A.is_equal)
         mk = lambda b: c("MK4", 15 - b, 143 - b)
-        group(c(y[0], y[1], y[1] + 2 * n),
-              [(Ih, c(src, n, 3 * n))] + [(mk(b), c(eq, w * b, w * b + 2 * n)) for b in range(16)], True, False)
-        k = group(c(y[0], y[1] + n, y[1] + 2 * n), [(mk(b), c(eq, w * b + 2 * n, w * b + w)) for b in range(16)],
-                  False, True)
+        for j in range(len(banks)):
+            bs = range(per * j, per * (j + 1))
+            group(c(y[0], y[1], y[1] + 2 * n), [(Ih, c(src, n, 3 * n))] * (j == 0)
+                  + [(mk(b), c(eq, w * b, w * b + 2 * n)) for b in bs] + (more if j else []), j == 0, False)
+            k = group(c(y[0], y[1] + n, y[1] + 2 * n), [(mk(b), c(eq, w * b + 2 * n, w * b + w)) for b in bs],
+                      False, j == len(banks) - 1)
         ts(c(off, 0, 2 * n, 2), c(y[0], y[1], y[1] + n), col(DUM), A.min)
         ts(c(off, 1, 2 * n, 2), c(y[0], y[1] + n, y[1] + 2 * n), col(DUM2), A.min)
         return k
@@ -325,11 +386,13 @@ def rank_program(g, core, T, topo):
         act(c("dead"), PN, F.Relu, -256.0 * 31, -256.0)
         act(c("r1"), c("n1"), F.Relu, col(S1), -1.0)
         act(c("pm"), c("r1"), F.Relu, 1.0, -1.0)
-        k = group(c("pb7", 256, 270), wrap("M1", "dead", 0, P))
+        group(c("pb7", 256, 270), wrap("M1", "dead", 0, P))
         for j in range(4):
             tt(c("Vh", 7 * j, 7 * j + 7), c("pb7", 256 + j // 2, 270, 2), c("V0", j // 2, 14, 2), A.add)
         distinct("Vh", 7, ["pb5"], "TZ", "eqz", ("pb5", 352), "zoff")
-        return [k]
+        k = len(ops)
+        soon["test"], soon["offsets"] = [k - 5], [k - 2, k - 1]
+        return [k - 6]
 
     def lengths():
         for k in range(4):
@@ -348,11 +411,14 @@ def rank_program(g, core, T, topo):
 
     for t in range(STEPS):
         last = t == STEPS - 1
-        ms, mr, ls, lr, cs, cr, js, jr = (x + str(t) for x in ("ms", "mr", "ls", "lr", "cs", "cr", "js", "jr"))
+        ls, lr, cs, cr, js, jr = (x + str(t) for x in ("ls", "lr", "cs", "cr", "js", "jr"))
         wide = [(16 * l0, 16 * l1) for l0, l1 in CH]
         gather = {"x": lambda k, af: act(c("G", *wide[k]), ind(XW, c("K", *CH[k])), after=af),
                   "d": lambda k, af: act(c("Dg", *wide[k]), ind(c("D"), c("K", *CH[k])), after=af)}
         prev = [gather["x"](0, [])]
+        if ZPE:
+            act(c("mt"), ind(c("W"), v14))
+            prev = [act(c("Zt"), ind(XW, v14), after=prev)]
         for k in range(4):
             piece = (512 * k, 512 * k + 512)
             if k < DPE:
@@ -360,17 +426,32 @@ def rank_program(g, core, T, topo):
                 prev = [act(c("D", *piece), c("pb%d" % k), after=prev)]
             else:
                 tt(c("D", *piece), c("X", *piece), c("pb%d" % k), A.add)
-        for kind, k in GORDER:
-            prev = [gather[kind](k, prev)]
+        for kind, k in [(x[0], int(x[1])) for x in GORDER[t > 0].split()]:
+            if kind == "x" and k in GV:
+                cp(c("G", *wide[k]), ind(XW, c("K", *CH[k])))
+            else:
+                prev = [gather[kind](k, prev)]
         for k, (l0, l1) in enumerate(CH):
             vk = c("v16", l0 // 16, l1 // 16)
             scan(c("SO", *wide[k]), c("A0", 0, 16 * (l1 - l0)), c("G", *wide[k]), 0.0, A.add, A.min)
-            tt(c("Zt", l0, l1), ind(c("W"), vk), c("SO", 16 * l0 + 15, 16 * l1, 16), A.add)
-            tt(c("Z", l0, l1), ind(XW, vk), c("Zt", l0, l1), A.min)
+            if ZPE:
+                group(c("pb2", l0, l1), [(I1, c("mt", l0, l1)), (I32, c("SO", 16 * l0 + 15, 16 * l1, 16))])
+                tt(c("Z", l0, l1), c("Zt", l0, l1), c("pb2", l0, l1), A.min)
+            else:
+                tt(c("Zt", l0, l1), ind(c("W"), vk), c("SO", 16 * l0 + 15, 16 * l1, 16), A.add)
+                tt(c("Z", l0, l1), ind(XW, vk), c("Zt", l0, l1), A.min)
             tt(c("Ind", *wide[k]), ind(c("Z", l0, l1), c("ZO", 0, l1 - l0)), c("Dg", *wide[k]), A.is_lt)
-            hb = c("pb4" if k % 2 == 0 else "pb3", l0, l1)
-            group(hb, [(c("M1", 15 - i, 143 - i), c("Ind", 16 * l0 + i, 16 * l1, 16)) for i in range(16)])
-            tt(c("hit", l0, l1), hb, c("dead", l0, l1), A.is_gt)
+            if k < 2:
+                ops[-1]["after"] |= set(soon["test" if k == 0 else "offsets"])
+            if t > 0 and k == HINT[0]:
+                ops[-1]["after"] |= set(soon["stack"])
+            if k == HINT[1]:
+                ops[-1]["after"] |= set(soon["hit"])
+            j, pt = [(j, pt) for j, pt in enumerate(PARTS) if pt[0] <= l0 < pt[1]][0]
+            hb = "pb4" if j % 2 == 0 else "pb3"
+            group(c(hb, l0, l1), [(c("M1", 15 - i, 143 - i), c("Ind", 16 * l0 + i, 16 * l1, 16)) for i in range(16)])
+            if l1 == pt[1]:
+                soon["hit"] = [tt(c("hit", *pt), c(hb, *pt), c("dead", *pt), A.is_gt)]
         for j in range(7):
             cp(ind(XW, c("zoff", 2 * j, 2 * j + 2)), c("Z", 32 * j, 32 * j + 32))
         for pt in PARTS:
@@ -400,17 +481,17 @@ def rank_program(g, core, T, topo):
         ts(c("inval"), c("JC"), c("cio", 1, 2), A.is_gt, 4096.0, A.mult)
         cp(ind(c("Bc"), c("pos", 0, 14)), c("B4"))
         PU = c("pb4", 256, 280)
-        pu = [group(PU, [(c("IW4", 12 - 4 * qq, 140 - 4 * qq), c("Bc", 24 * qq, 24 * qq + 24)) for qq in range(4)])]
-        cp(c(ms, 0, 24), PU)
+        pu = [group(PU, [(c("IW4", 12 - 4 * qq, 140 - 4 * qq), c("Bc", qq, 96, 4)) for qq in range(4)])]
         cp(c("U16"), PU)
-        exchange(t, c(mr), c(ms), "r%dn" % t)
+        cp(c(ls, 0, 24), PU)
         for hh in range(2):
-            half = (192 * hh, 192 * hh + 192)
+            half = (24 + 192 * hh, 216 + 192 * hh)
             act(c(ls, *half), ind(XW, c("U16", 12 * hh, 12 * hh + 12)))
-            exchange(t, c(lr, *half), c(ls, *half), "r%d%s" % (t, "ab"[hh]))
+            sent = (half[0] * hh, half[1])
+            exchange(t, c(lr, *sent), c(ls, *sent), "r%d%s" % (t, "ab"[hh]))
         for j in range(4):
-            tt(c("Uh", 12 * j, 12 * j + 12), c("pb4", 256 + j // 2, 280, 2), c("inval", j // 2, 24, 2), A.max)
-        pu.append(distinct("Uh", 12, ["pb7", "pb3"], "TJ", "eqj", ("pb4", 128), js))
+            cp(c("Uh", 12 * j, 12 * j + 12), c("pb4", 256 + j // 2, 280, 2))
+        pu.append(distinct("Uh", 12, ["pb7", "pb3"], "TJ", "eqj", ("pb4", 128), js, [(I1, c("inval"))]))
         exchange(t, c(jr), c(js), "r%dj" % t)
         PE_ = c("pb0", 288, 302)
         group(PE_, wrap("M16", "RG", 2 * P, 3 * P), True, False)
@@ -425,12 +506,13 @@ def rank_program(g, core, T, topo):
             tt(c("T2"), c("m2"), c("Sold"), A.mult)
             group(PV, wrap("Mh", "T1", 0, P), True, False)
             group(PV, wrap("Mh", "T2", 0, P), False, False)
-        cp(c("Uf"), c(mr))
-        cp(c("Uq"), c(mr))
+        cp(c("Uf"), c(lr, 0, 24))
+        cp(c("Uq"), c(lr, 0, 24))
         group([(c("pb4", 24 * qq, 24 * qq + 24), [(c("INV", 128 * qq, 128 * qq + 128), c("Uf"))]) for qq in range(4)],
               None)
         act(c("MK"), xm(0, 112), F.Sign, c("cio", 0, 1), -1.0)
-        tt(c("RB", 0, 96), c("pb4", 0, 96), c("MK", 0, 96), A.mult)
+        for qq in range(4):
+            tt(c("RB", qq, 96, 4), c("pb4", 24 * qq, 24 * qq + 24), c("MK", qq, 96, 4), A.mult)
         act(c("GW"), xm(0, P), F.Sign, c("cio", 1, 2), -1.0)
         ts(c("Rg"), ind(c("RB"), c("epos", 0, 14)), 0.0, A.max)
         late = [act(c("recv"), ind(c("MK"), c("epos", 0, 14)), F.Relu),
@@ -441,18 +523,18 @@ def rank_program(g, core, T, topo):
             pu += popped()
         group(PS, [(I32, c("B4"))], True, False, pu[:1])
         for s in range(4, 16):
-            push(s, s == 15, pu if s >= EARLY else pu[:1], late=late if s >= LATE else ())
+            push(s, s == 15, pu if s >= EARLY else pu[:2], late=late if s >= LATE else ())
         tt(c("Bg"), PS, c("giv"), A.mult)
-        act(c("ostk"), PS)
-        group(PS, [(I32, c("ostk")), (c("SHI"), c("Bg")), (Ih, c("Rg"))])
+        cp(c("T1"), PS)
+        group(PS, [(Ih, c("T1")), (c("SHI"), c("Bg")), (Ih, c("Rg"))])
         for hh in range(2):
             half = (192 * hh, 192 * hh + 192)
-            tt(c("jm", *half), ind(XW, c("Uq", 12 * hh, 12 * hh + 12)), c(lr, *half), A.min)
+            tt(c("jm", *half), ind(XW, c("Uq", 12 * hh, 12 * hh + 12)), c(lr, half[0] + 24, half[1] + 24), A.min)
         for j in range(12):
             cp(ind(XW, c(jr, 2 * j, 2 * j + 2)), c("jm", 32 * j, 32 * j + 32))
         if not last:
             lengths()
-            tt(c("Sold"), PS, c("pm"), A.mult)
+            soon["stack"] = [tt(c("Sold"), PS, c("pm"), A.mult)]
         else:
             act(c("ocnt"), PN, F.Identity, 32.0)
             store("ac", T.ycnt[:], (T["ocnt"][0:128:16, :],) + c("ocnt")[1:], "ycnt", 0)

@@ -2,49 +2,63 @@ import numpy as np
 from concourse.mybir import AluOpType as A, ActivationFunctionType as F
 
 V, P, STEPS = 2048, 224, 3
-CH = [(0, 64), (64, 128), (128, 192), (192, 224)]
-DPE = 1
-ZPE, GV, HINT = True, [], (1, 2)
-GORDER = ["x1 d0 x2 d1 x3 d2 d3", "x1 d0 x2 d1 x3 d2 d3"]
+DEAD, WIDE = V + 32, V + 48
+CH = [(0, 32), (32, 96), (96, 160), (160, 224)]
+PARTS = [(0, 160), (160, P)]
+SPLIT, EARLY = [256], False
+ONS = [2, 5]
+ENG = dict(own="v", H="s", hit="s", U16="s", Uh="v", Uq="s", Rg="v", v16="v", Vh="v", Kf="v", Wp="v",
+           T1="s", Wv="s", B4h="s")
+ONV, BATCH = [], 4
+HITS = [96, 160, P]
+BANKS, SUMS = [0, 7, 5, 6, 1, 2, 4], "pb0"
+NARROW = [0]
+LOW, GV = [7, 3], [1]
+TURN = [("pb3", 128 * (k % 4), 128 * (k % 4) + 128) for k in range(len(CH))]
+HV = []
+PULL = ["g2 g0 g3 g4 g5 g6 H0 H1 H2 t2 H3 t5", "g1 d s1 s0 m1 n1 m0 n0 s2 n2 m2 s3 t0 m3 n3 t1 t4 t3 t6"]
+LOADS = ["nb", "ln", "lab0", "lab1", "lab2", "lab3"]
 BIG = 2097152.0
 f32, b16, h16, i32, u16 = "float32", "bfloat16", "float16", "int32", "uint16"
+PAD = 128 * len(CH) + 64
 _B = {
-    "nbs": (V, i32), "labs": (V, i32), "W": (V, b16), "X": (V + 32, f32), "D": (V, f32),
+    "nbs": (WIDE, i32), "labs": (V, i32), "W": (WIDE, b16), "X": (WIDE, f32),
     "stks": (P, i32), "cnts": (P, i32), "cntb": (P, b16),
-    "G": (P * 16, f32), "A0": (1536, b16), "SO": (P * 16, f32), "Dg": (P * 16, f32), "Ind": (P * 16, b16),
-    "Zt": (P, f32), "Z": (P, f32),
-    "XM": (256, f32), "GM": (128, f32), "PI": (4, i32), "CC": (16, f32), "NB": (16, f32), "QS": (4, f32),
-    "TJ": (576, f32), "TZ": (336, f32), "ZO": (96, u16), "C1": (16, f32), "JC": (24, f32), "ONE": (P, b16),
-    "M1": (144, b16), "M16": (144, b16), "MK4": (144, b16), "Mh": (144, h16), "M3h": (144, h16),
-    "PQ": (144, f32), "Q15": (144, f32), "IW": (144, f32),
-    "I1": (128, b16), "In1": (128, b16), "I2k": (128, b16), "In2k": (128, b16), "I4": (128, b16), "In4": (128, b16),
+    "G": (P * 16, f32), "A0": (1024, b16), "SO": (P * 16, f32), "Wg": (P * 16, b16), "Ind": (P * 16, b16),
+    "E": (1024, h16), "E0": (1024, b16), "DV": (P, f32), "Wv": (P, f32),
+    "Mb": (PAD, f32), "Hh": (PAD, h16), "Wp": (PAD, b16), "HT": (128 * len(CH), h16),
+    "XM": (256, f32), "GM": (128, f32), "PI": (4, i32), "CC": (32, f32), "SPL": (128, b16),
+    "TJ": (576, f32), "TZ": (336, f32), "C1": (16, f32), "JC": (24, f32), "ONE": (P, b16), "RS": (P, b16),
+    "M1": (144, b16), "MP": (144, b16), "MK4": (144, b16), "Mh": (144, h16), "M35": (144, h16), "ME": (144, b16),
+    "MD": (144, b16), "PQ": (144, f32), "Q15": (144, f32), "IW": (144, f32),
+    "I1": (128, b16), "I2k": (128, b16), "In2k": (128, b16), "In4": (128, b16), "In1": (128, b16),
+    "Id": (128, b16), "Xo": (WIDE, f32), "Inf": (128, f32), "Inh": (128, h16), "IL4": (128, h16), "SE4": (128, h16),
     "Ih": (128, h16), "SHI": (128, h16), "ONES": (128, b16), "REP": (128, b16), "TR1": (128, b16), "TR2": (128, b16),
-    "IW4": (144, f32), "NS": (V, h16), "INV": (512, h16),
-    "v16": (16, u16), "Vh": (28, h16), "V0": (16, h16), "K": (P, u16), "Kf": (P, h16),
-    "n1": (P, b16), "dead": (P, b16), "r1": (P, b16), "r2": (P, b16), "pm": (P, b16), "Sold": (P, h16),
-    "eqz": (336, b16), "zoff": (14, u16), "hit": (P, b16), "RG": (4 * P, b16), "nnm": (P, b16),
-    "q": (16 * P, f32), "B4": (P, f32), "Bc": (P, f32), "tw": (32, f32), "pos": (16, u16), "epos": (16, u16),
-    "U16": (24, u16), "mt": (P, b16), "m2": (P, b16), "ab1": (P, b16), "T1": (P, h16), "T2": (P, h16),
-    "Uh": (48, h16), "Uq": (24, u16), "cio": (2, f32), "MK": (112, b16), "inval": (24, b16), "RB": (104, f32),
-    "Rg": (P, h16), "eqj": (576, b16), "GW": (P, b16), "recv": (P, b16), "giv": (P, b16),
-    "jm": (384, f32), "Bg": (P, h16), "ostk": (P, f32), "ocnt": (P, f32), "Uf": (24, h16),
+    "IW4": (144, f32), "NS": (V, h16),
+    "v16": (16, u16), "Vh": (28, h16), "K": (P, u16), "Kf": (P, h16),
+    "n1": (P, b16), "r1": (P, b16), "r2": (P, b16), "pm": (P, b16), "Sold": (P, h16),
+    "eqz": (336, b16), "zoff": (14, u16), "hit": (P, b16), "RG": (2 * P, b16), "em": (P, b16), "er": (P, b16),
+    "qu": (16 * P, u16), "qh": (16 * P, h16), "nv": (P, u16), "B4h": (P, h16), "Qh": (144, h16),
+    "IhG": (128, h16), "I2G": (128, b16), "In2G": (128, b16),
+    "nq": (P, b16), "q": (4 * P, f32), "B4": (P, f32), "B4f": (128, f32), "pos": (16, u16),
+    "epos": (16, u16), "U16": (24, u16), "mt": (P, b16), "m2": (P, b16), "T1": (P, h16), "T2": (P, h16),
+    "T3": (P, h16), "Uh": (48, h16), "Uq": (24, u16), "cio": (2, f32), "inval": (24, b16),
+    "joff": (24, u16), "Rg": (P, h16), "eqj": (576, b16), "giv": (P, b16),
+    "jm": (384, f32), "Bg": (P, h16), "ostk": (P, f32), "ocnt": (P, f32),
 }
 for _t in range(STEPS):
-    _B.update({"ls%d" % _t: (408, f32), "lr%d" % _t: (408, f32),
-               "cs%d" % _t: (2, f32), "cr%d" % _t: (2, f32), "js%d" % _t: (24, u16), "jr%d" % _t: (24, u16)})
+    _B.update({"ls%d" % _t: (384, f32), "lr%d" % _t: (384, f32), "ms%d" % _t: (456, f32), "mr%d" % _t: (248, f32)})
 SCRATCH = {k: ("sbuf", [128, n], d) for k, (n, d) in _B.items()}
 for _k in range(8):
     SCRATCH["pb%d" % _k] = ("psum", [128, 512], f32)
 
-LOADS = ["stk", "cnt", "lab0", "lab1", "nb", "ln", "ylab", "ystk", "ycnt"]
-SEMAPHORES = (["ve", "ac", "pe", "po", "sent"] + ["d_" + s for s in LOADS]
-              + ["r%d%s" % (t, s) for t in range(STEPS) for s in "cabj"])
+SEMAPHORES = (["ve", "ac", "pe", "po", "sent"] + ["d_" + s for s in LOADS + ["stk", "cnt", "ylab", "ystk", "ycnt"]]
+              + ["r%d%s" % (t, s) for t in range(STEPS) for s in "cnabj"])
 
-CYC, GATHER, SCATTER = np.array([0.85e-3, 1.0e-3]), np.array([1.7, 1.3]), np.array([3.0, 4.2])
-PECYC, HBM, LINK, FLY = np.array([0.42e-3, 0.52e-3]), np.array([400e3, 260e3]), np.array([100e3, 60e3]), np.array([1.4, 2.0])
-FIX, WAKE, ISSUE, SLACK, MOVES, EAGER = 0.06, 0.1, 1.0, 0.1, 5000, 1.0
-ROUNDS, MIX, EARLY, LATE, SHAKE = 16, 0.5, 16, 16, 1.5
-PARTS = [(0, 128), (128, P)]
+CYC, GATHER, SCATTER = np.array([0.83e-3, 1.1e-3]), np.array([1.3, 1.6]), np.array([2.5, 4.0])
+PECYC, HBM, LINK, FLY = np.array([0.42e-3, 0.55e-3]), np.array([300e3, 260e3]), np.array([100e3, 35e3]), np.array([1.0, 2.0])
+FIX, WAKE, WAKE1, ISSUE, EAGER = 0.01, 0.22, 0.36, 1.0, 0.3
+ROUNDS, SWEEPS, STRETCH, MOVES, MIX, SHAKE, HEAT = 150, 3, 100, 5000, 0.5, 3.0, 0.6
 _PLAN = {}
 
 
@@ -56,102 +70,159 @@ def order_calls(ops):
         for d, lag in pred[k]:
             succ[d].append((k, lag))
 
-    def plan(before, behind, rank):
-        end, free, bank, due = [0.0] * n, {}, {}, [0.0] * n
-        left = [len(x) for x in before]
-        pool = [k for k in range(n) if left[k] == 0]
-        order, extra = [], [set() for _ in range(n)]
-        while pool:
-            at = {k: max([due[k], free.get(ops[k]["q"], 0.0)]
-                         + [end[d] + WAKE for b in ops[k]["banks"] for q, d in bank.get(b, {}).items()
-                            if q != ops[k]["q"]]) for k in pool}
-            pick = first = min(pool, key=lambda j: (at[j], -rank[j], j))
-            for k in sorted((j for j in pool if ops[j]["q"] == ops[first]["q"]), key=lambda j: (at[j], j)):
-                if rank[k] > rank[pick] and at[pick] + ops[pick]["cost"] > at[k] + SLACK:
-                    pick = k
-            o = ops[pick]
-            end[pick] = free[o["q"]] = at[pick] + o["cost"]
+    def plan(before, rank, first):
+        end, busy = [0.0] * n, {}
+        for k in sorted(range(n), key=lambda j: -rank[j]):
+            o, t = ops[k], max([end[d] + lag for d, lag in before[k]], default=first[k])
+            rows = [(x, y) for x, y, q in busy.get(o["q"], []) if y > t]
             for b in o["banks"]:
-                extra[pick] |= {d for q, d in bank.get(b, {}).items() if q != o["q"]}
-                bank.setdefault(b, {})[o["q"]] = pick
-            order.append(pick)
-            pool.remove(pick)
-            for s, lag in behind[pick]:
-                due[s] = max(due[s], end[pick] + lag)
-                left[s] -= 1
-                if left[s] == 0:
-                    pool.append(s)
-        return max(end[k] + ops[k]["lat"] for k in range(n)), end, order, extra
+                rows += [(x - WAKE, y + WAKE) for x, y, q in busy.get(b, []) if q != o["q"] and y + WAKE > t]
+            for x, y in sorted(rows):
+                if x >= t + o["cost"]:
+                    break
+                t = max(t, y)
+            end[k] = t + o["cost"]
+            for r in [o["q"]] + sorted(o["banks"]):
+                busy.setdefault(r, []).append((t, end[k], o["q"]))
+        return end
 
-    rank = [0.0] * n
-    for k in range(n - 1, -1, -1):
+    rank, left = [0.0] * n, [len(x) for x in succ]
+    back = [k for k in range(n) if not left[k]]
+    for k in back:
         rank[k] = ops[k]["cost"] + max([lag + rank[s] for s, lag in succ[k]], default=ops[k]["lat"])
+        for d, lag in pred[k]:
+            left[d] -= 1
+            if not left[d]:
+                back.append(d)
     best, seed = None, 1
     for r in range(ROUNDS):
-        made = plan(pred, succ, rank)
-        if best is None or made[0] < best[0]:
-            best, kept = made, rank
-        if r % 4 == 3:
-            rank = []
-            for x in kept:
+        end = plan(pred, rank, [0.0] * n)
+        span = max(end[k] + ops[k]["lat"] for k in range(n))
+        if best is None or span < best[0]:
+            best, kept = (span, end, sorted(range(n), key=lambda j: (end[j] - ops[j]["cost"], end[j], j))), rank
+        if r % 3 == 2:
+            rank = [0.0] * n
+            for k in back:
                 seed = (seed * 1103515245 + 12345) % 2147483648
-                rank.append(x + SHAKE * seed / 2147483648)
+                shake = SHAKE * (seed / 2147483648 - 0.5) * ((seed >> 9) % 8 == 0)
+                rank[k] = max([kept[k] + shake] + [rank[s] + 1e-6 for s, lag in succ[k]])
         else:
-            back = plan(succ, pred, made[1])[1]
-            rank = [MIX * x + (1 - MIX) * y for x, y in zip(back, rank)]
-    sets = [([float(o["both"][0][s]) for o in ops],
-             [[(d, float(ops[d]["both"][1][s]) + WAKE if d in o["wait"] else 0.0) for d in o["after"]] for o in ops],
-             [float(o["both"][1][s]) for o in ops]) for s in range(2)]
-    queue, banks = [o["q"] for o in ops], [sorted(o["banks"]) for o in ops]
+            rank = plan(succ, end, [o["lat"] for o in ops])
+    cost = [[float(o["both"][0][s]) for o in ops] + [0.0] for s in range(2)]
+    lat = [[float(o["both"][1][s]) for o in ops] for s in range(2)]
+    wake = (WAKE, WAKE1)
+    before = [[(d, lat[0][d] + WAKE, lat[1][d] + WAKE1) if d in o["wait"] else (d, 0.0, 0.0) for d in o["after"]]
+              for o in ops]
+    queue, banks = [o["q"] for o in ops] + [None], [sorted(o["banks"]) for o in ops]
+    behind = [{s for s, lag in x} for x in succ]
+    c0, c1 = cost
 
-    def length(order):
-        total = 0.0
-        for cost, before, lat in sets:
-            end, free, bank, worst = [0.0] * n, {}, {}, 0.0
-            for k in order:
-                q = queue[k]
-                t = free.get(q, 0.0)
-                for d, lag in before[k]:
-                    if end[d] + lag > t:
-                        t = end[d] + lag
-                for b in banks[k]:
-                    x = bank.get(b)
-                    if x and x[0] != q and x[1] + WAKE > t:
-                        t = x[1] + WAKE
-                t += cost[k]
-                end[k] = free[q] = t
-                for b in banks[k]:
-                    bank[b] = (q, t)
-                if t + lat[k] > worst:
-                    worst = t + lat[k]
-            total += worst + EAGER * sum(end) / n
-        return total
+    def holders(part, last, bank):
+        held = {}
+        for k in part:
+            held[k] = [(last.get(queue[k], n), 0)] + [(bank[b], 1) for b in banks[k] if queue[bank.get(b, k)] != queue[k]]
+            last[queue[k]] = k
+            for b in banks[k]:
+                bank[b] = k
+        return held
+
+    def run(part, e0, e1, last, bank):
+        for k in part:
+            q = queue[k]
+            d = last.get(q, n)
+            t0, t1 = e0[d], e1[d]
+            for d, x, y in before[k]:
+                x += e0[d]
+                if x > t0:
+                    t0 = x
+                y += e1[d]
+                if y > t1:
+                    t1 = y
+            for b in banks[k]:
+                d = bank.get(b)
+                if d is not None and queue[d] != q:
+                    t0, t1 = max(t0, e0[d] + WAKE), max(t1, e1[d] + WAKE1)
+                bank[b] = k
+            e0[k], e1[k], last[q] = t0 + c0[k], t1 + c1[k], k
 
     order = best[2]
-    now = length(order)
-    ahead, behind = [o["after"] for o in ops], [{s for s, lag in x} for x in succ]
-    for _ in range(MOVES):
-        seed = (seed * 1103515245 + 12345) % 2147483648
-        i = (seed >> 8) % n
-        k, step = order[i], 1 if seed & 64 else -1
-        j, hops, stop = i, 1 + (seed >> 3) % 3, behind[k] if step > 0 else ahead[k]
-        to = i
-        while hops and 0 <= j + step < n and order[j + step] not in stop:
-            j += step
-            if queue[order[j]] == queue[k]:
-                hops, to = hops - 1, j
-        if to != i:
-            new = order[:i] + order[i + 1:]
-            new.insert(to, k)
-            t = length(new)
-            if t <= now:
-                order, now = new, t
+    for lo in [x for r in range(SWEEPS) for x in range(0, max(1, n - STRETCH // 2), STRETCH // 2)]:
+        part, rest = order[lo:lo + STRETCH], order[lo + STRETCH:]
+        base, last0, bank0 = ([0.0] * (n + 1), [0.0] * (n + 1)), {}, {}
+        run(order[:lo], base[0], base[1], last0, bank0)
+        held, tail = holders(rest, {}, {}), (lat[0] + [0.0], lat[1] + [0.0])
+        for k in reversed(rest):
+            for s in range(2):
+                for d in before[k]:
+                    tail[s][d[0]] = max(tail[s][d[0]], d[1 + s] + cost[s][k] + tail[s][k])
+                for d, w in held[k]:
+                    tail[s][d] = max(tail[s][d], w * wake[s] + cost[s][k] + tail[s][k])
+        nextq = {q: next((k for k in rest if queue[k] == q), n) for q in set(queue[:n])}
+        nextb = {b: next((k for k in rest if b in banks[k]), n) for x in banks for b in x}
+        tail[0][n] = tail[1][n] = 0.0
+        early = [max([base[s][k] + tail[s][k] for k in order[:lo]], default=0.0) for s in range(2)]
+
+        def length(part):
+            e, last, bank = (base[0][:], base[1][:]), dict(last0), dict(bank0)
+            run(part, e[0], e[1], last, bank)
+            total, ends = 0.0, []
+            for s in range(2):
+                top = [(e[s][k] + tail[s][k], k) for k in part]
+                top += [(e[s][k] + cost[s][nextq[q]] + tail[s][nextq[q]], k) for q, k in last.items()]
+                top += [(e[s][k] + wake[s] * (queue[k] != queue[nextb[b]]) + cost[s][nextb[b]] + tail[s][nextb[b]], k)
+                        for b, k in bank.items()]
+                ends.append(max(top))
+                total += (1, MIX)[s] * (max(ends[s][0], early[s]) + EAGER * sum(e[s][k] for k in part) / len(part))
+            return total, e, ends
+
+        now = length(part)
+        top, pairs = (now[0], part), None
+        for move in range(MOVES):
+            seed = (seed * 1103515245 + 12345) % 2147483648
+            if pairs is None:
+                s, place, pairs = (seed >> 20) & 1, {k: j for j, k in enumerate(part)}, []
+                held, end, k = holders(part, dict(last0), dict(bank0)), now[1][s], now[2][s][1]
+                while k in place:
+                    t = end[k] - cost[s][k] - 1e-9
+                    nxt = [x[0] for x in before[k] if end[x[0]] + x[1 + s] > t]
+                    if not nxt:
+                        nxt = [d for d, w in held[k] if end[d] + w * wake[s] > t]
+                        pairs += [(d, k) for d in nxt if d in place]
+                    k = nxt[0] if nxt else n
+            seed = (seed * 1103515245 + 12345) % 2147483648
+            pick, far, soon = seed >> 14, (seed >> 10) % 3, (seed >> 13) & 1
+            if (seed >> 8) & 3 and pairs:
+                u, v = pairs[pick % len(pairs)]
+            else:
+                v = part[pick % len(part)]
+                u = next((part[j] for j in range(place[v] - 1, -1, -1) if queue[part[j]] == queue[v]), v)
+            i, j = place[u], place[v]
+            for _ in range(far):
+                if soon:
+                    i = next((x for x in range(i - 1, -1, -1) if queue[part[x]] == queue[v]), i)
+                else:
+                    j = next((x for x in range(j + 1, len(part)) if queue[part[x]] == queue[u]), j)
+            span, took = part[i:j + 1], {v if soon else u}
+            for x in reversed(span) if soon else span:
+                if (behind[x] if soon else ops[x]["after"]) & took:
+                    took.add(x)
+            if part[i if soon else j] in took:
+                continue
+            new = part[:i] + [x for x in span if (x in took) == soon] + [x for x in span if (x in took) != soon] + part[j + 1:]
+            made = length(new)
+            if made[0] <= now[0] + HEAT * (1 - move / MOVES) * ((seed >> 4) % 64) / 64:
+                part, now, pairs = new, made, None
+                if now[0] < top[0]:
+                    top = (now[0], part)
+        order = order[:lo] + top[1] + rest
+    fin = ([0.0] * (n + 1), [0.0] * (n + 1))
+    run(order, fin[0], fin[1], {}, {})
+    _PLAN["time"], _PLAN["ends"] = [round(max(x), 1) for x in fin], fin[0]
     extra, seen = [set() for _ in range(n)], {}
     for k in order:
         for b in banks[k]:
             extra[k] |= {d for q, d in seen.get(b, {}).items() if q != queue[k]}
             seen.setdefault(b, {})[queue[k]] = k
-    _PLAN["time"] = now / 2
     return order, extra
 
 
@@ -160,7 +231,7 @@ def rank_program(g, core, T, topo):
     if rank is None:
         return
     Q = {"ve": g.vector, "ac": g.scalar, "pe": g.tensor, "po": g, "sy": g.sync}
-    ops, hist, soon = [], {}, {}
+    ops, hist = [], {}
 
     def c(name, a=0, b=None, st=1, p=None):
         b = SCRATCH[name][1][1] if b is None else b
@@ -184,13 +255,15 @@ def rank_program(g, core, T, topo):
                 same = ops[k2]["q"] == q and ops[k2]["sem"] is None and sem is None
                 if l2 < hi and lo < h2 and (w or w2) and not (st == s2 > 1 and (lo - l2) % st):
                     (order if same and ops[k2]["open"] else wait).add(k2)
-                elif q == "pe" and same and name.startswith("pb"):
+                elif q == "pe" and same and name.startswith("pb") and (opened or ops[k2]["open"]):
                     order.add(k2)
         for (name, lo, hi, st), w in acc:
+            if w and st == 1:
+                hist[name] = [x for x in hist.get(name, []) if not (lo <= x[0] and x[1] <= hi)]
             hist.setdefault(name, []).append((lo, hi, st, k, w))
         both = (cost + np.zeros(2), lat + np.zeros(2))
-        ops.append(dict(q=q, call=call, sem=sem, inc=inc, wait=wait, after=wait | order, both=both,
-                        cost=float(both[0].mean()), lat=float(both[1].mean()),
+        ops.append(dict(q=q, call=call, sem=sem, inc=inc, wait=wait - {k}, after=(wait | order) - {k}, both=both,
+                        cost=float(both[0][0]), lat=float(both[1][0]),
                         open=opened, banks={r[0] for r, w in acc if r[0].startswith("pb")}))
         return k
 
@@ -221,12 +294,20 @@ def rank_program(g, core, T, topo):
         rec("ve", lambda e: e.memset(o[0], v), [o], [], price(o, o, narrow(o)))
 
     def scan(o, x, y, init, op0, op1):
-        rec("ve", lambda e: e.tensor_tensor_scan(o[0], x[0], y[0], init, op0, op1), [o], [x, y],
-            price(o, x, narrow(o, x, y)))
+        return rec("ve", lambda e: e.tensor_tensor_scan(o[0], x[0], y[0], a(init), op0, op1), [o], [x, y, init],
+                   price(o, x, narrow(o, x, y)))
 
-    def act(o, x, f=F.Identity, bias=0.0, scale=1.0, after=()):
-        return rec("ac", lambda e: e.activation(o[0], x[0], f, bias=a(bias), scale=a(scale)), [o], [x, bias, scale],
-                   price(o, x, 1), after=after)
+    def act(o, x, f=F.Identity, bias=0.0, scale=1.0, after=(), total=None):
+        if total is None:
+            call = lambda e: e.activation(o[0], x[0], f, bias=a(bias), scale=a(scale))
+        else:
+            call = lambda e: e.activation(o[0], x[0], f, bias=a(bias), scale=a(scale), accum_out=total[0])
+        return rec("ac", call, [o] + [total] * (total is not None), [x, bias, scale], price(o, x, 1), after=after)
+
+    def move(who, o, x, scale=None):
+        if ENG[who] == "s":
+            return act(o, x, scale=1.0 if scale is None else scale)
+        return cp(o, x) if scale is None else ts(o, x, scale, A.mult)
 
     def group(o, terms, start=True, stop=True, after=()):
         parts = o if isinstance(o, list) else [(o, terms)]
@@ -269,89 +350,115 @@ def rank_program(g, core, T, topo):
     def exchange(t, dst, src, s):
         rid, pid = topo.addr(peers[t])[:2]
         k = rec("po", lambda e: e.remote_dma(dst[0], src[0], T.sem[s], T.sem["sent"], pid, rid, emask),
-                [], [src], ISSUE, "sent", len(common(core)), 0.0, sends[-1:])
+                [], [src], ISSUE * (1 if sends else 2.5), "sent", len(common(core)), 0.0, sends[-1:])
         sends.append(k)
         prev = [j for j, x in enumerate(ops) if x["q"] == "rx"]
         rec("rx", None, [dst], [], 512 * src[3] / LINK, s, len(common(peers[t])), FLY, [k] + prev[-1:])
 
     col = lambda j: c("CC", j, j + 1)
-    PCOL, ACOL, QCOL, GCOL, DUM, LT4, GE4, EQ3, S1, SM31, Q24, G16, DUM2, HALF = range(14)
+    (PCOL, ACOL, QCOL, LANE, GCOL, DUM, LT4, GE4, EQ4, S1, SM15, S15, Q24, G16, DUM2, HALF, LT8, EW, R35, E44,
+     PAT, NG, EQ5, PW, SGN, THR) = range(26)
     I1, I2k, In2k, Ih = c("I1"), c("I2k"), c("In2k"), c("Ih")
     xm = lambda o, n: c("XM", 16 + o, 16 + o + n)
     m143 = lambda s: c(s, 0, 143)
 
-    load("ac", c("cnts", p=(0, 8)), T.cnt[:], "cnt", 0)
-    load("ac", c("stks"), T.stk[:], "stk", 1e5)
-    load("sy", c("labs", 0, 1024), T.lab[:, 0:1024], "lab0", 5e5)
-    load("sy", c("labs", 1024, V), T.lab[:, 1024:V], "lab1", 5e5)
-    load("sy", c("nbs"), T.nb[:], "nb", 1e6)
-    load("sy", c("W"), T.ln[:], "ln", 5e5)
+    load("sy", c("cnts", p=(0, 8)), T.cnt[:], "cnt", 0)
+    load("sy", c("stks"), T.stk[:], "stk", 1e5)
+    big = {"nb": (c("nbs", 0, V), T.nb[:], 1e6), "ln": (c("W", 0, V), T.ln[:], 5e5)}
+    for j in range(0, V, 512):
+        big["lab%d" % (j // 512)] = (c("labs", j, j + 512), T.lab[:, j:j + 512], 2.6e5)
+    for s in LOADS:
+        load("sy", big[s][0], big[s][1], s, big[s][2])
     iota(c("PI", 0, 1), [[0, 1]], 0, 1)
     iota(col(PCOL), [[0, 1]], 0, 1)
     iota(col(G16), [[0, 1]], 0, 16)
     iota(c("GM"), [[16, 8], [0, 16]], 0, 0)
     iota(c("XM"), [[1, 256]], -16, 0)
-    iota(c("C1"), [[-16, 16]], P, 0)
-    most = max(l1 - l0 for l0, l1 in CH)
-    fill(c("A0", 0, 16 * most), 0.0)
-    fill(c("A0", 0, 16 * most, 16), BIG)
+    iota(c("C1"), [[16, 16]], P, 0)
+    iota(c("E0"), [[1, 64], [0, 16]], 0, 0)
+    fill(c("A0"), 0.0)
+    fill(c("A0", 0, 1024, 16), -BIG)
     ts(c("PI", 1, 2), c("PI", 0, 1), 15, A.bitwise_and)
     ts(c("PI", 2, 3), c("PI", 0, 1), 2, A.arith_shift_right, 3, A.bitwise_and)
-    cp(c("CC", ACOL, ACOL + 2), c("PI", 1, 3))
+    ts(c("PI", 3, 4), c("PI", 0, 1), 63, A.bitwise_and)
+    cp(c("CC", ACOL, ACOL + 3), c("PI", 1, 4))
     tt(col(GCOL), col(PCOL), col(ACOL), A.subtract)
-    for j, s in ((SM31, -31.0), (S1, 1.0), (DUM, float(V)), (DUM2, V + 16.0)):
+    for j, s in ((SM15, -15.0), (S1, 1.0), (DUM, float(V)), (DUM2, V + 16.0), (HALF, 0.5)):
         act(col(j), col(ACOL), bias=s)
+    act(col(S15), col(ACOL), bias=15.0, scale=-1.0)
     act(col(Q24), col(QCOL), bias=4.0)
     ts(col(LT4), col(ACOL), 4.0, A.is_lt)
     ts(col(GE4), col(ACOL), 4.0, A.is_ge)
-    ts(col(EQ3), col(ACOL), 3.0, A.is_equal)
+    ts(col(EQ4), col(ACOL), 4.0, A.is_equal)
+    ts(col(LT8), col(ACOL), 8.0, A.is_lt)
+    ts(col(EQ5), col(ACOL), 5.0, A.is_equal)
+    act(col(PAT), col(EQ5), scale=float(DEAD))
+    act(col(EW), col(LT8), bias=-32.0, scale=32.125)
+    act(col(PW), col(LT8), bias=64.0, scale=-63.875)
+    act(col(SGN), col(LT8), bias=-1.0, scale=2.0)
+    act(col(THR), col(LT8), bias=-4.0, scale=9.0)
+    act(col(E44), col(ACOL), F.Abs, -4.0)
+    ts(col(R35), col(E44), 1.0, A.is_equal)
     ts(c("REP", p=(0, 8)), c("GM", p=(0, 8)), c("CC", G16, G16 + 1, p=(0, 8)), A.is_equal)
     ts(m143("Mh"), xm(-15, 143), col(GCOL), A.is_equal)
-    ts(m143("M3h"), m143("Mh"), col(EQ3), A.mult)
+    ts(m143("M35"), m143("Mh"), col(R35), A.mult)
     cp(m143("M1"), m143("Mh"))
-    act(m143("M16"), m143("M1"), scale=0.0625)
-    act(m143("MK4"), m143("M1"), scale=4096.0)
-    act(m143("Q15"), m143("M1"), scale=-1.0)
+    for nm, s in (("MP", col(PW)), ("MK4", 4096.0), ("Q15", -1.0), ("Qh", -1.0), ("MD", DEAD / 16.0), ("ME", col(EW))):
+        act(m143(nm), m143("M1"), scale=s)
     ts(c("IW", 0, 140), xm(-12, 140), col(PCOL), A.is_equal)
     I32 = c("IW", 12, 140)
     cp(Ih, I32)
     act(c("IW4", 0, 140), c("IW", 0, 140), scale=col(LT4))
-    for nm, s in (("I1", 1.0), ("In1", -1.0), ("I2k", 2048.0), ("In2k", -2048.0), ("I4", 4.0), ("In4", -4.0)):
-        act(c(nm), I32, scale=s)
-    act(c("B4", 0, 128), I32, scale=-32.0)
-    cp(c("ZO"), xm(0, 96))
+    act(col(NG), col(GCOL), bias=-1.5, scale=-1.0)
+    act(c("DV", 0, 140), xm(-12, 140), F.Abs, col(NG))
+    ts(c("DV", 0, 140), c("DV", 0, 140), 2.0, A.is_lt, col(EQ5), A.mult)
+    tt(c("IW4", 0, 140), c("IW4", 0, 140), c("DV", 0, 140), A.add)
+    for nm, s in (("I1", 1.0), ("In1", -1.0), ("I2k", 2048.0), ("In2k", -2048.0), ("In4", -4.0), ("Id", -1 / 32),
+                  ("Inh", -1.0), ("IL4", col(LT4)), ("B4", -32.0)) + (("Inf", -1.0),) * bool(ONS):
+        act(c(nm, 0, 128), I32, scale=s)
+    act(c("IhG"), I32, scale=col(GE4))
+    act(c("I2G"), c("IhG"), scale=2048.0)
+    act(c("In2G"), c("IhG"), scale=-2048.0)
+    ts(c("E"), c("E0"), col(LANE), A.is_equal)
     ts(c("ONES"), c("GM"), col(GCOL), A.is_equal)
-    ts(c("NB"), xm(0, 16), col(ACOL), A.is_equal, -1.0, A.mult)
-    for b in range(16):
-        ts(c("NS", 128 * b, 128 * b + 128), c("ONES"), c("NB", b, b + 1), A.mult)
-    act(col(HALF), col(ACOL), bias=0.5)
+    ts(c("SE4"), c("ONES"), col(EQ4), A.mult, 4.0, A.mult)
+    iota(c("Wg", 0, V), [[1, 16], [16, 8], [0, 16]], 0, 0)
+    ts(c("NS"), c("Wg", 0, V), col(PCOL), A.is_equal, -1.0, A.mult)
     for nm, n in (("TZ", 7), ("TJ", 12)):
         iota(c(nm), [[1, 16], [0, 3 * n]], 0, 0)
         rec("po", lambda e, x=c(nm), n=n: e.affine_select(x[0], x[0], [[0, 16], [1, 3], [0, n]], A.not_equal, 100.0, -1, 0),
             [c(nm)], [c(nm)], 0.17 + 2 * CYC * 48 * n)
-        act(c(nm), c(nm), F.Sign, col(HALF), -1.0)
-        act(c(nm), c(nm), F.Relu, scale=0.5)
-    ts(c("Zt", 0, 128), xm(0, 128), col(PCOL), A.is_ge)
-    tt(c("Zt", 0, 128), c("Zt", 0, 128), c("ONES"), A.mult)
-    tt(c("TR1"), c("Zt", 0, 128), c("B4", 0, 128), A.add)
+        act(c(nm), c(nm), F.Relu, col(HALF), -1.0)
+    ts(c("B4f", 0, 128), xm(0, 128), col(PCOL), A.is_ge)
+    tt(c("B4f", 0, 128), c("B4f", 0, 128), c("ONES"), A.mult)
+    tt(c("TR1"), c("B4f", 0, 128), c("B4", 0, 128), A.add)
     act(c("TR2"), c("TR1"), scale=2048.0)
     ts(m143("PQ"), xm(-16, 143), col(GCOL), A.is_equal)
     tt(m143("PQ"), m143("PQ"), m143("Q15"), A.add)
     fill(c("ONE"), 1.0)
-    ts(c("C1"), c("C1"), col(ACOL), A.subtract)
-    ts(c("QS"), xm(0, 4), col(QCOL), A.is_equal)
-    ts(c("Bc", 0, 128), xm(4, 128), col(PCOL), A.is_equal, col(GE4), A.mult)
-    tt(c("SHI"), c("Bc", 0, 128), I32, A.subtract)
+    act(c("RS"), c("ONE"), scale=col(LT8))
+    act(c("C1"), c("C1"), bias=col(ACOL))
+    act(c("SPL"), c("ONES"), scale=col(PW))
+    ts(c("DV", 0, 128), xm(4, 128), col(PCOL), A.is_equal, col(GE4), A.mult)
+    tt(c("SHI"), c("DV", 0, 128), I32, A.subtract)
     act(c("JC", 0, 12), xm(0, 12), bias=col(QCOL), scale=8.0)
     act(c("JC", 12, 24), xm(0, 12), bias=col(Q24), scale=8.0)
-    for qq in range(4):
-        ts(c("INV", 128 * qq, 128 * qq + 128), xm(4 * qq, 128), col(PCOL), A.is_equal, c("QS", qq, qq + 1), A.mult)
-    fill(c("RB", 96, 104), 0.0)
-    fill(c("X", V, V + 32), 0.0)
+    fill(c("X", V, WIDE), 0.0)
+    fill(c("W", V, WIDE), 1.0)
+    fill(c("nbs", V, WIDE), DEAD)
+    fill(c("Hh"), 0.0)
+    for nm in ("Mb", "Wp"):
+        iota(c(nm), [[0, PAD]], 0, 0)
+    for t in range(STEPS):
+        act(c("ms%d" % t, 0, 104), xm(0, 104), bias=col(PAT), scale=0.0)
+        iota(c("ms%d" % t, 104, 456), [[0, 352]], 0, 0)
+        act(c("mr%d" % t, 104, 240), xm(0, 136), bias=col(PAT), scale=0.0)
+        fill(c("mr%d" % t, 240, 248), 0.0)
 
     XW, v14 = c("X"), c("v16", 0, 14)
-    PA, PB, PC = c("pb0", 0, P), c("pb1", 0, P), c("pb2", 0, P)
-    PV, PS, PN = c("pb5", 0, 14), c("pb6", 0, P), c("pb7", 0, P)
+    PA, PB, PS, PN = c("pb6", 256, 256 + P), c("pb6", 0, P), c("pb7", 0, P), c("pb5", 256, 256 + P)
+    PV, PU, PC, PY = c("pb4", 320, 334), c("pb3", 0, 24), c("pb0", 0, P), c("pb0", 256, 256 + P)
+    slot = lambda nm, k, a0, b0: c(nm, 128 * k + 64 + a0, 128 * k + 64 + b0)
 
     def distinct(src, n, banks, tri, eq, y, off, more=None):
         per, w = 16 // len(banks), 3 * n
@@ -366,181 +473,183 @@ def rank_program(g, core, T, topo):
             bs = range(per * j, per * (j + 1))
             group(c(y[0], y[1], y[1] + 2 * n), [(Ih, c(src, n, 3 * n))] * (j == 0)
                   + [(mk(b), c(eq, w * b, w * b + 2 * n)) for b in bs] + (more if j else []), j == 0, False)
-            k = group(c(y[0], y[1] + n, y[1] + 2 * n), [(mk(b), c(eq, w * b + 2 * n, w * b + w)) for b in bs],
-                      False, j == len(banks) - 1)
+            group(c(y[0], y[1] + n, y[1] + 2 * n), [(mk(b), c(eq, w * b + 2 * n, w * b + w)) for b in bs],
+                  False, j == len(banks) - 1)
         ts(c(off, 0, 2 * n, 2), c(y[0], y[1], y[1] + n), col(DUM), A.min)
         ts(c(off, 1, 2 * n, 2), c(y[0], y[1] + n, y[1] + 2 * n), col(DUM2), A.min)
-        return k
-
-    def push(s, stop=False, after=(), pt=(0, P), late=()):
-        qs = c("q", P * s + pt[0], P * s + pt[1])
-        act(qs, c("pb1", *pt), F.Relu, 2048.0 * (s + 1) - 63488.0, -1.0, late)
-        group(c("pb6", *pt), [(c("Q15" if s == 15 else "PQ", 15 - s, 143 - s), qs)], False, stop, after)
 
     def popped():
-        cp(v14, PV)
-        cp(c("V0", 0, 14), PV)
+        move("v16", v14, PV)
         cp(c("K"), ind(c("nbs"), v14))
-        cp(c("Kf"), c("K"))
-        act(c("n1"), PN, F.Relu, 31.0)
-        act(c("dead"), PN, F.Relu, -256.0 * 31, -256.0)
+        move("Kf", c("Kf"), c("K"))
+        prev = []
+        for j in range(7):
+            prev = [act(c("Wg", 512 * j, 512 * j + 512), ind(c("W"), c("K", 32 * j, 32 * j + 32)), after=prev)]
+        move("Wv", c("Wv"), ind(c("W"), v14), -1 / 32)
+        for k, (l0, l1) in enumerate(CH):
+            move("Wp", slot("Wp", k, 0, l1 - l0), c("Wv", l0, l1))
+        act(c("n1"), PN, F.Relu, 15.0)
         act(c("r1"), c("n1"), F.Relu, col(S1), -1.0)
         act(c("pm"), c("r1"), F.Relu, 1.0, -1.0)
-        group(c("pb7", 256, 270), wrap("M1", "dead", 0, P))
         for j in range(4):
-            tt(c("Vh", 7 * j, 7 * j + 7), c("pb7", 256 + j // 2, 270, 2), c("V0", j // 2, 14, 2), A.add)
-        distinct("Vh", 7, ["pb5"], "TZ", "eqz", ("pb5", 352), "zoff")
-        k = len(ops)
-        soon["test"], soon["offsets"] = [k - 5], [k - 2, k - 1]
-        return [k - 6]
+            move("Vh", c("Vh", 7 * j, 7 * j + 7), c("pb4", 320 + j // 2, 334, 2))
+        distinct("Vh", 7, ["pb4"], "TZ", "eqz", ("pb4", 352), "zoff")
 
-    def lengths():
-        for k in range(4):
-            group(c("pb%d" % k), [(c("In1"), c("W", 512 * k, 512 * k + 512))], True, k >= DPE)
-
-    ts(c("cntb", p=(0, 8)), c("cnts", p=(0, 8)), 32.0, A.subtract)
+    ts(c("cntb", p=(0, 8)), c("cnts", p=(0, 8)), 16.0, A.subtract)
     group(PN, [(c("REP", p=(0, 8)), c("cntb", p=(0, 8)))])
-    ts(c("m2"), PN, col(SM31), A.is_equal)
+    ts(c("m2"), PN, col(SM15), A.is_equal)
+    act(c("em"), PN, F.Relu, -15.0, -1.0)
     tt(c("T2"), c("m2"), c("stks"), A.mult)
-    group(PV, wrap("Mh", "T2", 0, P))
-    cp(c("X", 0, 1024), c("labs", 0, 1024))
-    cp(c("X", 1024, V), c("labs", 1024, V))
+    group(PV, wrap("MD", "em", 0, P), True, False)
+    group(PV, wrap("Mh", "T2", 0, P), False, True)
+    for j in range(4):
+        ts(c("X", 512 * j, 512 * j + 512), c("labs", 512 * j, 512 * j + 512), -1 / 32, A.mult)
     popped()
-    lengths()
     tt(c("Sold"), c("pm"), c("stks"), A.mult)
 
     for t in range(STEPS):
         last = t == STEPS - 1
-        ls, lr, cs, cr, js, jr = (x + str(t) for x in ("ls", "lr", "cs", "cr", "js", "jr"))
-        wide = [(16 * l0, 16 * l1) for l0, l1 in CH]
-        gather = {"x": lambda k, af: act(c("G", *wide[k]), ind(XW, c("K", *CH[k])), after=af),
-                  "d": lambda k, af: act(c("Dg", *wide[k]), ind(c("D"), c("K", *CH[k])), after=af)}
-        prev = [gather["x"](0, [])]
-        if ZPE:
-            act(c("mt"), ind(c("W"), v14))
-            prev = [act(c("Zt"), ind(XW, v14), after=prev)]
-        for k in range(4):
-            piece = (512 * k, 512 * k + 512)
-            if k < DPE:
-                group(c("pb%d" % k), [(I32, c("X", *piece))], False, True)
-                prev = [act(c("D", *piece), c("pb%d" % k), after=prev)]
-            else:
-                tt(c("D", *piece), c("X", *piece), c("pb%d" % k), A.add)
-        for kind, k in [(x[0], int(x[1])) for x in GORDER[t > 0].split()]:
-            if kind == "x" and k in GV:
-                cp(c("G", *wide[k]), ind(XW, c("K", *CH[k])))
-            else:
-                prev = [gather[kind](k, prev)]
-        for k, (l0, l1) in enumerate(CH):
-            vk = c("v16", l0 // 16, l1 // 16)
-            scan(c("SO", *wide[k]), c("A0", 0, 16 * (l1 - l0)), c("G", *wide[k]), 0.0, A.add, A.min)
-            if ZPE:
-                group(c("pb2", l0, l1), [(I1, c("mt", l0, l1)), (I32, c("SO", 16 * l0 + 15, 16 * l1, 16))])
-                tt(c("Z", l0, l1), c("Zt", l0, l1), c("pb2", l0, l1), A.min)
-            else:
-                tt(c("Zt", l0, l1), ind(c("W"), vk), c("SO", 16 * l0 + 15, 16 * l1, 16), A.add)
-                tt(c("Z", l0, l1), ind(XW, vk), c("Zt", l0, l1), A.min)
-            tt(c("Ind", *wide[k]), ind(c("Z", l0, l1), c("ZO", 0, l1 - l0)), c("Dg", *wide[k]), A.is_lt)
-            if k < 2:
-                ops[-1]["after"] |= set(soon["test" if k == 0 else "offsets"])
-            if t > 0 and k == HINT[0]:
-                ops[-1]["after"] |= set(soon["stack"])
-            if k == HINT[1]:
-                ops[-1]["after"] |= set(soon["hit"])
-            j, pt = [(j, pt) for j, pt in enumerate(PARTS) if pt[0] <= l0 < pt[1]][0]
-            hb = "pb4" if j % 2 == 0 else "pb3"
-            group(c(hb, l0, l1), [(c("M1", 15 - i, 143 - i), c("Ind", 16 * l0 + i, 16 * l1, 16)) for i in range(16)])
-            if l1 == pt[1]:
-                soon["hit"] = [tt(c("hit", *pt), c(hb, *pt), c("dead", *pt), A.is_gt)]
+        ls, lr, ms, mr = (x + str(t) for x in ("ls", "lr", "ms", "mr"))
+        tag = {"d": tt(c("DV"), ind(XW, v14), c("Wv"), A.subtract)}
         for j in range(7):
-            cp(ind(XW, c("zoff", 2 * j, 2 * j + 2)), c("Z", 32 * j, 32 * j + 32))
+            gather = cp if j in GV else act
+            tag["g%d" % j] = gather(c("G", 512 * j, 512 * j + 512), ind(XW, c("K", 32 * j, 32 * j + 32)))
+        for k, (l0, l1) in enumerate(CH):
+            n = l1 - l0
+            M, PT = slot("Mb", k, 0, n), c(*TURN[k])
+            tag["s%d" % k] = scan(c("SO", 16 * l0, 16 * l1), c("A0", 0, 16 * n), c("G", 16 * l0, 16 * l1), 0.0, A.add, A.max)
+            tag["m%d" % k] = tt(M, c("SO", 16 * l0 + 15, 16 * l1, 16), c("DV", l0, l1), A.max)
+            tag["n%d" % k] = tt(slot("Hh", k, 0, n), c("SO", 16 * l0 + 15, 16 * l1, 16), c("DV", l0, l1), A.max)
+            tag["T%d" % k] = group(PT, [(slot("Wp", k, -64, 64), I1), (slot("Mb", k, -64, 64), I32),
+                                        (slot("Hh", k, 0, 128), Ih), (slot("Hh", k, -64, 64), c("Inh"))])
+            HT = c("HT", 128 * k, 128 * k + 128)
+            tag["H%d" % k] = (cp if k in HV else act)(HT, PT)
+            for j in range(l0 // 32, l1 // 32):
+                bank, piece = c("pb%d" % BANKS[j]), (512 * j, 512 * j + 512)
+                tag["w%d" % j] = group(bank, [(c("Id"), c("Wg", *piece))], True, False)
+                if j in ONS:
+                    tag["x%d" % j] = group(bank, [(c("Inf"), c("G", *piece))], False, False)
+                tag["e%d" % j] = group(bank, [(HT, c("E", 512 * j - 16 * l0, 512 * j + 512 - 16 * l0))], False, True)
+                if j in ONS:
+                    tag["t%d" % j] = act(c("Ind", *piece), bank, F.Relu)
+                else:
+                    tag["t%d" % j] = tt(c("Ind", *piece), c("G", *piece), bank, A.is_lt)
+                at = 32 * j - l0
+                tag["z%d" % j] = tt(ind(XW, c("zoff", 2 * j, 2 * j + 2)), slot("Mb", k, at, at + 32),
+                                    c("Wv", 32 * j, 32 * j + 32), A.add)
+            if l1 in HITS:
+                h0 = ([0] + HITS)[HITS.index(l1)]
+                tag["h%d" % HITS.index(l1)] = group(c(SUMS, h0, l1), [
+                    (c("M1", 15 - i, 143 - i), c("Ind", 16 * h0 + i, 16 * l1, 16)) for i in range(16)])
+        for line in PULL:
+            for x, y in zip(line.split(), line.split()[1:]):
+                ops[tag[y]]["after"].add(tag[x])
         for pt in PARTS:
-            group(c("pb0", *pt), [(I1, c("n1", *pt))], True, False)
-            group(c("pb0", *pt), [(c("ONES"), c("hit", *pt))], False, True)
-            group(c("pb1", *pt), [(I2k, c("n1", *pt)), (Ih, c("Kf", *pt))], True, False)
-            group(c("pb1", *pt), [(c("TR2"), c("hit", *pt))], False, True)
-            group(c("pb6", *pt), [(Ih, c("Sold", *pt)), (I2k, c("r1", *pt))], True, False)
-            for s in range(4):
-                push(s, pt=pt)
-            act(c("r2", *pt), c("pb0", *pt), F.Relu, col(S1), -1.0)
-            group(c("pb6", *pt), [(In2k, c("r2", *pt))], False, True)
-            act(c("B4", *pt), c("pb6", *pt))
-        ts(c("RG", P, 2 * P), PA, 5.0, A.is_lt)
-        ts(c("nnm"), PA, 16.0, A.min, 32.0, A.subtract)
-        scan(c("RG", 0, P), c("ONE"), c("RG", P, 2 * P), -1.0, A.add, A.subtract)
-        ts(c("RG", 3 * P, 4 * P), c("nnm"), -32.0, A.is_gt)
-        scan(c("RG", 2 * P, 3 * P), c("ONE"), c("RG", 3 * P, 4 * P), -1.0, A.add, A.subtract)
-        group(c("pb5", 0, 28), wrap("M16", "RG", 0, 2 * P))
-        tt(c("tw", 0, 14), c("pb5", 14, 28), c("C1", 0, 14), A.mult)
-        tt(c("tw", 16, 30), c("pb5", 0, 14), c("tw", 0, 14), A.add)
-        cp(c("pos", 0, 14), c("tw", 16, 30))
-        act(c(cs, 0, 2), c("RG", P - 1, 3 * P, 2 * P), bias=0.5)
-        exchange(t, c(cr), c(cs), "r%dc" % t)
-        ts(c("cio", 0, 1), c(cr, 0, 1), c(cs, 1, 2), A.min, 95.5, A.min)
-        ts(c("cio", 1, 2), c(cr, 1, 2), c(cs, 0, 1), A.min, 95.5, A.min)
-        ts(c("inval"), c("JC"), c("cio", 1, 2), A.is_gt, 4096.0, A.mult)
-        cp(ind(c("Bc"), c("pos", 0, 14)), c("B4"))
-        PU = c("pb4", 256, 280)
-        pu = [group(PU, [(c("IW4", 12 - 4 * qq, 140 - 4 * qq), c("Bc", qq, 96, 4)) for qq in range(4)])]
-        cp(c("U16"), PU)
-        cp(c(ls, 0, 24), PU)
-        for hh in range(2):
-            half = (24 + 192 * hh, 216 + 192 * hh)
-            act(c(ls, *half), ind(XW, c("U16", 12 * hh, 12 * hh + 12)))
-            sent = (half[0] * hh, half[1])
-            exchange(t, c(lr, *sent), c(ls, *sent), "r%d%s" % (t, "ab"[hh]))
+            if ENG["hit"] == "s":
+                act(c("hit", *pt), c(SUMS, *pt), F.Sign)
+            else:
+                ts(c("hit", *pt), c(SUMS, *pt), 0.0, A.is_gt)
+            group(c("pb6", *pt), [(I2k, c("n1", *pt)), (Ih, c("Kf", *pt)), (c("TR2"), c("hit", *pt))])
+            high = c("pb6", 256 + pt[0], 256 + pt[1])
+            for x in (c("pb5", *pt), high):
+                group(x, [(I1, c("n1", *pt)), (c("ONES"), c("hit", *pt))])
+            low = c("pb%d" % LOW[PARTS.index(pt)], *pt)
+            group(low, [(Ih, c("Sold", *pt)), (I2k, c("r1", *pt))], True, False)
+            act(c("r2", *pt), high, F.Relu, col(S1), -1.0)
+            group(low, [(In2k, c("r2", *pt))], False, False)
+            n, at = pt[1] - pt[0], 4 * pt[0]
+            if PARTS.index(pt) in NARROW:
+                for s in range(4):
+                    act(c("qu", at + n * s, at + n * s + n), c("pb6", *pt), F.Relu, 2048.0 * (s + 1) - 63488.0, -1.0)
+                ts(c("qh", at, at + 4 * n), c("qu", at, at + 4 * n), 2048.0, A.min)
+                group(low, [(c("Qh", 15 - s, 143 - s), c("qh", at + n * s, at + n * s + n)) for s in range(4)], False, True)
+            else:
+                for s in range(4):
+                    qs = c("q", at + n * s, at + n * s + n)
+                    act(qs, c("pb6", *pt), F.Relu, 2048.0 * (s + 1) - 63488.0, -1.0)
+                    group(low, [(c("PQ", 15 - s, 143 - s), qs)], False, s == 3)
+            act(c("B4", *pt), low, bias=col(EQ4), scale=col(LT4))
+            flag = c("RG", P + pt[0], P + pt[1])
+            ts(flag, c("pb5", *pt), col(SGN), A.mult, col(THR), A.is_ge)
+            scan(c("RG", *pt), c("RS", *pt), flag, c("RG", pt[0] - 1, pt[0]) if pt[0] else -1.0, A.mult, A.add)
+        move("B4h", c("B4h"), c("B4"), col(LT4))
+        group(c("pb4", 256, 270), wrap("MP", "RG", 0, P))
+        tt(c("pos", 0, 14), c("pb4", 256, 270), c("C1", 0, 14), A.min)
+        act(c("em"), PA, F.Relu, 1.0, -1.0, total=c(ms, 4, 5))
+        if EARLY:
+            exchange(t, c(mr, 4, 6), c(ms, 4, 6), "r%dc" % t)
+        cp(ind(c(ms, 8, 456), c("pos", 0, 14)), c("B4"))
+        exchange(t, c(mr, 8 if EARLY else 4, 104), c(ms, 8 if EARLY else 4, 104), "r%dn" % t)
+        wrapped = lambda x: [(c("IW4", 12 - 4 * qq, 140 - 4 * qq), c(x, 8 + qq, 104, 4)) for qq in range(4)]
+        group(PU, wrapped(ms))
+        move("U16", c("U16"), PU)
+        halves = list(zip([0] + SPLIT, SPLIT + [384]))
+        for j, (h0, h1) in enumerate(halves):
+            act(c(ls, h0, h1), ind(XW, c("U16", h0 // 16, h1 // 16)))
+            exchange(t, c(lr, h0, h1), c(ls, h0, h1), "r%d%s" % (t, "abj"[j]))
+        ts(c("inval"), c("JC"), c(ms, 4, 5), A.is_ge, 4096.0, A.mult)
+        group(c("pb3", 24, 48), wrapped(mr))
         for j in range(4):
-            cp(c("Uh", 12 * j, 12 * j + 12), c("pb4", 256 + j // 2, 280, 2))
-        pu.append(distinct("Uh", 12, ["pb7", "pb3"], "TJ", "eqj", ("pb4", 128), js, [(I1, c("inval"))]))
-        exchange(t, c(jr), c(js), "r%dj" % t)
-        PE_ = c("pb0", 288, 302)
-        group(PE_, wrap("M16", "RG", 2 * P, 3 * P), True, False)
-        group(PE_, wrap("MK4", "RG", 3 * P, 4 * P), False, True)
-        ts(c("epos", 0, 14), PE_, 96.0, A.min)
+            move("Uh", c("Uh", 12 * j, 12 * j + 12), c("pb3", 24 + j // 2, 48, 2))
+        move("Uq", c("Uq"), c("pb3", 24, 48))
+        distinct("Uh", 12, ["pb1", "pb2"], "TJ", "eqj", ("pb3", 128), "joff", [(I1, c("inval"))])
+        ts(c("cio", 0, 1), c(mr, 4, 5), 96.0, A.min)
+        act(c("nq"), PA, F.Relu, 16.0, -1.0)
+        scan(c("er"), c("RS"), c("em"), 0.0, A.mult, A.add)
+        PE_ = c("pb4", 288, 302)
+        group(PE_, wrap("ME", "er", 0, P))
+        ts(c("epos", 0, 14), PE_, 255.0, A.add, 232.0, A.min)
         if not last:
-            group(PC, [(I1, c("n1")), (c("TR1"), c("hit")), (c("In1"), c("nnm"))])
-            act(c("ab1"), PC, F.Abs)
-            act(c("mt"), c("ab1"), F.Relu, 1.0, -1.0)
-            ts(c("m2"), c("nnm"), col(SM31), A.is_equal)
+            group(PC, [(I1, c("n1")), (c("TR1"), c("hit")), (I1, c("nq"))])
+            ts(c("mt"), PC, -16.0, A.is_equal)
+            ts(c("m2"), c("nq"), col(S15), A.is_equal)
             tt(c("T1"), c("mt"), c("Kf"), A.mult)
             tt(c("T2"), c("m2"), c("Sold"), A.mult)
             group(PV, wrap("Mh", "T1", 0, P), True, False)
             group(PV, wrap("Mh", "T2", 0, P), False, False)
-        cp(c("Uf"), c(lr, 0, 24))
-        cp(c("Uq"), c(lr, 0, 24))
-        group([(c("pb4", 24 * qq, 24 * qq + 24), [(c("INV", 128 * qq, 128 * qq + 128), c("Uf"))]) for qq in range(4)],
-              None)
-        act(c("MK"), xm(0, 112), F.Sign, c("cio", 0, 1), -1.0)
-        for qq in range(4):
-            tt(c("RB", qq, 96, 4), c("pb4", 24 * qq, 24 * qq + 24), c("MK", qq, 96, 4), A.mult)
-        act(c("GW"), xm(0, P), F.Sign, c("cio", 1, 2), -1.0)
-        ts(c("Rg"), ind(c("RB"), c("epos", 0, 14)), 0.0, A.max)
-        late = [act(c("recv"), ind(c("MK"), c("epos", 0, 14)), F.Relu),
-                act(c("giv"), ind(c("GW"), c("pos", 0, 14)), F.Relu)]
-        pn = group(PN, [(I1, c("nnm")), (c("I4"), c("recv")), (c("In4"), c("giv"))])
+        group(PY, [(c("SPL"), c("RG", 0, P))])
+        if ONV:
+            ts(c("nv"), PB, -1.0, A.mult, -30720.0, A.add)
+        group(PS, [(Ih, c("B4h")), (c("IhG"), c("Sold")), (c("I2G"), c("r1")), (c("In2G"), c("r2"))], True, False)
+        for s0 in range(4, 16, BATCH):
+            for s in range(s0, s0 + BATCH):
+                if s in ONV:
+                    ts(c("qu", P * s, P * s + P), c("nv"), 2048.0 * (15 - s), A.subtract, 0.0, A.max)
+                else:
+                    act(c("qu", P * s, P * s + P), PB, F.Relu, 2048.0 * (s + 1) - 63488.0, -1.0)
+            ts(c("qh", P * s0, P * (s0 + BATCH)), c("qu", P * s0, P * (s0 + BATCH)), 2048.0, A.min)
+            group(PS, [(c("Qh", 15 - s, 143 - s), c("qh", P * s, P * s + P)) for s in range(s0, s0 + BATCH)],
+                  False, s0 + BATCH == 16)
+        move("Rg", c("Rg"), ind(c(mr, 8, 248), c("epos", 0, 14)))
+        ts(c("giv"), PY, c("cio", 0, 1), A.is_lt)
+        group(PN, [(c("In1"), c("nq")), (c("SE4"), c("Rg")), (c("In4"), c("giv"))])
         if not last:
-            pu += [pn, group(PV, wrap("M3h", "Rg", 0, P), False, True)]
-            pu += popped()
-        group(PS, [(I32, c("B4"))], True, False, pu[:1])
-        for s in range(4, 16):
-            push(s, s == 15, pu if s >= EARLY else pu[:2], late=late if s >= LATE else ())
+            group(PV, wrap("M35", "Rg", 0, P), False, True)
+            popped()
         tt(c("Bg"), PS, c("giv"), A.mult)
-        cp(c("T1"), PS)
-        group(PS, [(Ih, c("T1")), (c("SHI"), c("Bg")), (Ih, c("Rg"))])
-        for hh in range(2):
-            half = (192 * hh, 192 * hh + 192)
-            tt(c("jm", *half), ind(XW, c("Uq", 12 * hh, 12 * hh + 12)), c(lr, half[0] + 24, half[1] + 24), A.min)
-        for j in range(12):
-            cp(ind(XW, c(jr, 2 * j, 2 * j + 2)), c("jm", 32 * j, 32 * j + 32))
-        if not last:
-            lengths()
-            soon["stack"] = [tt(c("Sold"), PS, c("pm"), A.mult)]
+        move("T1", c("T3"), PS)
+        group(PS, [(Ih, c("T3")), (c("SHI"), c("Bg")), (c("IL4"), c("Rg"))])
+        if last:
+            for j in range(0, WIDE, WIDE // 4):
+                act(c("Xo", j, j + WIDE // 4), c("X", j, j + WIDE // 4), scale=-32.0)
+            for h0, h1 in halves:
+                tt(c("jm", h0, h1), ind(XW, c("Uq", h0 // 16, h1 // 16)), c(lr, h0, h1), A.max)
         else:
-            act(c("ocnt"), PN, F.Identity, 32.0)
+            move("own", c("jm"), ind(XW, c("Uq")))
+        for j in range(12):
+            off, x = c("joff", 2 * j, 2 * j + 2), c("jm", 32 * j, 32 * j + 32)
+            if last:
+                ts(ind(c("Xo"), off), x, -32.0, A.mult, 0.0, A.add)
+            else:
+                tt(ind(XW, off), x, c(lr, 32 * j, 32 * j + 32), A.max)
+        if not last:
+            tt(c("Sold"), PS, c("pm"), A.mult)
+        else:
+            act(c("ocnt"), PN, F.Identity, 16.0)
             store("ac", T.ycnt[:], (T["ocnt"][0:128:16, :],) + c("ocnt")[1:], "ycnt", 0)
             act(c("ostk"), PS)
             store("ac", T.ystk[:], c("ostk"), "ystk", 1e5)
-            store("sy", T.ylab[:], c("X", 0, V), "ylab", 1e6)
+            store("sy", T.ylab[:], c("Xo", 0, V), "ylab", 1e6)
 
     if "order" not in _PLAN:
         _PLAN["order"] = order_calls(ops)

@@ -2,22 +2,30 @@ import numpy as np
 from concourse.mybir import AluOpType as A, ActivationFunctionType as F
 
 V, P, STEPS = 2048, 224, 3
-DEAD, WIDE = V + 32, V + 48
+DEAD, WIDE = V + 64, V + 80
 CH = [(0, 32), (32, 96), (96, 160), (160, 224)]
 PARTS = [(0, 160), (160, P)]
-SPLIT, EARLY = [256], False
-ONS = [2, 5]
-ENG = dict(own="v", H="s", hit="s", U16="s", Uh="v", Uq="s", Rg="v", v16="v", Vh="v", Kf="v", Wp="v",
+WRITES = [(256, 384), (0, 256)]
+EARLY = False
+ONS = [2]
+ENG = dict(own="s", H="s", hit="s", U16="s", Uh="v", Uq="s", Rg="v", v16="v", Uf="v", Kf="v", Wp="v",
            T1="s", Wv="s", B4h="s")
-ONV, BATCH = [], 4
+BATCH = 4
 HITS = [96, 160, P]
 BANKS, SUMS = [0, 7, 5, 6, 1, 2, 4], "pb0"
 NARROW = [0]
-LOW, GV = [7, 3], [1]
+LOW, GV = [(7, 5, 6), (3, 2, 1)], [1]
 TURN = [("pb3", 128 * (k % 4), 128 * (k % 4) + 128) for k in range(len(CH))]
-HV = []
-PULL = ["g2 g0 g3 g4 g5 g6 H0 H1 H2 t2 H3 t5", "g1 d s1 s0 m1 n1 m0 n0 s2 n2 m2 s3 t0 m3 n3 t1 t4 t3 t6"]
-LOADS = ["nb", "ln", "lab0", "lab1", "lab2", "lab3"]
+HV, WV = [], []
+PLACES = [((0, 160), "pb5"), ((160, P), "pb4")]
+PULL = ["g2 g0 g3 g4 g5 g6 H1 H0 H2 t2 H3", "g1 d s1 s0 n1 m1 n0 m0 s2 n2 m2 s3 t1 m3 n3 t0 t4 t3 t5 t6",
+        "x2 T1 T0 e1 T2 e2 e0 e4 e3 T3 h0 e5 h1 e6 h2"]
+LOADS, LAB = ["nb", "ln", "lab0", "lab1", "lab2", "lab3"], [0, 768, 1408, 1856, V]
+JW, JBANKS = 4, ["pb1", "pb2"]
+PAIRS = lambda wide: [(i, j) for i in range(wide) for j in range(i, -1, -1)]
+LISTS = {"J": (24, JW, 0, 0, 12 * (JW + 1), 64), "Z": (14, 2, 128, 24, 21, 32)}
+NSS = 4
+RAMPS = "PI CC GM XM jm TZ E0 Wp Mb SP C1 ms0 TJ ms1 ms2".split()
 BIG = 2097152.0
 f32, b16, h16, i32, u16 = "float32", "bfloat16", "float16", "int32", "uint16"
 PAD = 128 * len(CH) + 64
@@ -28,22 +36,23 @@ _B = {
     "E": (1024, h16), "E0": (1024, b16), "DV": (P, f32), "Wv": (P, f32),
     "Mb": (PAD, f32), "Hh": (PAD, h16), "Wp": (PAD, b16), "HT": (128 * len(CH), h16),
     "XM": (256, f32), "GM": (128, f32), "PI": (4, i32), "CC": (32, f32), "SPL": (128, b16),
-    "TJ": (576, f32), "TZ": (336, f32), "C1": (16, f32), "JC": (24, f32), "ONE": (P, b16), "RS": (P, b16),
+    "TJ": (960, b16), "TZ": (336, b16), "C1": (16, f32), "JC": (64, f32), "Uf": (40, f32), "LU": (16, u16),
+    "RST": (192, b16), "yz": (192, f32), "ONE": (P, b16), "RS": (P, b16),
     "M1": (144, b16), "MP": (144, b16), "MK4": (144, b16), "Mh": (144, h16), "M35": (144, h16), "ME": (144, b16),
     "MD": (144, b16), "PQ": (144, f32), "Q15": (144, f32), "IW": (144, f32),
     "I1": (128, b16), "I2k": (128, b16), "In2k": (128, b16), "In4": (128, b16), "In1": (128, b16),
     "Id": (128, b16), "Xo": (WIDE, f32), "Inf": (128, f32), "Inh": (128, h16), "IL4": (128, h16), "SE4": (128, h16),
     "Ih": (128, h16), "SHI": (128, h16), "ONES": (128, b16), "REP": (128, b16), "TR1": (128, b16), "TR2": (128, b16),
     "IW4": (144, f32), "NS": (V, h16),
-    "v16": (16, u16), "Vh": (28, h16), "K": (P, u16), "Kf": (P, h16),
+    "v16": (16, u16), "K": (P, u16), "Kf": (P, h16),
     "n1": (P, b16), "r1": (P, b16), "r2": (P, b16), "pm": (P, b16), "Sold": (P, h16),
-    "eqz": (336, b16), "zoff": (14, u16), "hit": (P, b16), "RG": (2 * P, b16), "em": (P, b16), "er": (P, b16),
-    "qu": (16 * P, u16), "qh": (16 * P, h16), "nv": (P, u16), "B4h": (P, h16), "Qh": (144, h16),
-    "IhG": (128, h16), "I2G": (128, b16), "In2G": (128, b16),
-    "nq": (P, b16), "q": (4 * P, f32), "B4": (P, f32), "B4f": (128, f32), "pos": (16, u16),
+    "eqZ": (336, b16), "zoff": (16, u16), "hit": (P, b16), "RG": (2 * P, b16), "em": (P, b16), "er": (P, b16),
+    "qh": (16 * P, h16), "SP": (32, f32), "B4h": (P, h16), "Qh": (144, h16),
+    "IhG": (128, h16), "In2G": (128, b16),
+    "nq": (P, b16), "q": (4 * P, f32), "B4": (P, f32), "pos": (16, u16),
     "epos": (16, u16), "U16": (24, u16), "mt": (P, b16), "m2": (P, b16), "T1": (P, h16), "T2": (P, h16),
-    "T3": (P, h16), "Uh": (48, h16), "Uq": (24, u16), "cio": (2, f32), "inval": (24, b16),
-    "joff": (24, u16), "Rg": (P, h16), "eqj": (576, b16), "giv": (P, b16),
+    "T3": (P, h16), "Uh": (192, h16), "Uq": (24, u16), "cio": (2, f32), "inval": (64, b16),
+    "joff": (32, u16), "Rg": (P, h16), "eqJ": (960, b16), "giv": (P, b16),
     "jm": (384, f32), "Bg": (P, h16), "ostk": (P, f32), "ocnt": (P, f32),
 }
 for _t in range(STEPS):
@@ -53,12 +62,12 @@ for _k in range(8):
     SCRATCH["pb%d" % _k] = ("psum", [128, 512], f32)
 
 SEMAPHORES = (["ve", "ac", "pe", "po", "sent"] + ["d_" + s for s in LOADS + ["stk", "cnt", "ylab", "ystk", "ycnt"]]
-              + ["r%d%s" % (t, s) for t in range(STEPS) for s in "cnabj"])
+              + ["r%d%s" % (t, s) for t in range(STEPS) for s in "cnab"] + ["h%d" % t for t in range(STEPS)])
 
-CYC, GATHER, SCATTER = np.array([0.83e-3, 1.1e-3]), np.array([1.3, 1.6]), np.array([2.5, 4.0])
-PECYC, HBM, LINK, FLY = np.array([0.42e-3, 0.55e-3]), np.array([300e3, 260e3]), np.array([100e3, 35e3]), np.array([1.0, 2.0])
-FIX, WAKE, WAKE1, ISSUE, EAGER = 0.01, 0.22, 0.36, 1.0, 0.3
-ROUNDS, SWEEPS, STRETCH, MOVES, MIX, SHAKE, HEAT = 150, 3, 100, 5000, 0.5, 3.0, 0.6
+CYC, GATHER, SCATTER = np.array([0.83e-3, 1.2e-3]), np.array([1.4, 1.9]), np.array([3.0, 5.2])
+PECYC, HBM, LINK, FLY = np.array([0.42e-3, 0.6e-3]), np.array([330e3, 240e3]), np.array([100e3, 40e3]), np.array([1.0, 2.0])
+FIX, WAKE, WAKE1, ISSUE, EAGER = 0.01, 0.22, 0.27, 1.0, 0.3
+ROUNDS, SWEEPS, STRETCH, MOVES, MIX, SHAKE, HEAT = 150, 3, 80, 4000, 0.5, 3.0, 0.5
 _PLAN = {}
 
 
@@ -227,11 +236,31 @@ def order_calls(ops):
 
 
 def rank_program(g, core, T, topo):
-    rank = T.rank_of(core)
-    if rank is None:
+    def peers(x):
+        return [T.cores[T.rank_of(x) ^ (1 << t)] for t in range(STEPS)]
+
+    def helper(x):
+        free = [y for y in topo.cores_of(x) if T.rank_of(y) is None and topo.die(y) != topo.die(x)
+                and all(topo.may_write(y, z) for z in peers(x))]
+        return free[[y for y in topo.cores_of(x) if T.rank_of(y) is not None].index(x)]
+
+    def engines(x):
+        main = [e for e in topo.engines(x, helper(x)) if all(e in topo.engines(x, y) for y in peers(x))]
+        return main, [e for e in topo.engines(x, helper(x)) if e not in main]
+
+    if T.rank_of(core) is None:
+        for x in [y for y in T.cores if helper(y) == core]:
+            sent = 0
+            for t, y in enumerate(peers(x)):
+                if topo.chip(y) != topo.chip(x):
+                    part, (rid, pid) = T["lr%d" % t][:, WRITES[0][0]:WRITES[0][1]], topo.addr(y)[:2]
+                    g.wait_ge(T.sem["h%d" % t], len(engines(x)[1]))
+                    g.remote_dma(part, part, T.sem["r%db" % t], T.sem["sent"], pid, rid, topo.mask(core, y))
+                    sent += len(topo.engines(core, y))
+            g.wait_ge(T.sem["sent"], sent)
         return
     Q = {"ve": g.vector, "ac": g.scalar, "pe": g.tensor, "po": g, "sy": g.sync}
-    ops, hist = [], {}
+    ops, hist, ramps = [], {}, []
 
     def c(name, a=0, b=None, st=1, p=None):
         b = SCRATCH[name][1][1] if b is None else b
@@ -327,9 +356,10 @@ def rank_program(g, core, T, topo):
 
     def iota(o, pat, base, cm):
         kw = {} if SCRATCH[o[4]][2] == i32 else {"allow_small_or_imprecise_dtypes": True}
-        rec("po", lambda e: e.iota(o[0], pat, base, cm, **kw), [o], [], 0.13 + 2 * CYC * o[3])
+        k = rec("po", lambda e: e.iota(o[0], pat, base, cm, **kw), [o], [], 0.13 + 2 * CYC * o[3])
+        ramps.append((RAMPS.index(o[4]), k))
 
-    landed = [2.0]
+    landed = [1.2]
 
     def load(q, o, src, s, nbytes):
         landed[0] = landed[0] + nbytes / HBM
@@ -339,25 +369,24 @@ def rank_program(g, core, T, topo):
     def store(q, dst, x, s, nbytes):
         rec(q, lambda e: e.dma_start(dst, x[0]), [], [x], 0.05, "d_" + s, 16, 2.0 + nbytes / HBM)
 
-    def common(x):
-        near = [T.cores[T.rank_of(x) ^ (1 << s)] for s in range(STEPS)]
-        return [e for e in topo.engines(x, near[0]) if all(e in topo.engines(x, y) for y in near)]
-
-    peers = [T.cores[rank ^ (1 << t)] for t in range(STEPS)]
-    emask = sum(1 << e for e in common(core))
     sends = []
 
-    def exchange(t, dst, src, s):
-        rid, pid = topo.addr(peers[t])[:2]
-        k = rec("po", lambda e: e.remote_dma(dst[0], src[0], T.sem[s], T.sem["sent"], pid, rid, emask),
-                [], [src], ISSUE * (1 if sends else 2.5), "sent", len(common(core)), 0.0, sends[-1:])
+    def exchange(t, dst, src, s, side=False):
+        far = side and topo.chip(peers(core)[t]) != topo.chip(core)
+        rid, pid = topo.addr(helper(core) if far else peers(core)[t])[:2]
+        eng, sem = engines(core)[side], T.sem["h%d" % t if far else s]
+        k = rec("po", lambda e: e.remote_dma(dst[0], src[0], sem, T.sem["sent"], pid, rid, sum(1 << x for x in eng)),
+                [], [src], ISSUE * (1 if sends else 2.5), "sent", len(eng), 0.0, sends[-1:])
         sends.append(k)
-        prev = [j for j, x in enumerate(ops) if x["q"] == "rx"]
-        rec("rx", None, [dst], [], 512 * src[3] / LINK, s, len(common(peers[t])), FLY, [k] + prev[-1:])
+        q, other = "rx%d" % side, peers(core)[t]
+        prev = [j for j, x in enumerate(ops) if x["q"] == q]
+        rec(q, None, [dst], [], 512 * src[3] / LINK, s,
+            len(topo.engines(helper(other), core) if far else engines(other)[side]),
+            FLY + far * (FLY + 2 * ISSUE + 512 * src[3] / LINK / 2), [k] + prev[-1:])
 
     col = lambda j: c("CC", j, j + 1)
-    (PCOL, ACOL, QCOL, LANE, GCOL, DUM, LT4, GE4, EQ4, S1, SM15, S15, Q24, G16, DUM2, HALF, LT8, EW, R35, E44,
-     PAT, NG, EQ5, PW, SGN, THR) = range(26)
+    (PCOL, ACOL, QCOL, LANE, GCOL, LT4, GE4, EQ4, S1, SM15, S15, G16, HALF, LT8, EW, R35, E44,
+     PAT, NG, EQ5, PW, SGN, THR) = range(23)
     I1, I2k, In2k, Ih = c("I1"), c("I2k"), c("In2k"), c("Ih")
     xm = lambda o, n: c("XM", 16 + o, 16 + o + n)
     m143 = lambda s: c(s, 0, 143)
@@ -365,8 +394,8 @@ def rank_program(g, core, T, topo):
     load("sy", c("cnts", p=(0, 8)), T.cnt[:], "cnt", 0)
     load("sy", c("stks"), T.stk[:], "stk", 1e5)
     big = {"nb": (c("nbs", 0, V), T.nb[:], 1e6), "ln": (c("W", 0, V), T.ln[:], 5e5)}
-    for j in range(0, V, 512):
-        big["lab%d" % (j // 512)] = (c("labs", j, j + 512), T.lab[:, j:j + 512], 2.6e5)
+    for j, (x, y) in enumerate(zip(LAB, LAB[1:])):
+        big["lab%d" % j] = (c("labs", x, y), T.lab[:, x:y], 512 * (y - x))
     for s in LOADS:
         load("sy", big[s][0], big[s][1], s, big[s][2])
     iota(c("PI", 0, 1), [[0, 1]], 0, 1)
@@ -383,10 +412,9 @@ def rank_program(g, core, T, topo):
     ts(c("PI", 3, 4), c("PI", 0, 1), 63, A.bitwise_and)
     cp(c("CC", ACOL, ACOL + 3), c("PI", 1, 4))
     tt(col(GCOL), col(PCOL), col(ACOL), A.subtract)
-    for j, s in ((SM15, -15.0), (S1, 1.0), (DUM, float(V)), (DUM2, V + 16.0), (HALF, 0.5)):
+    for j, s in ((SM15, -15.0), (S1, 1.0), (HALF, 0.5)):
         act(col(j), col(ACOL), bias=s)
     act(col(S15), col(ACOL), bias=15.0, scale=-1.0)
-    act(col(Q24), col(QCOL), bias=4.0)
     ts(col(LT4), col(ACOL), 4.0, A.is_lt)
     ts(col(GE4), col(ACOL), 4.0, A.is_ge)
     ts(col(EQ4), col(ACOL), 4.0, A.is_equal)
@@ -417,21 +445,35 @@ def rank_program(g, core, T, topo):
                   ("Inh", -1.0), ("IL4", col(LT4)), ("B4", -32.0)) + (("Inf", -1.0),) * bool(ONS):
         act(c(nm, 0, 128), I32, scale=s)
     act(c("IhG"), I32, scale=col(GE4))
-    act(c("I2G"), c("IhG"), scale=2048.0)
     act(c("In2G"), c("IhG"), scale=-2048.0)
     ts(c("E"), c("E0"), col(LANE), A.is_equal)
     ts(c("ONES"), c("GM"), col(GCOL), A.is_equal)
     ts(c("SE4"), c("ONES"), col(EQ4), A.mult, 4.0, A.mult)
-    iota(c("Wg", 0, V), [[1, 16], [16, 8], [0, 16]], 0, 0)
-    ts(c("NS"), c("Wg", 0, V), col(PCOL), A.is_equal, -1.0, A.mult)
-    for nm, n in (("TZ", 7), ("TJ", 12)):
-        iota(c(nm), [[1, 16], [0, 3 * n]], 0, 0)
-        rec("po", lambda e, x=c(nm), n=n: e.affine_select(x[0], x[0], [[0, 16], [1, 3], [0, n]], A.not_equal, 100.0, -1, 0),
-            [c(nm)], [c(nm)], 0.17 + 2 * CYC * 48 * n)
-        act(c(nm), c(nm), F.Relu, col(HALF), -1.0)
-    ts(c("B4f", 0, 128), xm(0, 128), col(PCOL), A.is_ge)
-    tt(c("B4f", 0, 128), c("B4f", 0, 128), c("ONES"), A.mult)
-    tt(c("TR1"), c("B4f", 0, 128), c("B4", 0, 128), A.add)
+    ts(c("ocnt", 0, 16), xm(0, 16), col(ACOL), A.is_equal, -1.0, A.mult)
+    for b in range(16):
+        (act(c("NS", 128 * b, 128 * b + 128), c("ONES"), scale=c("ocnt", b, b + 1)) if b % NSS == 0 else
+         ts(c("NS", 128 * b, 128 * b + 128), c("ONES"), c("ocnt", b, b + 1), A.mult))
+    fill(c("qh", 0, 256), 0.0)
+    fill(c("RST"), 1.0)
+    for kind, (n, wide, at, src, w, pad) in LISTS.items():
+        pairs, calls, tri = PAIRS(wide), n // wide, c("jm", 128 + at, 128 + at + 16 * n // wide)
+        iota(tri, [[1, 16], [0, calls]], 0, 0)
+        iota(c("T" + kind, 0, 16 * w), [[0, 16 * w]], 0, 0)
+        for r, (i, j) in enumerate(pairs):
+            for x, y in ((0, j), (pad, i)):
+                act(c("qh", at + x + r, at + x + w, len(pairs)), xm(0, calls), bias=y / 16, scale=wide / 16)
+            if j == 0:
+                act(c("qh", 192 + at // 4 + i, 192 + at // 4 + n, wide), xm(0, calls), bias=r / 16, scale=len(pairs) / 16)
+            if i == j:
+                act(c("T" + kind, r, 16 * w, len(pairs)), tri, F.Relu, col(HALF), -1.0)
+                fill(c("RST", at + r, at + w, len(pairs)), 0.0)
+    group(c("pb7", 0, 16), wrap("Mh", "qh", 0, 256))
+    cp(c("LU"), c("pb7", 0, 16))
+    iota(c("SP"), [[0, 32 // JW], [16, JW]], V, 0)
+    act(c("SP"), c("SP"), bias=col(ACOL))
+    ts(c("jm", 0, 128), xm(0, 128), col(PCOL), A.is_ge)
+    tt(c("jm", 0, 128), c("jm", 0, 128), c("ONES"), A.mult)
+    tt(c("TR1"), c("jm", 0, 128), c("B4", 0, 128), A.add)
     act(c("TR2"), c("TR1"), scale=2048.0)
     ts(m143("PQ"), xm(-16, 143), col(GCOL), A.is_equal)
     tt(m143("PQ"), m143("PQ"), m143("Q15"), A.add)
@@ -441,8 +483,8 @@ def rank_program(g, core, T, topo):
     act(c("SPL"), c("ONES"), scale=col(PW))
     ts(c("DV", 0, 128), xm(4, 128), col(PCOL), A.is_equal, col(GE4), A.mult)
     tt(c("SHI"), c("DV", 0, 128), I32, A.subtract)
-    act(c("JC", 0, 12), xm(0, 12), bias=col(QCOL), scale=8.0)
-    act(c("JC", 12, 24), xm(0, 12), bias=col(Q24), scale=8.0)
+    act(c("yz", 0, 24), xm(0, 24), bias=col(QCOL), scale=4.0)
+    act(c("JC"), ind(c("yz", 0, 24), c("LU", 4, 8)))
     fill(c("X", V, WIDE), 0.0)
     fill(c("W", V, WIDE), 1.0)
     fill(c("nbs", V, WIDE), DEAD)
@@ -455,45 +497,47 @@ def rank_program(g, core, T, topo):
         act(c("mr%d" % t, 104, 240), xm(0, 136), bias=col(PAT), scale=0.0)
         fill(c("mr%d" % t, 240, 248), 0.0)
 
+    for (_, x), (_, y) in zip(sorted(ramps), sorted(ramps)[1:]):
+        ops[y]["after"].add(x)
+
     XW, v14 = c("X"), c("v16", 0, 14)
     PA, PB, PS, PN = c("pb6", 256, 256 + P), c("pb6", 0, P), c("pb7", 0, P), c("pb5", 256, 256 + P)
     PV, PU, PC, PY = c("pb4", 320, 334), c("pb3", 0, 24), c("pb0", 0, P), c("pb0", 256, 256 + P)
     slot = lambda nm, k, a0, b0: c(nm, 128 * k + 64 + a0, 128 * k + 64 + b0)
 
-    def distinct(src, n, banks, tri, eq, y, off, more=None):
-        per, w = 16 // len(banks), 3 * n
-        for j, bk in enumerate(banks):
-            group([(c(bk, w * b, w * b + w), [(Ih, c(src, 0, w)),
-                                              (c("NS", 128 * (per * j + b), 128 * (per * j + b) + 128), c(src, n, 4 * n))])
-                   for b in range(per)], None)
-            piece = (w * per * j, w * per * (j + 1))
-            tt(c(eq, *piece), c(bk, 0, w * per), c(tri, *piece), A.is_equal)
-        mk = lambda b: c("MK4", 15 - b, 143 - b)
-        for j in range(len(banks)):
-            bs = range(per * j, per * (j + 1))
-            group(c(y[0], y[1], y[1] + 2 * n), [(Ih, c(src, n, 3 * n))] * (j == 0)
-                  + [(mk(b), c(eq, w * b, w * b + 2 * n)) for b in bs] + (more if j else []), j == 0, False)
-            group(c(y[0], y[1] + n, y[1] + 2 * n), [(mk(b), c(eq, w * b + 2 * n, w * b + w)) for b in bs],
-                  False, j == len(banks) - 1)
-        ts(c(off, 0, 2 * n, 2), c(y[0], y[1], y[1] + n), col(DUM), A.min)
-        ts(c(off, 1, 2 * n, 2), c(y[0], y[1] + n, y[1] + 2 * n), col(DUM2), A.min)
+    def distinct(kind, names, banks, y, off, more=()):
+        n, wide, at, src, w, pad = LISTS[kind]
+        per = -(-16 // len(banks))
+        rows = [range(per * j, min(16, per * j + per)) for j in range(len(banks))]
+        move("Uf", c("Uf", src, src + n), names)
+        move("Uh", c("Uh", at, at + 2 * pad), ind(c("Uf", src, src + n), c("LU", at // 16, (at + 2 * pad) // 16)))
+        mine, other, eq = c("Uh", at + pad, at + pad + w), c("Uh", at, at + w), "eq" + kind
+        for bk, bs in zip(banks, rows):
+            group([(c(bk, w * (b - bs[0]), w * (b - bs[0] + 1)), [(Ih, other), (c("NS", 128 * b, 128 * b + 128), mine)])
+                   for b in bs], None)
+            piece = (w * bs[0], w * (bs[-1] + 1))
+            tt(c(eq, *piece), c(bk, 0, w * len(bs)), c("T" + kind, *piece), A.is_equal)
+        y = c(y[0], y[1], y[1] + w)
+        for j, bs in enumerate(rows):
+            group(y, [(Ih, mine)] * (j == 0) + list(more) * (j == 0)
+                  + [(c("MK4", 15 - b, 143 - b), c(eq, w * b, w * b + w)) for b in bs], j == 0, j == len(banks) - 1)
+        scan(c("yz", at, at + w), c("RST", at, at + w), y, 0.0, A.mult, A.max)
+        ends = 12 + at // 64
+        tt(c(off), ind(c("yz", at, at + w), c("LU", ends, ends + (n + 15) // 16)), c("SP", 0, SCRATCH[off][1][1]), A.min)
 
     def popped():
         move("v16", v14, PV)
         cp(c("K"), ind(c("nbs"), v14))
         move("Kf", c("Kf"), c("K"))
-        prev = []
         for j in range(7):
-            prev = [act(c("Wg", 512 * j, 512 * j + 512), ind(c("W"), c("K", 32 * j, 32 * j + 32)), after=prev)]
+            (cp if j in WV else act)(c("Wg", 512 * j, 512 * j + 512), ind(c("W"), c("K", 32 * j, 32 * j + 32)))
         move("Wv", c("Wv"), ind(c("W"), v14), -1 / 32)
         for k, (l0, l1) in enumerate(CH):
             move("Wp", slot("Wp", k, 0, l1 - l0), c("Wv", l0, l1))
-        act(c("n1"), PN, F.Relu, 15.0)
-        act(c("r1"), c("n1"), F.Relu, col(S1), -1.0)
-        act(c("pm"), c("r1"), F.Relu, 1.0, -1.0)
-        for j in range(4):
-            move("Vh", c("Vh", 7 * j, 7 * j + 7), c("pb4", 320 + j // 2, 334, 2))
-        distinct("Vh", 7, ["pb4"], "TZ", "eqz", ("pb4", 352), "zoff")
+        ts(c("n1"), PN, 15.0, A.add, 0.0, A.max)
+        ts(c("r1"), c("n1"), col(S1), A.subtract, 0.0, A.min)
+        ts(c("pm"), c("n1"), col(ACOL), A.is_gt)
+        distinct("Z", PV, ["pb4"], ("pb4", 352), "zoff")
 
     ts(c("cntb", p=(0, 8)), c("cnts", p=(0, 8)), 16.0, A.subtract)
     group(PN, [(c("REP", p=(0, 8)), c("cntb", p=(0, 8)))])
@@ -502,8 +546,8 @@ def rank_program(g, core, T, topo):
     tt(c("T2"), c("m2"), c("stks"), A.mult)
     group(PV, wrap("MD", "em", 0, P), True, False)
     group(PV, wrap("Mh", "T2", 0, P), False, True)
-    for j in range(4):
-        ts(c("X", 512 * j, 512 * j + 512), c("labs", 512 * j, 512 * j + 512), -1 / 32, A.mult)
+    for x, y in zip(LAB, LAB[1:]):
+        ts(c("X", x, y), c("labs", x, y), -1 / 32, A.mult)
     popped()
     tt(c("Sold"), c("pm"), c("stks"), A.mult)
 
@@ -537,10 +581,9 @@ def rank_program(g, core, T, topo):
                 at = 32 * j - l0
                 tag["z%d" % j] = tt(ind(XW, c("zoff", 2 * j, 2 * j + 2)), slot("Mb", k, at, at + 32),
                                     c("Wv", 32 * j, 32 * j + 32), A.add)
-            if l1 in HITS:
-                h0 = ([0] + HITS)[HITS.index(l1)]
-                tag["h%d" % HITS.index(l1)] = group(c(SUMS, h0, l1), [
-                    (c("M1", 15 - i, 143 - i), c("Ind", 16 * h0 + i, 16 * l1, 16)) for i in range(16)])
+        for j, (h0, h1) in enumerate(zip([0] + HITS, HITS)):
+            tag["h%d" % j] = group(c(SUMS, h0, h1), [
+                (c("M1", 15 - i, 143 - i), c("Ind", 16 * h0 + i, 16 * h1, 16)) for i in range(16)])
         for line in PULL:
             for x, y in zip(line.split(), line.split()[1:]):
                 ops[tag[y]]["after"].add(tag[x])
@@ -549,51 +592,52 @@ def rank_program(g, core, T, topo):
                 act(c("hit", *pt), c(SUMS, *pt), F.Sign)
             else:
                 ts(c("hit", *pt), c(SUMS, *pt), 0.0, A.is_gt)
-            group(c("pb6", *pt), [(I2k, c("n1", *pt)), (Ih, c("Kf", *pt)), (c("TR2"), c("hit", *pt))])
-            high = c("pb6", 256 + pt[0], 256 + pt[1])
-            for x in (c("pb5", *pt), high):
-                group(x, [(I1, c("n1", *pt)), (c("ONES"), c("hit", *pt))])
-            low = c("pb%d" % LOW[PARTS.index(pt)], *pt)
-            group(low, [(Ih, c("Sold", *pt)), (I2k, c("r1", *pt))], True, False)
+            j = PARTS.index(pt)
+            low, forv, fors = ("pb%d" % x for x in LOW[j])
+            low, val, high = c(low, *pt), c(fors, *pt), c(fors, 256 + pt[0], 256 + pt[1])
+            for x in sorted({fors, "pb6"}):
+                group(c(x, *pt), [(I2k, c("n1", *pt)), (Ih, c("Kf", *pt)), (c("TR2"), c("hit", *pt))])
+                group(c(x, 256 + pt[0], 256 + pt[1]), [(I1, c("n1", *pt)), (c("ONES"), c("hit", *pt))])
+            group(c(forv, *pt), [(I1, c("n1", *pt)), (c("ONES"), c("hit", *pt))])
+            group(low, [(Ih, c("Sold", *pt)), (In2k, c("r1", *pt))], True, False)
             act(c("r2", *pt), high, F.Relu, col(S1), -1.0)
+            act(c("em", *pt), high, F.Relu, 1.0, -1.0, total=c(ms, 4 + j, 5 + j))
             group(low, [(In2k, c("r2", *pt))], False, False)
             n, at = pt[1] - pt[0], 4 * pt[0]
-            if PARTS.index(pt) in NARROW:
+            if j in NARROW:
                 for s in range(4):
-                    act(c("qu", at + n * s, at + n * s + n), c("pb6", *pt), F.Relu, 2048.0 * (s + 1) - 63488.0, -1.0)
-                ts(c("qh", at, at + 4 * n), c("qu", at, at + 4 * n), 2048.0, A.min)
+                    act(c("qh", at + n * s, at + n * s + n), val, F.Relu, 2048.0 * (s + 1) - 63488.0, -1.0)
+                ts(c("qh", at, at + 4 * n), c("qh", at, at + 4 * n), 2048.0, A.min)
                 group(low, [(c("Qh", 15 - s, 143 - s), c("qh", at + n * s, at + n * s + n)) for s in range(4)], False, True)
             else:
                 for s in range(4):
                     qs = c("q", at + n * s, at + n * s + n)
-                    act(qs, c("pb6", *pt), F.Relu, 2048.0 * (s + 1) - 63488.0, -1.0)
+                    act(qs, val, F.Relu, 2048.0 * (s + 1) - 63488.0, -1.0)
                     group(low, [(c("PQ", 15 - s, 143 - s), qs)], False, s == 3)
             act(c("B4", *pt), low, bias=col(EQ4), scale=col(LT4))
             flag = c("RG", P + pt[0], P + pt[1])
-            ts(flag, c("pb5", *pt), col(SGN), A.mult, col(THR), A.is_ge)
+            ts(flag, c(forv, *pt), col(SGN), A.mult, col(THR), A.is_ge)
             scan(c("RG", *pt), c("RS", *pt), flag, c("RG", pt[0] - 1, pt[0]) if pt[0] else -1.0, A.mult, A.add)
         move("B4h", c("B4h"), c("B4"), col(LT4))
-        group(c("pb4", 256, 270), wrap("MP", "RG", 0, P))
-        tt(c("pos", 0, 14), c("pb4", 256, 270), c("C1", 0, 14), A.min)
-        act(c("em"), PA, F.Relu, 1.0, -1.0, total=c(ms, 4, 5))
+        for (l0, l1), bank in PLACES:
+            group(c(bank, 256 + l0 // 16, 256 + l1 // 16), wrap("MP", "RG", l0, l1))
+            tt(c("pos", l0 // 16, l1 // 16), c(bank, 256 + l0 // 16, 256 + l1 // 16), c("C1", l0 // 16, l1 // 16), A.min)
+            cp(ind(c(ms, 8, 456), c("pos", l0 // 16, l1 // 16)), c("B4", l0, l1))
         if EARLY:
             exchange(t, c(mr, 4, 6), c(ms, 4, 6), "r%dc" % t)
-        cp(ind(c(ms, 8, 456), c("pos", 0, 14)), c("B4"))
         exchange(t, c(mr, 8 if EARLY else 4, 104), c(ms, 8 if EARLY else 4, 104), "r%dn" % t)
         wrapped = lambda x: [(c("IW4", 12 - 4 * qq, 140 - 4 * qq), c(x, 8 + qq, 104, 4)) for qq in range(4)]
         group(PU, wrapped(ms))
         move("U16", c("U16"), PU)
-        halves = list(zip([0] + SPLIT, SPLIT + [384]))
-        for j, (h0, h1) in enumerate(halves):
+        for j, (h0, h1) in enumerate(WRITES):
             act(c(ls, h0, h1), ind(XW, c("U16", h0 // 16, h1 // 16)))
-            exchange(t, c(lr, h0, h1), c(ls, h0, h1), "r%d%s" % (t, "abj"[j]))
-        ts(c("inval"), c("JC"), c(ms, 4, 5), A.is_ge, 4096.0, A.mult)
+            exchange(t, c(lr, h0, h1), c(ls, h0, h1), "r%d%s" % (t, "bac"[j]), j == 0)
+        act(c("cio", 1, 2), c(ms, 4, 5), bias=c(ms, 5, 6))
+        ts(c("inval"), c("JC"), c("cio", 1, 2), A.is_ge, 4096.0, A.mult)
         group(c("pb3", 24, 48), wrapped(mr))
-        for j in range(4):
-            move("Uh", c("Uh", 12 * j, 12 * j + 12), c("pb3", 24 + j // 2, 48, 2))
-        move("Uq", c("Uq"), c("pb3", 24, 48))
-        distinct("Uh", 12, ["pb1", "pb2"], "TJ", "eqj", ("pb3", 128), "joff", [(I1, c("inval"))])
-        ts(c("cio", 0, 1), c(mr, 4, 5), 96.0, A.min)
+        distinct("J", c("pb3", 24, 48), JBANKS, ("pb3", 128), "joff", [(I1, c("inval", 0, LISTS["J"][4]))])
+        move("Uq", c("Uq"), c("Uf", 0, 24))
+        ts(c("cio", 0, 1), c(mr, 4, 5), c(mr, 5, 6), A.add, 96.0, A.min)
         act(c("nq"), PA, F.Relu, 16.0, -1.0)
         scan(c("er"), c("RS"), c("em"), 0.0, A.mult, A.add)
         PE_ = c("pb4", 288, 302)
@@ -608,16 +652,11 @@ def rank_program(g, core, T, topo):
             group(PV, wrap("Mh", "T1", 0, P), True, False)
             group(PV, wrap("Mh", "T2", 0, P), False, False)
         group(PY, [(c("SPL"), c("RG", 0, P))])
-        if ONV:
-            ts(c("nv"), PB, -1.0, A.mult, -30720.0, A.add)
-        group(PS, [(Ih, c("B4h")), (c("IhG"), c("Sold")), (c("I2G"), c("r1")), (c("In2G"), c("r2"))], True, False)
+        group(PS, [(Ih, c("B4h")), (c("IhG"), c("Sold")), (c("In2G"), c("r1")), (c("In2G"), c("r2"))], True, False)
         for s0 in range(4, 16, BATCH):
             for s in range(s0, s0 + BATCH):
-                if s in ONV:
-                    ts(c("qu", P * s, P * s + P), c("nv"), 2048.0 * (15 - s), A.subtract, 0.0, A.max)
-                else:
-                    act(c("qu", P * s, P * s + P), PB, F.Relu, 2048.0 * (s + 1) - 63488.0, -1.0)
-            ts(c("qh", P * s0, P * (s0 + BATCH)), c("qu", P * s0, P * (s0 + BATCH)), 2048.0, A.min)
+                act(c("qh", P * s, P * s + P), PB, F.Relu, 2048.0 * (s + 1) - 63488.0, -1.0)
+            ts(c("qh", P * s0, P * (s0 + BATCH)), c("qh", P * s0, P * (s0 + BATCH)), 2048.0, A.min)
             group(PS, [(c("Qh", 15 - s, 143 - s), c("qh", P * s, P * s + P)) for s in range(s0, s0 + BATCH)],
                   False, s0 + BATCH == 16)
         move("Rg", c("Rg"), ind(c(mr, 8, 248), c("epos", 0, 14)))
@@ -632,23 +671,23 @@ def rank_program(g, core, T, topo):
         if last:
             for j in range(0, WIDE, WIDE // 4):
                 act(c("Xo", j, j + WIDE // 4), c("X", j, j + WIDE // 4), scale=-32.0)
-            for h0, h1 in halves:
+            for h0, h1 in sorted(WRITES):
                 tt(c("jm", h0, h1), ind(XW, c("Uq", h0 // 16, h1 // 16)), c(lr, h0, h1), A.max)
         else:
             move("own", c("jm"), ind(XW, c("Uq")))
-        for j in range(12):
-            off, x = c("joff", 2 * j, 2 * j + 2), c("jm", 32 * j, 32 * j + 32)
+        for j in range(0, 24, JW):
+            off, x = c("joff", j, j + JW), c("jm", 16 * j, 16 * (j + JW))
             if last:
                 ts(ind(c("Xo"), off), x, -32.0, A.mult, 0.0, A.add)
             else:
-                tt(ind(XW, off), x, c(lr, 32 * j, 32 * j + 32), A.max)
+                tt(ind(XW, off), x, c(lr, 16 * j, 16 * (j + JW)), A.max)
         if not last:
             tt(c("Sold"), PS, c("pm"), A.mult)
         else:
             act(c("ocnt"), PN, F.Identity, 16.0)
-            store("ac", T.ycnt[:], (T["ocnt"][0:128:16, :],) + c("ocnt")[1:], "ycnt", 0)
+            store("ac", T.ycnt[:], (T["ocnt"][0:128:16, :],) + c("ocnt")[1:], "ycnt", 1.2e6)
             act(c("ostk"), PS)
-            store("ac", T.ystk[:], c("ostk"), "ystk", 1e5)
+            store("ac", T.ystk[:], c("ostk"), "ystk", 1.2e6)
             store("sy", T.ylab[:], c("Xo", 0, V), "ylab", 1e6)
 
     if "order" not in _PLAN:
@@ -659,7 +698,7 @@ def rank_program(g, core, T, topo):
     need, covered, signal = {}, {}, set()
     for k in order:
         best = {}
-        if ops[k]["q"] != "rx":
+        if ops[k]["call"]:
             for d in ops[k]["wait"] | extra[k]:
                 if place[d] > place.get(best.get(keyof(d)), -1):
                     best[keyof(d)] = d
@@ -676,7 +715,7 @@ def rank_program(g, core, T, topo):
             value[k] = total[keyof(k)]
     for k in order:
         o = ops[k]
-        if o["q"] == "rx":
+        if not o["call"]:
             continue
         e = Q[o["q"]]
         for key, d in need[k].items():

import numpy as np
from concourse.mybir import AluOpType as A, ActivationFunctionType as F

V, P, STEPS = 2048, 224, 3
DEAD, WIDE = V + 64, V + 80
CH = [(0, 32), (32, 96), (96, 160), (160, 224)]
PARTS = [(0, 160), (160, P)]
WRITES = [(256, 384), (0, 256)]
EARLY = False
ONS = [2]
ENG = dict(own="s", H="s", hit="s", U16="s", Uh="v", Uq="s", Rg="v", v16="v", Uf="v", Kf="v", Wp="v",
           T1="s", Wv="s", B4h="s")
BATCH = 4
HITS = [96, 160, P]
BANKS, SUMS = [0, 7, 5, 6, 1, 2, 4], "pb0"
NARROW = [0]
LOW, GV = [(7, 5, 6), (3, 2, 1)], [1]
TURN = [("pb3", 128 * (k % 4), 128 * (k % 4) + 128) for k in range(len(CH))]
HV, WV = [], []
PLACES = [((0, 160), "pb5"), ((160, P), "pb4")]
PULL = ["g2 g0 g3 g4 g5 g6 H1 H0 H2 t2 H3", "g1 d s1 s0 n1 m1 n0 m0 s2 n2 m2 s3 t1 m3 n3 t0 t4 t3 t5 t6",
        "x2 T1 T0 e1 T2 e2 e0 e4 e3 T3 h0 e5 h1 e6 h2"]
LOADS, LAB = ["nb", "ln", "lab0", "lab1", "lab2", "lab3"], [0, 768, 1408, 1856, V]
JW, JBANKS = 4, ["pb1", "pb2"]
PAIRS = lambda wide: [(i, j) for i in range(wide) for j in range(i, -1, -1)]
LISTS = {"J": (24, JW, 0, 0, 12 * (JW + 1), 64), "Z": (14, 2, 128, 24, 21, 32)}
NSS = 4
RAMPS = "PI CC GM XM jm TZ E0 Wp Mb SP C1 ms0 TJ ms1 ms2".split()
BIG = 2097152.0
f32, b16, h16, i32, u16 = "float32", "bfloat16", "float16", "int32", "uint16"
PAD = 128 * len(CH) + 64
_B = {
    "nbs": (WIDE, i32), "labs": (V, i32), "W": (WIDE, b16), "X": (WIDE, f32),
    "stks": (P, i32), "cnts": (P, i32), "cntb": (P, b16),
    "G": (P * 16, f32), "A0": (1024, b16), "SO": (P * 16, f32), "Wg": (P * 16, b16), "Ind": (P * 16, b16),
    "E": (1024, h16), "E0": (1024, b16), "DV": (P, f32), "Wv": (P, f32),
    "Mb": (PAD, f32), "Hh": (PAD, h16), "Wp": (PAD, b16), "HT": (128 * len(CH), h16),
    "XM": (256, f32), "GM": (128, f32), "PI": (4, i32), "CC": (32, f32), "SPL": (128, b16),
    "TJ": (960, b16), "TZ": (336, b16), "C1": (16, f32), "JC": (64, f32), "Uf": (40, f32), "LU": (16, u16),
    "RST": (192, b16), "yz": (192, f32), "ONE": (P, b16), "RS": (P, b16),
    "M1": (144, b16), "MP": (144, b16), "MK4": (144, b16), "Mh": (144, h16), "M35": (144, h16), "ME": (144, b16),
    "MD": (144, b16), "PQ": (144, f32), "Q15": (144, f32), "IW": (144, f32),
    "I1": (128, b16), "I2k": (128, b16), "In2k": (128, b16), "In4": (128, b16), "In1": (128, b16),
    "Id": (128, b16), "Xo": (WIDE, f32), "Inf": (128, f32), "Inh": (128, h16), "IL4": (128, h16), "SE4": (128, h16),
    "Ih": (128, h16), "SHI": (128, h16), "ONES": (128, b16), "REP": (128, b16), "TR1": (128, b16), "TR2": (128, b16),
    "IW4": (144, f32), "NS": (V, h16),
    "v16": (16, u16), "K": (P, u16), "Kf": (P, h16),
    "n1": (P, b16), "r1": (P, b16), "r2": (P, b16), "pm": (P, b16), "Sold": (P, h16),
    "eqZ": (336, b16), "zoff": (16, u16), "hit": (P, b16), "RG": (2 * P, b16), "em": (P, b16), "er": (P, b16),
    "qh": (16 * P, h16), "SP": (32, f32), "B4h": (P, h16), "Qh": (144, h16),
    "IhG": (128, h16), "In2G": (128, b16),
    "nq": (P, b16), "q": (4 * P, f32), "B4": (P, f32), "pos": (16, u16),
    "epos": (16, u16), "U16": (24, u16), "mt": (P, b16), "m2": (P, b16), "T1": (P, h16), "T2": (P, h16),
    "T3": (P, h16), "Uh": (192, h16), "Uq": (24, u16), "cio": (2, f32), "inval": (64, b16),
    "joff": (32, u16), "Rg": (P, h16), "eqJ": (960, b16), "giv": (P, b16),
    "jm": (384, f32), "Bg": (P, h16), "ostk": (P, f32), "ocnt": (P, f32),
}
for _t in range(STEPS):
    _B.update({"ls%d" % _t: (384, f32), "lr%d" % _t: (384, f32), "ms%d" % _t: (456, f32), "mr%d" % _t: (248, f32)})
SCRATCH = {k: ("sbuf", [128, n], d) for k, (n, d) in _B.items()}
for _k in range(8):
    SCRATCH["pb%d" % _k] = ("psum", [128, 512], f32)

SEMAPHORES = (["ve", "ac", "pe", "po", "sent"] + ["d_" + s for s in LOADS + ["stk", "cnt", "ylab", "ystk", "ycnt"]]
              + ["r%d%s" % (t, s) for t in range(STEPS) for s in "cnab"] + ["h%d" % t for t in range(STEPS)])

CYC, GATHER, SCATTER = np.array([0.83e-3, 1.2e-3]), np.array([1.4, 1.9]), np.array([3.0, 5.2])
PECYC, HBM, LINK, FLY = np.array([0.42e-3, 0.6e-3]), np.array([330e3, 240e3]), np.array([100e3, 40e3]), np.array([1.0, 2.0])
FIX, WAKE, WAKE1, ISSUE, EAGER = 0.01, 0.22, 0.27, 1.0, 0.3
ROUNDS, SWEEPS, STRETCH, MOVES, MIX, SHAKE, HEAT = 150, 3, 80, 4000, 0.5, 3.0, 0.5
_PLAN = {}


def order_calls(ops):
    n = len(ops)
    pred = [[(d, ops[d]["lat"] + WAKE if d in o["wait"] else 0.0) for d in sorted(o["after"])] for o in ops]
    succ = [[] for _ in range(n)]
    for k in range(n):
        for d, lag in pred[k]:
            succ[d].append((k, lag))

    def plan(before, rank, first):
        end, busy = [0.0] * n, {}
        for k in sorted(range(n), key=lambda j: -rank[j]):
            o, t = ops[k], max([end[d] + lag for d, lag in before[k]], default=first[k])
            rows = [(x, y) for x, y, q in busy.get(o["q"], []) if y > t]
            for b in o["banks"]:
                rows += [(x - WAKE, y + WAKE) for x, y, q in busy.get(b, []) if q != o["q"] and y + WAKE > t]
            for x, y in sorted(rows):
                if x >= t + o["cost"]:
                    break
                t = max(t, y)
            end[k] = t + o["cost"]
            for r in [o["q"]] + sorted(o["banks"]):
                busy.setdefault(r, []).append((t, end[k], o["q"]))
        return end

    rank, left = [0.0] * n, [len(x) for x in succ]
    back = [k for k in range(n) if not left[k]]
    for k in back:
        rank[k] = ops[k]["cost"] + max([lag + rank[s] for s, lag in succ[k]], default=ops[k]["lat"])
        for d, lag in pred[k]:
            left[d] -= 1
            if not left[d]:
                back.append(d)
    best, seed = None, 1
    for r in range(ROUNDS):
        end = plan(pred, rank, [0.0] * n)
        span = max(end[k] + ops[k]["lat"] for k in range(n))
        if best is None or span < best[0]:
            best, kept = (span, end, sorted(range(n), key=lambda j: (end[j] - ops[j]["cost"], end[j], j))), rank
        if r % 3 == 2:
            rank = [0.0] * n
            for k in back:
                seed = (seed * 1103515245 + 12345) % 2147483648
                shake = SHAKE * (seed / 2147483648 - 0.5) * ((seed >> 9) % 8 == 0)
                rank[k] = max([kept[k] + shake] + [rank[s] + 1e-6 for s, lag in succ[k]])
        else:
            rank = plan(succ, end, [o["lat"] for o in ops])
    cost = [[float(o["both"][0][s]) for o in ops] + [0.0] for s in range(2)]
    lat = [[float(o["both"][1][s]) for o in ops] for s in range(2)]
    wake = (WAKE, WAKE1)
    before = [[(d, lat[0][d] + WAKE, lat[1][d] + WAKE1) if d in o["wait"] else (d, 0.0, 0.0) for d in o["after"]]
              for o in ops]
    queue, banks = [o["q"] for o in ops] + [None], [sorted(o["banks"]) for o in ops]
    behind = [{s for s, lag in x} for x in succ]
    c0, c1 = cost

    def holders(part, last, bank):
        held = {}
        for k in part:
            held[k] = [(last.get(queue[k], n), 0)] + [(bank[b], 1) for b in banks[k] if queue[bank.get(b, k)] != queue[k]]
            last[queue[k]] = k
            for b in banks[k]:
                bank[b] = k
        return held

    def run(part, e0, e1, last, bank):
        for k in part:
            q = queue[k]
            d = last.get(q, n)
            t0, t1 = e0[d], e1[d]
            for d, x, y in before[k]:
                x += e0[d]
                if x > t0:
                    t0 = x
                y += e1[d]
                if y > t1:
                    t1 = y
            for b in banks[k]:
                d = bank.get(b)
                if d is not None and queue[d] != q:
                    t0, t1 = max(t0, e0[d] + WAKE), max(t1, e1[d] + WAKE1)
                bank[b] = k
            e0[k], e1[k], last[q] = t0 + c0[k], t1 + c1[k], k

    order = best[2]
    for lo in [x for r in range(SWEEPS) for x in range(0, max(1, n - STRETCH // 2), STRETCH // 2)]:
        part, rest = order[lo:lo + STRETCH], order[lo + STRETCH:]
        base, last0, bank0 = ([0.0] * (n + 1), [0.0] * (n + 1)), {}, {}
        run(order[:lo], base[0], base[1], last0, bank0)
        held, tail = holders(rest, {}, {}), (lat[0] + [0.0], lat[1] + [0.0])
        for k in reversed(rest):
            for s in range(2):
                for d in before[k]:
                    tail[s][d[0]] = max(tail[s][d[0]], d[1 + s] + cost[s][k] + tail[s][k])
                for d, w in held[k]:
                    tail[s][d] = max(tail[s][d], w * wake[s] + cost[s][k] + tail[s][k])
        nextq = {q: next((k for k in rest if queue[k] == q), n) for q in set(queue[:n])}
        nextb = {b: next((k for k in rest if b in banks[k]), n) for x in banks for b in x}
        tail[0][n] = tail[1][n] = 0.0
        early = [max([base[s][k] + tail[s][k] for k in order[:lo]], default=0.0) for s in range(2)]

        def length(part):
            e, last, bank = (base[0][:], base[1][:]), dict(last0), dict(bank0)
            run(part, e[0], e[1], last, bank)
            total, ends = 0.0, []
            for s in range(2):
                top = [(e[s][k] + tail[s][k], k) for k in part]
                top += [(e[s][k] + cost[s][nextq[q]] + tail[s][nextq[q]], k) for q, k in last.items()]
                top += [(e[s][k] + wake[s] * (queue[k] != queue[nextb[b]]) + cost[s][nextb[b]] + tail[s][nextb[b]], k)
                        for b, k in bank.items()]
                ends.append(max(top))
                total += (1, MIX)[s] * (max(ends[s][0], early[s]) + EAGER * sum(e[s][k] for k in part) / len(part))
            return total, e, ends

        now = length(part)
        top, pairs = (now[0], part), None
        for move in range(MOVES):
            seed = (seed * 1103515245 + 12345) % 2147483648
            if pairs is None:
                s, place, pairs = (seed >> 20) & 1, {k: j for j, k in enumerate(part)}, []
                held, end, k = holders(part, dict(last0), dict(bank0)), now[1][s], now[2][s][1]
                while k in place:
                    t = end[k] - cost[s][k] - 1e-9
                    nxt = [x[0] for x in before[k] if end[x[0]] + x[1 + s] > t]
                    if not nxt:
                        nxt = [d for d, w in held[k] if end[d] + w * wake[s] > t]
                        pairs += [(d, k) for d in nxt if d in place]
                    k = nxt[0] if nxt else n
            seed = (seed * 1103515245 + 12345) % 2147483648
            pick, far, soon = seed >> 14, (seed >> 10) % 3, (seed >> 13) & 1
            if (seed >> 8) & 3 and pairs:
                u, v = pairs[pick % len(pairs)]
            else:
                v = part[pick % len(part)]
                u = next((part[j] for j in range(place[v] - 1, -1, -1) if queue[part[j]] == queue[v]), v)
            i, j = place[u], place[v]
            for _ in range(far):
                if soon:
                    i = next((x for x in range(i - 1, -1, -1) if queue[part[x]] == queue[v]), i)
                else:
                    j = next((x for x in range(j + 1, len(part)) if queue[part[x]] == queue[u]), j)
            span, took = part[i:j + 1], {v if soon else u}
            for x in reversed(span) if soon else span:
                if (behind[x] if soon else ops[x]["after"]) & took:
                    took.add(x)
            if part[i if soon else j] in took:
                continue
            new = part[:i] + [x for x in span if (x in took) == soon] + [x for x in span if (x in took) != soon] + part[j + 1:]
            made = length(new)
            if made[0] <= now[0] + HEAT * (1 - move / MOVES) * ((seed >> 4) % 64) / 64:
                part, now, pairs = new, made, None
                if now[0] < top[0]:
                    top = (now[0], part)
        order = order[:lo] + top[1] + rest
    fin = ([0.0] * (n + 1), [0.0] * (n + 1))
    run(order, fin[0], fin[1], {}, {})
    _PLAN["time"], _PLAN["ends"] = [round(max(x), 1) for x in fin], fin[0]
    extra, seen = [set() for _ in range(n)], {}
    for k in order:
        for b in banks[k]:
            extra[k] |= {d for q, d in seen.get(b, {}).items() if q != queue[k]}
            seen.setdefault(b, {})[queue[k]] = k
    return order, extra


def rank_program(g, core, T, topo):
    def peers(x):
        return [T.cores[T.rank_of(x) ^ (1 << t)] for t in range(STEPS)]

    def helper(x):
        free = [y for y in topo.cores_of(x) if T.rank_of(y) is None and topo.die(y) != topo.die(x)
                and all(topo.may_write(y, z) for z in peers(x))]
        return free[[y for y in topo.cores_of(x) if T.rank_of(y) is not None].index(x)]

    def engines(x):
        main = [e for e in topo.engines(x, helper(x)) if all(e in topo.engines(x, y) for y in peers(x))]
        return main, [e for e in topo.engines(x, helper(x)) if e not in main]

    if T.rank_of(core) is None:
        for x in [y for y in T.cores if helper(y) == core]:
            sent = 0
            for t, y in enumerate(peers(x)):
                if topo.chip(y) != topo.chip(x):
                    part, (rid, pid) = T["lr%d" % t][:, WRITES[0][0]:WRITES[0][1]], topo.addr(y)[:2]
                    g.wait_ge(T.sem["h%d" % t], len(engines(x)[1]))
                    g.remote_dma(part, part, T.sem["r%db" % t], T.sem["sent"], pid, rid, topo.mask(core, y))
                    sent += len(topo.engines(core, y))
            g.wait_ge(T.sem["sent"], sent)
        return
    Q = {"ve": g.vector, "ac": g.scalar, "pe": g.tensor, "po": g, "sy": g.sync}
    ops, hist, ramps = [], {}, []

    def c(name, a=0, b=None, st=1, p=None):
        b = SCRATCH[name][1][1] if b is None else b
        ps = slice(None) if p is None else slice(p[0], p[1])
        ap = T[name][ps, a:b] if st == 1 else T[name][ps, a:b:st]
        return (ap, [(name, a, b, st)], [], len(range(a, b, st)), name, False)

    def ind(win, off):
        return (win[0].indirect(off[0]), win[1], off[1], 16 * off[3], win[4], True)

    def rec(q, call, outs, ins, cost, sem=None, inc=1, lat=0.0, after=(), opened=False):
        k = len(ops)
        wait, order, acc = set(), set(after), []
        for o in outs:
            acc += [(r, True) for r in o[1]] + [(r, False) for r in o[2]]
        for o in ins:
            if isinstance(o, tuple):
                acc += [(r, False) for r in o[1] + o[2]]
        for (name, lo, hi, st), w in acc:
            for l2, h2, s2, k2, w2 in hist.get(name, []):
                same = ops[k2]["q"] == q and ops[k2]["sem"] is None and sem is None
                if l2 < hi and lo < h2 and (w or w2) and not (st == s2 > 1 and (lo - l2) % st):
                    (order if same and ops[k2]["open"] else wait).add(k2)
                elif q == "pe" and same and name.startswith("pb") and (opened or ops[k2]["open"]):
                    order.add(k2)
        for (name, lo, hi, st), w in acc:
            if w and st == 1:
                hist[name] = [x for x in hist.get(name, []) if not (lo <= x[0] and x[1] <= hi)]
            hist.setdefault(name, []).append((lo, hi, st, k, w))
        both = (cost + np.zeros(2), lat + np.zeros(2))
        ops.append(dict(q=q, call=call, sem=sem, inc=inc, wait=wait - {k}, after=(wait | order) - {k}, both=both,
                        cost=float(both[0][0]), lat=float(both[1][0]),
                        open=opened, banks={r[0] for r, w in acc if r[0].startswith("pb")}))
        return k

    def a(x):
        return x[0] if isinstance(x, tuple) else x

    def price(o, x, per):
        return FIX + CYC * (SCATTER * o[3] if o[5] else GATHER * o[3] if x[5] else max(64, per * o[3]))

    def narrow(*xs):
        return 0.5 if all(SCRATCH[x[4]][2] in (b16, h16, u16) for x in xs) else 1

    def tt(o, x, y, op):
        per = 1 if x[4].startswith("pb") or y[4].startswith("pb") else 2
        return rec("ve", lambda e: e.tensor_tensor(o[0], x[0], y[0], op), [o], [x, y], price(o, x, per))

    def ts(o, x, s1, op0, s2=None, op1=None):
        if op1 is None:
            call = lambda e: e.tensor_scalar(o[0], x[0], a(s1), None, op0)
        else:
            call = lambda e: e.tensor_scalar(o[0], x[0], a(s1), a(s2), op0, op1)
        return rec("ve", call, [o], [x, s1, s2], price(o, x, narrow(o, x)))

    def cp(o, x):
        return rec("ve", lambda e: e.tensor_copy(o[0], x[0]), [o], [x], price(o, x, narrow(o, x)))

    def fill(o, v):
        rec("ve", lambda e: e.memset(o[0], v), [o], [], price(o, o, narrow(o)))

    def scan(o, x, y, init, op0, op1):
        return rec("ve", lambda e: e.tensor_tensor_scan(o[0], x[0], y[0], a(init), op0, op1), [o], [x, y, init],
                   price(o, x, narrow(o, x, y)))

    def act(o, x, f=F.Identity, bias=0.0, scale=1.0, after=(), total=None):
        if total is None:
            call = lambda e: e.activation(o[0], x[0], f, bias=a(bias), scale=a(scale))
        else:
            call = lambda e: e.activation(o[0], x[0], f, bias=a(bias), scale=a(scale), accum_out=total[0])
        return rec("ac", call, [o] + [total] * (total is not None), [x, bias, scale], price(o, x, 1), after=after)

    def move(who, o, x, scale=None):
        if ENG[who] == "s":
            return act(o, x, scale=1.0 if scale is None else scale)
        return cp(o, x) if scale is None else ts(o, x, scale, A.mult)

    def group(o, terms, start=True, stop=True, after=()):
        parts = o if isinstance(o, list) else [(o, terms)]

        def call(e):
            for out, tm in parts:
                for j, (l, r) in enumerate(tm):
                    ins = e.matmul(out[0], l[0], r[0], start and j == 0, stop and j == len(tm) - 1)
            return ins
        cost = sum(PECYC * max(64, r[3]) * (4 if SCRATCH[r[4]][2] == f32 else 1) for out, tm in parts for l, r in tm)
        outs = [out if start and stop else c(out[4]) for out, tm in parts]
        return rec("pe", call, outs, [x for out, tm in parts for lr in tm for x in lr], cost,
                   opened=not stop, after=after)

    def wrap(m, name, a0, b0):
        return [(c(m, 15 - p, 143 - p), c(name, a0 + p, b0, 16)) for p in range(16)]

    def iota(o, pat, base, cm):
        kw = {} if SCRATCH[o[4]][2] == i32 else {"allow_small_or_imprecise_dtypes": True}
        k = rec("po", lambda e: e.iota(o[0], pat, base, cm, **kw), [o], [], 0.13 + 2 * CYC * o[3])
        ramps.append((RAMPS.index(o[4]), k))

    landed = [1.2]

    def load(q, o, src, s, nbytes):
        landed[0] = landed[0] + nbytes / HBM
        prev = [k for k, x in enumerate(ops) if x["q"] == q]
        rec(q, lambda e: e.dma_start(o[0], src), [o], [], 0.05, "d_" + s, 16, landed[0], prev[-1:])

    def store(q, dst, x, s, nbytes):
        rec(q, lambda e: e.dma_start(dst, x[0]), [], [x], 0.05, "d_" + s, 16, 2.0 + nbytes / HBM)

    sends = []

    def exchange(t, dst, src, s, side=False):
        far = side and topo.chip(peers(core)[t]) != topo.chip(core)
        rid, pid = topo.addr(helper(core) if far else peers(core)[t])[:2]
        eng, sem = engines(core)[side], T.sem["h%d" % t if far else s]
        k = rec("po", lambda e: e.remote_dma(dst[0], src[0], sem, T.sem["sent"], pid, rid, sum(1 << x for x in eng)),
                [], [src], ISSUE * (1 if sends else 2.5), "sent", len(eng), 0.0, sends[-1:])
        sends.append(k)
        q, other = "rx%d" % side, peers(core)[t]
        prev = [j for j, x in enumerate(ops) if x["q"] == q]
        rec(q, None, [dst], [], 512 * src[3] / LINK, s,
            len(topo.engines(helper(other), core) if far else engines(other)[side]),
            FLY + far * (FLY + 2 * ISSUE + 512 * src[3] / LINK / 2), [k] + prev[-1:])

    col = lambda j: c("CC", j, j + 1)
    (PCOL, ACOL, QCOL, LANE, GCOL, LT4, GE4, EQ4, S1, SM15, S15, G16, HALF, LT8, EW, R35, E44,
     PAT, NG, EQ5, PW, SGN, THR) = range(23)
    I1, I2k, In2k, Ih = c("I1"), c("I2k"), c("In2k"), c("Ih")
    xm = lambda o, n: c("XM", 16 + o, 16 + o + n)
    m143 = lambda s: c(s, 0, 143)

    load("sy", c("cnts", p=(0, 8)), T.cnt[:], "cnt", 0)
    load("sy", c("stks"), T.stk[:], "stk", 1e5)
    big = {"nb": (c("nbs", 0, V), T.nb[:], 1e6), "ln": (c("W", 0, V), T.ln[:], 5e5)}
    for j, (x, y) in enumerate(zip(LAB, LAB[1:])):
        big["lab%d" % j] = (c("labs", x, y), T.lab[:, x:y], 512 * (y - x))
    for s in LOADS:
        load("sy", big[s][0], big[s][1], s, big[s][2])
    iota(c("PI", 0, 1), [[0, 1]], 0, 1)
    iota(col(PCOL), [[0, 1]], 0, 1)
    iota(col(G16), [[0, 1]], 0, 16)
    iota(c("GM"), [[16, 8], [0, 16]], 0, 0)
    iota(c("XM"), [[1, 256]], -16, 0)
    iota(c("C1"), [[16, 16]], P, 0)
    iota(c("E0"), [[1, 64], [0, 16]], 0, 0)
    fill(c("A0"), 0.0)
    fill(c("A0", 0, 1024, 16), -BIG)
    ts(c("PI", 1, 2), c("PI", 0, 1), 15, A.bitwise_and)
    ts(c("PI", 2, 3), c("PI", 0, 1), 2, A.arith_shift_right, 3, A.bitwise_and)
    ts(c("PI", 3, 4), c("PI", 0, 1), 63, A.bitwise_and)
    cp(c("CC", ACOL, ACOL + 3), c("PI", 1, 4))
    tt(col(GCOL), col(PCOL), col(ACOL), A.subtract)
    for j, s in ((SM15, -15.0), (S1, 1.0), (HALF, 0.5)):
        act(col(j), col(ACOL), bias=s)
    act(col(S15), col(ACOL), bias=15.0, scale=-1.0)
    ts(col(LT4), col(ACOL), 4.0, A.is_lt)
    ts(col(GE4), col(ACOL), 4.0, A.is_ge)
    ts(col(EQ4), col(ACOL), 4.0, A.is_equal)
    ts(col(LT8), col(ACOL), 8.0, A.is_lt)
    ts(col(EQ5), col(ACOL), 5.0, A.is_equal)
    act(col(PAT), col(EQ5), scale=float(DEAD))
    act(col(EW), col(LT8), bias=-32.0, scale=32.125)
    act(col(PW), col(LT8), bias=64.0, scale=-63.875)
    act(col(SGN), col(LT8), bias=-1.0, scale=2.0)
    act(col(THR), col(LT8), bias=-4.0, scale=9.0)
    act(col(E44), col(ACOL), F.Abs, -4.0)
    ts(col(R35), col(E44), 1.0, A.is_equal)
    ts(c("REP", p=(0, 8)), c("GM", p=(0, 8)), c("CC", G16, G16 + 1, p=(0, 8)), A.is_equal)
    ts(m143("Mh"), xm(-15, 143), col(GCOL), A.is_equal)
    ts(m143("M35"), m143("Mh"), col(R35), A.mult)
    cp(m143("M1"), m143("Mh"))
    for nm, s in (("MP", col(PW)), ("MK4", 4096.0), ("Q15", -1.0), ("Qh", -1.0), ("MD", DEAD / 16.0), ("ME", col(EW))):
        act(m143(nm), m143("M1"), scale=s)
    ts(c("IW", 0, 140), xm(-12, 140), col(PCOL), A.is_equal)
    I32 = c("IW", 12, 140)
    cp(Ih, I32)
    act(c("IW4", 0, 140), c("IW", 0, 140), scale=col(LT4))
    act(col(NG), col(GCOL), bias=-1.5, scale=-1.0)
    act(c("DV", 0, 140), xm(-12, 140), F.Abs, col(NG))
    ts(c("DV", 0, 140), c("DV", 0, 140), 2.0, A.is_lt, col(EQ5), A.mult)
    tt(c("IW4", 0, 140), c("IW4", 0, 140), c("DV", 0, 140), A.add)
    for nm, s in (("I1", 1.0), ("In1", -1.0), ("I2k", 2048.0), ("In2k", -2048.0), ("In4", -4.0), ("Id", -1 / 32),
                  ("Inh", -1.0), ("IL4", col(LT4)), ("B4", -32.0)) + (("Inf", -1.0),) * bool(ONS):
        act(c(nm, 0, 128), I32, scale=s)
    act(c("IhG"), I32, scale=col(GE4))
    act(c("In2G"), c("IhG"), scale=-2048.0)
    ts(c("E"), c("E0"), col(LANE), A.is_equal)
    ts(c("ONES"), c("GM"), col(GCOL), A.is_equal)
    ts(c("SE4"), c("ONES"), col(EQ4), A.mult, 4.0, A.mult)
    ts(c("ocnt", 0, 16), xm(0, 16), col(ACOL), A.is_equal, -1.0, A.mult)
    for b in range(16):
        (act(c("NS", 128 * b, 128 * b + 128), c("ONES"), scale=c("ocnt", b, b + 1)) if b % NSS == 0 else
         ts(c("NS", 128 * b, 128 * b + 128), c("ONES"), c("ocnt", b, b + 1), A.mult))
    fill(c("qh", 0, 256), 0.0)
    fill(c("RST"), 1.0)
    for kind, (n, wide, at, src, w, pad) in LISTS.items():
        pairs, calls, tri = PAIRS(wide), n // wide, c("jm", 128 + at, 128 + at + 16 * n // wide)
        iota(tri, [[1, 16], [0, calls]], 0, 0)
        iota(c("T" + kind, 0, 16 * w), [[0, 16 * w]], 0, 0)
        for r, (i, j) in enumerate(pairs):
            for x, y in ((0, j), (pad, i)):
                act(c("qh", at + x + r, at + x + w, len(pairs)), xm(0, calls), bias=y / 16, scale=wide / 16)
            if j == 0:
                act(c("qh", 192 + at // 4 + i, 192 + at // 4 + n, wide), xm(0, calls), bias=r / 16, scale=len(pairs) / 16)
            if i == j:
                act(c("T" + kind, r, 16 * w, len(pairs)), tri, F.Relu, col(HALF), -1.0)
                fill(c("RST", at + r, at + w, len(pairs)), 0.0)
    group(c("pb7", 0, 16), wrap("Mh", "qh", 0, 256))
    cp(c("LU"), c("pb7", 0, 16))
    iota(c("SP"), [[0, 32 // JW], [16, JW]], V, 0)
    act(c("SP"), c("SP"), bias=col(ACOL))
    ts(c("jm", 0, 128), xm(0, 128), col(PCOL), A.is_ge)
    tt(c("jm", 0, 128), c("jm", 0, 128), c("ONES"), A.mult)
    tt(c("TR1"), c("jm", 0, 128), c("B4", 0, 128), A.add)
    act(c("TR2"), c("TR1"), scale=2048.0)
    ts(m143("PQ"), xm(-16, 143), col(GCOL), A.is_equal)
    tt(m143("PQ"), m143("PQ"), m143("Q15"), A.add)
    fill(c("ONE"), 1.0)
    act(c("RS"), c("ONE"), scale=col(LT8))
    act(c("C1"), c("C1"), bias=col(ACOL))
    act(c("SPL"), c("ONES"), scale=col(PW))
    ts(c("DV", 0, 128), xm(4, 128), col(PCOL), A.is_equal, col(GE4), A.mult)
    tt(c("SHI"), c("DV", 0, 128), I32, A.subtract)
    act(c("yz", 0, 24), xm(0, 24), bias=col(QCOL), scale=4.0)
    act(c("JC"), ind(c("yz", 0, 24), c("LU", 4, 8)))
    fill(c("X", V, WIDE), 0.0)
    fill(c("W", V, WIDE), 1.0)
    fill(c("nbs", V, WIDE), DEAD)
    fill(c("Hh"), 0.0)
    for nm in ("Mb", "Wp"):
        iota(c(nm), [[0, PAD]], 0, 0)
    for t in range(STEPS):
        act(c("ms%d" % t, 0, 104), xm(0, 104), bias=col(PAT), scale=0.0)
        iota(c("ms%d" % t, 104, 456), [[0, 352]], 0, 0)
        act(c("mr%d" % t, 104, 240), xm(0, 136), bias=col(PAT), scale=0.0)
        fill(c("mr%d" % t, 240, 248), 0.0)

    for (_, x), (_, y) in zip(sorted(ramps), sorted(ramps)[1:]):
        ops[y]["after"].add(x)

    XW, v14 = c("X"), c("v16", 0, 14)
    PA, PB, PS, PN = c("pb6", 256, 256 + P), c("pb6", 0, P), c("pb7", 0, P), c("pb5", 256, 256 + P)
    PV, PU, PC, PY = c("pb4", 320, 334), c("pb3", 0, 24), c("pb0", 0, P), c("pb0", 256, 256 + P)
    slot = lambda nm, k, a0, b0: c(nm, 128 * k + 64 + a0, 128 * k + 64 + b0)

    def distinct(kind, names, banks, y, off, more=()):
        n, wide, at, src, w, pad = LISTS[kind]
        per = -(-16 // len(banks))
        rows = [range(per * j, min(16, per * j + per)) for j in range(len(banks))]
        move("Uf", c("Uf", src, src + n), names)
        move("Uh", c("Uh", at, at + 2 * pad), ind(c("Uf", src, src + n), c("LU", at // 16, (at + 2 * pad) // 16)))
        mine, other, eq = c("Uh", at + pad, at + pad + w), c("Uh", at, at + w), "eq" + kind
        for bk, bs in zip(banks, rows):
            group([(c(bk, w * (b - bs[0]), w * (b - bs[0] + 1)), [(Ih, other), (c("NS", 128 * b, 128 * b + 128), mine)])
                   for b in bs], None)
            piece = (w * bs[0], w * (bs[-1] + 1))
            tt(c(eq, *piece), c(bk, 0, w * len(bs)), c("T" + kind, *piece), A.is_equal)
        y = c(y[0], y[1], y[1] + w)
        for j, bs in enumerate(rows):
            group(y, [(Ih, mine)] * (j == 0) + list(more) * (j == 0)
                  + [(c("MK4", 15 - b, 143 - b), c(eq, w * b, w * b + w)) for b in bs], j == 0, j == len(banks) - 1)
        scan(c("yz", at, at + w), c("RST", at, at + w), y, 0.0, A.mult, A.max)
        ends = 12 + at // 64
        tt(c(off), ind(c("yz", at, at + w), c("LU", ends, ends + (n + 15) // 16)), c("SP", 0, SCRATCH[off][1][1]), A.min)

    def popped():
        move("v16", v14, PV)
        cp(c("K"), ind(c("nbs"), v14))
        move("Kf", c("Kf"), c("K"))
        for j in range(7):
            (cp if j in WV else act)(c("Wg", 512 * j, 512 * j + 512), ind(c("W"), c("K", 32 * j, 32 * j + 32)))
        move("Wv", c("Wv"), ind(c("W"), v14), -1 / 32)
        for k, (l0, l1) in enumerate(CH):
            move("Wp", slot("Wp", k, 0, l1 - l0), c("Wv", l0, l1))
        ts(c("n1"), PN, 15.0, A.add, 0.0, A.max)
        ts(c("r1"), c("n1"), col(S1), A.subtract, 0.0, A.min)
        ts(c("pm"), c("n1"), col(ACOL), A.is_gt)
        distinct("Z", PV, ["pb4"], ("pb4", 352), "zoff")

    ts(c("cntb", p=(0, 8)), c("cnts", p=(0, 8)), 16.0, A.subtract)
    group(PN, [(c("REP", p=(0, 8)), c("cntb", p=(0, 8)))])
    ts(c("m2"), PN, col(SM15), A.is_equal)
    act(c("em"), PN, F.Relu, -15.0, -1.0)
    tt(c("T2"), c("m2"), c("stks"), A.mult)
    group(PV, wrap("MD", "em", 0, P), True, False)
    group(PV, wrap("Mh", "T2", 0, P), False, True)
    for x, y in zip(LAB, LAB[1:]):
        ts(c("X", x, y), c("labs", x, y), -1 / 32, A.mult)
    popped()
    tt(c("Sold"), c("pm"), c("stks"), A.mult)

    for t in range(STEPS):
        last = t == STEPS - 1
        ls, lr, ms, mr = (x + str(t) for x in ("ls", "lr", "ms", "mr"))
        tag = {"d": tt(c("DV"), ind(XW, v14), c("Wv"), A.subtract)}
        for j in range(7):
            gather = cp if j in GV else act
            tag["g%d" % j] = gather(c("G", 512 * j, 512 * j + 512), ind(XW, c("K", 32 * j, 32 * j + 32)))
        for k, (l0, l1) in enumerate(CH):
            n = l1 - l0
            M, PT = slot("Mb", k, 0, n), c(*TURN[k])
            tag["s%d" % k] = scan(c("SO", 16 * l0, 16 * l1), c("A0", 0, 16 * n), c("G", 16 * l0, 16 * l1), 0.0, A.add, A.max)
            tag["m%d" % k] = tt(M, c("SO", 16 * l0 + 15, 16 * l1, 16), c("DV", l0, l1), A.max)
            tag["n%d" % k] = tt(slot("Hh", k, 0, n), c("SO", 16 * l0 + 15, 16 * l1, 16), c("DV", l0, l1), A.max)
            tag["T%d" % k] = group(PT, [(slot("Wp", k, -64, 64), I1), (slot("Mb", k, -64, 64), I32),
                                        (slot("Hh", k, 0, 128), Ih), (slot("Hh", k, -64, 64), c("Inh"))])
            HT = c("HT", 128 * k, 128 * k + 128)
            tag["H%d" % k] = (cp if k in HV else act)(HT, PT)
            for j in range(l0 // 32, l1 // 32):
                bank, piece = c("pb%d" % BANKS[j]), (512 * j, 512 * j + 512)
                tag["w%d" % j] = group(bank, [(c("Id"), c("Wg", *piece))], True, False)
                if j in ONS:
                    tag["x%d" % j] = group(bank, [(c("Inf"), c("G", *piece))], False, False)
                tag["e%d" % j] = group(bank, [(HT, c("E", 512 * j - 16 * l0, 512 * j + 512 - 16 * l0))], False, True)
                if j in ONS:
                    tag["t%d" % j] = act(c("Ind", *piece), bank, F.Relu)
                else:
                    tag["t%d" % j] = tt(c("Ind", *piece), c("G", *piece), bank, A.is_lt)
                at = 32 * j - l0
                tag["z%d" % j] = tt(ind(XW, c("zoff", 2 * j, 2 * j + 2)), slot("Mb", k, at, at + 32),
                                    c("Wv", 32 * j, 32 * j + 32), A.add)
        for j, (h0, h1) in enumerate(zip([0] + HITS, HITS)):
            tag["h%d" % j] = group(c(SUMS, h0, h1), [
                (c("M1", 15 - i, 143 - i), c("Ind", 16 * h0 + i, 16 * h1, 16)) for i in range(16)])
        for line in PULL:
            for x, y in zip(line.split(), line.split()[1:]):
                ops[tag[y]]["after"].add(tag[x])
        for pt in PARTS:
            if ENG["hit"] == "s":
                act(c("hit", *pt), c(SUMS, *pt), F.Sign)
            else:
                ts(c("hit", *pt), c(SUMS, *pt), 0.0, A.is_gt)
            j = PARTS.index(pt)
            low, forv, fors = ("pb%d" % x for x in LOW[j])
            low, val, high = c(low, *pt), c(fors, *pt), c(fors, 256 + pt[0], 256 + pt[1])
            for x in sorted({fors, "pb6"}):
                group(c(x, *pt), [(I2k, c("n1", *pt)), (Ih, c("Kf", *pt)), (c("TR2"), c("hit", *pt))])
                group(c(x, 256 + pt[0], 256 + pt[1]), [(I1, c("n1", *pt)), (c("ONES"), c("hit", *pt))])
            group(c(forv, *pt), [(I1, c("n1", *pt)), (c("ONES"), c("hit", *pt))])
            group(low, [(Ih, c("Sold", *pt)), (In2k, c("r1", *pt))], True, False)
            act(c("r2", *pt), high, F.Relu, col(S1), -1.0)
            act(c("em", *pt), high, F.Relu, 1.0, -1.0, total=c(ms, 4 + j, 5 + j))
            group(low, [(In2k, c("r2", *pt))], False, False)
            n, at = pt[1] - pt[0], 4 * pt[0]
            if j in NARROW:
                for s in range(4):
                    act(c("qh", at + n * s, at + n * s + n), val, F.Relu, 2048.0 * (s + 1) - 63488.0, -1.0)
                ts(c("qh", at, at + 4 * n), c("qh", at, at + 4 * n), 2048.0, A.min)
                group(low, [(c("Qh", 15 - s, 143 - s), c("qh", at + n * s, at + n * s + n)) for s in range(4)], False, True)
            else:
                for s in range(4):
                    qs = c("q", at + n * s, at + n * s + n)
                    act(qs, val, F.Relu, 2048.0 * (s + 1) - 63488.0, -1.0)
                    group(low, [(c("PQ", 15 - s, 143 - s), qs)], False, s == 3)
            act(c("B4", *pt), low, bias=col(EQ4), scale=col(LT4))
            flag = c("RG", P + pt[0], P + pt[1])
            ts(flag, c(forv, *pt), col(SGN), A.mult, col(THR), A.is_ge)
            scan(c("RG", *pt), c("RS", *pt), flag, c("RG", pt[0] - 1, pt[0]) if pt[0] else -1.0, A.mult, A.add)
        move("B4h", c("B4h"), c("B4"), col(LT4))
        for (l0, l1), bank in PLACES:
            group(c(bank, 256 + l0 // 16, 256 + l1 // 16), wrap("MP", "RG", l0, l1))
            tt(c("pos", l0 // 16, l1 // 16), c(bank, 256 + l0 // 16, 256 + l1 // 16), c("C1", l0 // 16, l1 // 16), A.min)
            cp(ind(c(ms, 8, 456), c("pos", l0 // 16, l1 // 16)), c("B4", l0, l1))
        if EARLY:
            exchange(t, c(mr, 4, 6), c(ms, 4, 6), "r%dc" % t)
        exchange(t, c(mr, 8 if EARLY else 4, 104), c(ms, 8 if EARLY else 4, 104), "r%dn" % t)
        wrapped = lambda x: [(c("IW4", 12 - 4 * qq, 140 - 4 * qq), c(x, 8 + qq, 104, 4)) for qq in range(4)]
        group(PU, wrapped(ms))
        move("U16", c("U16"), PU)
        for j, (h0, h1) in enumerate(WRITES):
            act(c(ls, h0, h1), ind(XW, c("U16", h0 // 16, h1 // 16)))
            exchange(t, c(lr, h0, h1), c(ls, h0, h1), "r%d%s" % (t, "bac"[j]), j == 0)
        act(c("cio", 1, 2), c(ms, 4, 5), bias=c(ms, 5, 6))
        ts(c("inval"), c("JC"), c("cio", 1, 2), A.is_ge, 4096.0, A.mult)
        group(c("pb3", 24, 48), wrapped(mr))
        distinct("J", c("pb3", 24, 48), JBANKS, ("pb3", 128), "joff", [(I1, c("inval", 0, LISTS["J"][4]))])
        move("Uq", c("Uq"), c("Uf", 0, 24))
        ts(c("cio", 0, 1), c(mr, 4, 5), c(mr, 5, 6), A.add, 96.0, A.min)
        act(c("nq"), PA, F.Relu, 16.0, -1.0)
        scan(c("er"), c("RS"), c("em"), 0.0, A.mult, A.add)
        PE_ = c("pb4", 288, 302)
        group(PE_, wrap("ME", "er", 0, P))
        ts(c("epos", 0, 14), PE_, 255.0, A.add, 232.0, A.min)
        if not last:
            group(PC, [(I1, c("n1")), (c("TR1"), c("hit")), (I1, c("nq"))])
            ts(c("mt"), PC, -16.0, A.is_equal)
            ts(c("m2"), c("nq"), col(S15), A.is_equal)
            tt(c("T1"), c("mt"), c("Kf"), A.mult)
            tt(c("T2"), c("m2"), c("Sold"), A.mult)
            group(PV, wrap("Mh", "T1", 0, P), True, False)
            group(PV, wrap("Mh", "T2", 0, P), False, False)
        group(PY, [(c("SPL"), c("RG", 0, P))])
        group(PS, [(Ih, c("B4h")), (c("IhG"), c("Sold")), (c("In2G"), c("r1")), (c("In2G"), c("r2"))], True, False)
        for s0 in range(4, 16, BATCH):
            for s in range(s0, s0 + BATCH):
                act(c("qh", P * s, P * s + P), PB, F.Relu, 2048.0 * (s + 1) - 63488.0, -1.0)
            ts(c("qh", P * s0, P * (s0 + BATCH)), c("qh", P * s0, P * (s0 + BATCH)), 2048.0, A.min)
            group(PS, [(c("Qh", 15 - s, 143 - s), c("qh", P * s, P * s + P)) for s in range(s0, s0 + BATCH)],
                  False, s0 + BATCH == 16)
        move("Rg", c("Rg"), ind(c(mr, 8, 248), c("epos", 0, 14)))
        ts(c("giv"), PY, c("cio", 0, 1), A.is_lt)
        group(PN, [(c("In1"), c("nq")), (c("SE4"), c("Rg")), (c("In4"), c("giv"))])
        if not last:
            group(PV, wrap("M35", "Rg", 0, P), False, True)
            popped()
        tt(c("Bg"), PS, c("giv"), A.mult)
        move("T1", c("T3"), PS)
        group(PS, [(Ih, c("T3")), (c("SHI"), c("Bg")), (c("IL4"), c("Rg"))])
        if last:
            for j in range(0, WIDE, WIDE // 4):
                act(c("Xo", j, j + WIDE // 4), c("X", j, j + WIDE // 4), scale=-32.0)
            for h0, h1 in sorted(WRITES):
                tt(c("jm", h0, h1), ind(XW, c("Uq", h0 // 16, h1 // 16)), c(lr, h0, h1), A.max)
        else:
            move("own", c("jm"), ind(XW, c("Uq")))
        for j in range(0, 24, JW):
            off, x = c("joff", j, j + JW), c("jm", 16 * j, 16 * (j + JW))
            if last:
                ts(ind(c("Xo"), off), x, -32.0, A.mult, 0.0, A.add)
            else:
                tt(ind(XW, off), x, c(lr, 16 * j, 16 * (j + JW)), A.max)
        if not last:
            tt(c("Sold"), PS, c("pm"), A.mult)
        else:
            act(c("ocnt"), PN, F.Identity, 16.0)
            store("ac", T.ycnt[:], (T["ocnt"][0:128:16, :],) + c("ocnt")[1:], "ycnt", 1.2e6)
            act(c("ostk"), PS)
            store("ac", T.ystk[:], c("ostk"), "ystk", 1.2e6)
            store("sy", T.ylab[:], c("Xo", 0, V), "ylab", 1e6)

    if "order" not in _PLAN:
        _PLAN["order"] = order_calls(ops)
    order, extra = _PLAN["order"]
    place = {k: j for j, k in enumerate(order)}
    keyof = lambda k: ops[k]["sem"] or ops[k]["q"]
    need, covered, signal = {}, {}, set()
    for k in order:
        best = {}
        if ops[k]["call"]:
            for d in ops[k]["wait"] | extra[k]:
                if place[d] > place.get(best.get(keyof(d)), -1):
                    best[keyof(d)] = d
        need[k] = {}
        for key, d in best.items():
            if covered.get((ops[k]["q"], key), -1) < place[d]:
                covered[(ops[k]["q"], key)] = place[d]
                need[k][key] = d
                signal.add(d)
    total, value = {}, {}
    for k in order:
        if ops[k]["sem"] or k in signal:
            total[keyof(k)] = total.get(keyof(k), 0) + ops[k]["inc"]
            value[k] = total[keyof(k)]
    for k in order:
        o = ops[k]
        if not o["call"]:
            continue
        e = Q[o["q"]]
        for key, d in need[k].items():
            e.wait_ge(T.sem[key], value[d])
        ins = o["call"](e)
        if o["sem"] != "sent" and k in value:
            ins.then_inc(T.sem[keyof(k)], o["inc"])
    for key, n in total.items():
        g.wait_ge(T.sem[key], n)
